import numpy as np
import ml_dtypes


def mxq(x, axis, fmt="e4m3"):
    dtype, down = {"e4m3": (ml_dtypes.float8_e4m3fn, 7), "e5m2": (ml_dtypes.float8_e5m2, 14)}[fmt]
    v = np.moveaxis(np.asarray(x, np.float32).astype(ml_dtypes.bfloat16).astype(np.float64), axis, -1)
    blocks = v.reshape(v.shape[:-1] + (-1, 32))
    amax = np.abs(blocks).max(-1, keepdims=True)
    byte = np.maximum(np.where(amax > 0, np.frexp(amax)[1] - 1 + 127, 0) - down, 1)
    scale = np.exp2(byte - 127.0)
    codes = (blocks / scale).astype(np.float32).astype(dtype).astype(np.float64)
    return np.moveaxis((codes * scale).reshape(v.shape), -1, axis)


WIDE = False


def mx_kscale(k):
    if not WIDE:
        return np.ones(k)
    levels = np.array([10, -10, 5, -5, 0])
    if k % 512:
        return np.exp2(np.random.permutation(np.resize(levels, k // 32))).repeat(32)
    a = np.empty((k // 512, 16))
    for p in range(k // 512):
        a[p, :8] = np.random.permutation(np.resize(levels, 8))
        for g in range(8):
            far = levels[np.abs(levels - a[p, g]) >= 10]
            a[p, g + 8] = far[np.random.randint(len(far))]
    return np.exp2(a.ravel()).repeat(32)


def f64(x):
    return np.asarray(x).astype(np.float64)


def striped(idx):
    return np.tile(idx.reshape(-1, 16).T, (8, 1)).astype(np.uint16)


def unstriped(offs):
    return offs[:16].T.reshape(-1).astype(np.int64)


E2M1 = np.array([0.0, 0.5, 1.0, 1.5, 2.0, 3.0, 4.0, 6.0, -0.0, -0.5, -1.0, -1.5, -2.0, -3.0, -4.0, -6.0])


def pack_weight(w, fmt):
    k, n = w.shape
    w = f64(np.asarray(w, np.float32).astype(ml_dtypes.bfloat16)).reshape(k // 32, 32, n)
    amax = np.abs(w).max(1)
    if fmt == "e4m3":
        byte = np.frexp(amax)[1] - 1 + 127 - 7
    else:
        mant, ex = np.frexp(amax / 6.0)
        byte = np.where(mant > 0.5, ex, ex - 1) + 127
    byte = np.clip(np.where(amax > 0, byte, 1), 1, 254)
    scaled = (w * np.exp2(127.0 - byte)[:, None, :]).reshape(k, n).astype(np.float32)
    by_word = np.ascontiguousarray(scaled.reshape(k // 512, 128, 4, n).transpose(0, 1, 3, 2))
    if fmt == "e4m3":
        words = by_word.astype(ml_dtypes.float8_e4m3fn).view(np.uint8)
    else:
        c = by_word.astype(ml_dtypes.float4_e2m1fn).view(np.uint8) & 0xF
        words = (c[..., 0::2] | (c[..., 1::2] << 4)).reshape(k // 512, 128, 2 * n)
    return np.ascontiguousarray(words), np.ascontiguousarray(byte.astype(np.uint8).reshape(k // 512, 16, n))


def unpack_weight(words, scales, fmt):
    g, _, n = scales.shape
    words = np.ascontiguousarray(words).reshape(g, 128, n, -1)
    if fmt == "e4m3":
        vals = words.view(ml_dtypes.float8_e4m3fn).astype(np.float64)
    else:
        nib = np.empty((g, 128, n, 4), np.uint8)
        nib[..., 0::2] = words & 0xF
        nib[..., 1::2] = words >> 4
        vals = E2M1[nib]
    vals = vals * np.repeat(np.exp2(scales.astype(np.float64) - 127.0), 8, axis=1)[..., None]
    return vals.transpose(0, 1, 3, 2).reshape(g * 512, n)


def pack_table4(v):
    words, scales = pack_weight(v, "e2m1")
    g, t = words.shape[0] // 2, v.shape[1]
    words = words.reshape(g, 2, 128, t, 2).transpose(0, 2, 3, 1, 4)
    return np.concatenate([words.reshape(g, -1), scales.reshape(g, -1)], axis=1)


def unpack_table4(tab):
    g, t = tab.shape[0], tab.shape[1] // 544
    words = tab[:, :512 * t].reshape(g, 128, t, 2, 2).transpose(0, 3, 1, 2, 4).reshape(2 * g, 128, 2 * t)
    return unpack_weight(words, tab[:, 512 * t:].reshape(2 * g, 16, t), "e2m1")


def pack_table(v):
    words, scales = pack_weight(v, "e4m3")
    return np.concatenate([words.reshape(words.shape[0], -1), scales.reshape(scales.shape[0], -1)], axis=1)


def unpack_table(tab):
    g, t = tab.shape[0], tab.shape[1] // 528
    return unpack_weight(tab[:, :512 * t].reshape(g, 128, t, 4), tab[:, 512 * t:].reshape(g, 16, t), "e4m3")


K, L, M, T, S = 1536, 2048, 512, 4096, 2048


def setup_inputs():
    n = np.random.standard_normal
    s1 = mx_kscale(K)[:, None]
    s2 = mx_kscale(L)[:, None]
    p_w4 = pack_weight(n((K, M)) / np.sqrt(K) / s1, "e2m1")
    return {
        "tab": pack_table(n((K, T)) * s1),
        "w4_words": p_w4[0],
        "w4_scales": p_w4[1],
        "tab2": pack_table4(n((L, T)) * s2),
        "u": (n((L, M)) / np.sqrt(L) / s2).astype(np.float32),
        "r": (n((512, 2048))).astype(np.float32),
        "offs": striped(np.random.permutation(T)[:S]),
        "offs2": striped(np.random.permutation(T)[:S]),
    }


def reference(tab, w4_words, w4_scales, tab2, u, r, offs, offs2):
    tab_ = unpack_table(tab)[:, unstriped(offs)]
    w4_ = unpack_weight(w4_words, w4_scales, "e2m1")
    tab2_ = unpack_table4(tab2)[:, unstriped(offs2)]
    u_ = mxq(f64(u), 0, "e4m3")
    y = w4_.T @ tab_ + u_.T @ tab2_
    return f64(r) + y

@@ -1,0 +1,283 @@
+from contextlib import ExitStack
+
+import concourse.mybir as mybir
+
+K, L, M, T, S = 1536, 2048, 512, 4096, 2048
+P = 128
+TAB_PASSES = K // 512
+U_PASSES = L // 512
+N = 512
+HALF = S // 2
+FLOPS = 2 * (K + L) * M * S
+
+F32 = mybir.dt.float32
+BF16 = mybir.dt.bfloat16
+I32 = mybir.dt.int32
+U32 = mybir.dt.uint32
+U16 = mybir.dt.uint16
+U8 = mybir.dt.uint8
+FP8X4 = mybir.dt.float8_e4m3fn_x4
+FP4X4 = mybir.dt.float4_e2m1fn_x4
+ADD = mybir.AluOpType.add
+
+
+def tile_list_tab48_res_kernel(tc, tab, w4_words, w4_scales, tab2, u, r, offs, offs2, out):
+    nc = tc.nc
+    with ExitStack() as ctx:
+        keep = ctx.enter_context(tc.tile_pool(name="keep", bufs=1))
+        stage = ctx.enter_context(tc.tile_pool(name="stage", bufs=2))
+        swap = ctx.enter_context(tc.tile_pool(name="swap", bufs=2))
+        ring = ctx.enter_context(tc.tile_pool(name="ring", bufs=8))
+        psum = ctx.enter_context(tc.psum_pool(name="psum", bufs=1))
+
+        offs_t = keep.tile([P, S // 16], U16, name="offs_t")
+        offs2_t = keep.tile([P, S // 16], U16, name="offs2_t")
+        tab_s0 = keep.tile([P, T // 4], I32, name="tab_s0", align_bytes=64)
+        tab_s12 = keep.tile([P, 2, T // 4], I32, name="tab_s12", align_bytes=64)
+        tab_s = [tab_s0[:], tab_s12[:, 0, :], tab_s12[:, 1, :]]
+        tab2_s = keep.tile([P, T // 4], I32, name="tab2_s", align_bytes=64)
+        tab_w = [keep.tile([P, T], I32, name=f"tab_w{a}", align_bytes=64) for a in range(2)]
+        tab2_w = [keep.tile([P, T], I32, name=f"tab2_w{m}", align_bytes=64) for m in range(2)]
+        w4_w = keep.tile([P, TAB_PASSES, M // 2], I32, name="w4_w", align_bytes=64)
+        w4_s = keep.tile([P, TAB_PASSES, M // 4], I32, name="w4_s", align_bytes=64)
+        moved = [keep.tile([P, S // 4], I32, name=f"moved{b}", align_bytes=64) for b in range(1, U_PASSES)]
+        u_raw = {}
+        r_t = {}
+
+        def load_tab_words(a):
+            if a == 2:
+                tab_w.append(keep.tile([P, T], I32, name="tab_w2", tag="tab_w1", align_bytes=64))
+            nc.sync.dma_start(tab_w[a][:], tab[a, 0 : 512 * T].rearrange("(p b) -> p b", p=P).bitcast(I32))
+
+        def load_tab2_words(m):
+            nc.sync.dma_start(tab2_w[m][:], tab2[m, 0 : 512 * T].rearrange("(p b) -> p b", p=P).bitcast(I32))
+
+        def load_u(a):
+            if a % 2 == 0:
+                pair = swap.tile([P, 2, 4, M], F32, name="pair_u", tag="swap")
+                u_raw[a] = pair[:, 0, :, :]
+                u_raw[a + 1] = pair[:, 1, :, :]
+            hold(u_raw[a][:, 0, 0:16])
+            nc.sync.dma_start(u_raw[a], u[512 * a : 512 * (a + 1), :].rearrange("(p j) n -> p j n", j=4))
+
+        def load_r(h):
+            r_t[h] = swap.tile([P, 4, HALF], F32, name="r_half", tag="swap")
+            nc.sync.dma_start(r_t[h][:], r[:, HALF * h : HALF * (h + 1)].rearrange("(m p) j -> p m j", p=P))
+
+        tab2_rows = tab2[:, 512 * T : 544 * T].rearrange("m (h q b) -> m h q b", h=2, q=16).bitcast(I32)
+
+        def hold(view):
+            nc.vector.memset(view, 0)
+        tab_rows = tab[1:3, 512 * T : 528 * T].rearrange("a (q b) -> q a b", q=16).bitcast(I32)
+        flat = tab.rearrange("a b -> (a b)")
+
+        def load_tab2_scales(m, q):
+            lo = 32 * q + 8 * m
+            nc.scalar.dma_start(tab2_s[lo : lo + 8, :], tab2_rows[m, :, 4 * q : 4 * q + 4, :])
+
+        def load_tab_scales(q):
+            nc.scalar.dma_start(tab_s12[32 * q : 32 * q + 4, :, :], tab_rows[4 * q : 4 * q + 4, :, :])
+
+        nc.vector.memset(tab2_s[:], 0)
+        nc.gpsimd.memset(w4_s[:], 0)
+        nc.sync.dma_start(offs_t[:], offs)
+        nc.sync.dma_start(offs2_t[:], offs2)
+        for q in range(4):
+            rows = flat[(512 + 4 * q) * T : (544 + 4 * q) * T].rearrange("(p b) -> p b", p=32).bitcast(I32)
+            nc.sync.dma_start(tab_s0[32 * q : 32 * (q + 1), :], rows)
+        load_tab_words(0)
+        nc.gpsimd.dma_start(w4_w[:], w4_words.rearrange("a p b -> p a b").bitcast(I32))
+        for q in range(4):
+            rows = w4_scales[:, 4 * q : 4 * q + 4, :].rearrange("a r b -> r a b").bitcast(I32)
+            nc.gpsimd.dma_start(w4_s[32 * q : 32 * q + 4, :, :], rows)
+        for m in range(2):
+            for q in range(4):
+                load_tab2_scales(m, q)
+        nc.vector.memset(moved[0][:, 0:256], 0)
+        hold(tab_w[1][:, 0:16])
+        load_tab_words(1)
+        nc.vector.memset(tab_s12[:], 0)
+        for q in range(4):
+            load_tab_scales(q)
+        hold(tab2_w[0][:, 0:16])
+        load_tab2_words(0)
+        load_u(0)
+        load_u(1)
+        hold(tab2_w[1][:, 0:16])
+        load_tab2_words(1)
+        load_u(2)
+        load_u(3)
+        nc.gpsimd.memset(moved[0][:, 256:512], 0)
+        for b in range(2, U_PASSES):
+            nc.gpsimd.memset(moved[b - 1][:], 0)
+
+        def cols(lo, n):
+            return slice(lo // 16, (lo + n) // 16)
+
+        gs = {}
+        gw = {}
+        g2s = {}
+        second_scales = []
+        g2w = {}
+
+        def gather_tab_scales(a, lo, n):
+            if lo == HALF:
+                if a == 1:
+                    second_scales.append(keep.tile([P, 2, HALF // 4], I32, name="gs_b", tag="late0", align_bytes=64))
+                t = second_scales[0][:, a - 1, :]
+            else:
+                whole = keep.tile([P, n // 4], I32, name=f"gs{a}_{lo}", align_bytes=64)
+                t = whole[:]
+            nc.vector.tensor_copy(t.bitcast(U8), tab_s[a].bitcast(U8).indirect(offs_t[:, cols(lo, n)]))
+            for c in range(lo, lo + n, N):
+                gs[a, c // N] = t.bitcast(U8)[:, c - lo : c - lo + N]
+
+        def gather_tab_words(a, lo, n):
+            if a == 2 and lo < HALF:
+                t = keep.tile([P, n], I32, name=f"gw{a}_{lo}", tag=f"late{lo // N}", align_bytes=64)
+            else:
+                t = keep.tile([P, n], I32, name=f"gw{a}_{lo}", align_bytes=64)
+            nc.vector.tensor_copy(t[:].bitcast(U32), tab_w[a][:].bitcast(U32).indirect(offs_t[:, cols(lo, n)]))
+            for c in range(lo, lo + n, N):
+                gw[a, c // N] = t[:, c - lo : c - lo + N].bitcast(FP8X4)
+
+        def gather_tab2_scales():
+            packed = keep.tile([P, S // 4], I32, name="g2s", align_bytes=64)
+            nc.vector.tensor_copy(packed[:].bitcast(U8), tab2_s[:].bitcast(U8).indirect(offs2_t[:]))
+            for b in range(U_PASSES):
+                t = packed if b == 0 else moved[b - 1]
+                if b > 0:
+                    nc.scalar.dma_start(t[0:112, :], packed[4 * b : 4 * b + 112, :])
+                for c in range(S // N):
+                    g2s[b, c] = t[:].bitcast(U8)[:, N * c : N * (c + 1)]
+
+        def gather_tab2_words(m, lo, n):
+            if lo == 0:
+                t = keep.tile([P, HALF], I32, name=f"pair{m}", align_bytes=64)
+            else:
+                t = keep.tile([P, N], I32, name=f"pair{m}_{lo}", tag="late1", align_bytes=64)
+            nc.vector.tensor_copy(t[:, 0:n].bitcast(U32), tab2_w[m][:].bitcast(U32).indirect(offs2_t[:, cols(lo, n)]))
+            w = keep.tile([P, 2, 2 * n], U8, name=f"g2w{m}_{lo}", align_bytes=64)
+            nc.vector.tensor_copy(w[:].bitcast(U16), t[:, 0:n].bitcast(U16).rearrange("p (n h) -> p h n", h=2))
+            for h in range(2):
+                for c in range(lo, lo + n, N):
+                    g2w[2 * m + h, c // N] = w[:, h, 2 * (c - lo) : 2 * (c - lo + N)].bitcast(FP4X4)
+
+        u_codes = {}
+        u_scales = {}
+
+        def interleave_u(a):
+            grouped = stage.tile([P, M, 4], BF16, name="grouped", align_bytes=64)
+            nc.scalar.copy(grouped[:], u_raw[a].rearrange("p j n -> p n j"))
+            u_codes[a] = keep.tile([P, M], U32, name=f"u_codes{a}", align_bytes=64)
+            u_scales[a] = keep.tile([P, M], U8, name=f"u_scales{a}", align_bytes=64)
+            return grouped
+
+        def quantise_u(a, grouped):
+            nc.vector.quantize_mx(
+                out=u_codes[a][:].bitcast(FP8X4), scales=u_scales[a][:], in_=grouped[:].rearrange("p n j -> p (n j)")
+            )
+
+        acc = {}
+
+        def banks(c):
+            for m in range(4):
+                acc[c, m] = psum.tile([P, N], F32, name=f"bank{c % 2}{m}")
+
+        def multiply_tab(a, c, start, stop):
+            for m in range(4):
+                nc.tensor.matmul_mx(
+                    out=acc[c, m][:],
+                    lhsT=w4_w[:, a, 64 * m : 64 * (m + 1)].bitcast(FP4X4),
+                    lhsT_scale=w4_s[:, a, 32 * m : 32 * (m + 1)].bitcast(U8),
+                    rhs=gw[a, c],
+                    rhs_scale=gs[a, c],
+                    start=start,
+                    stop=stop,
+                )
+
+        def multiply_tab2(b, c, start, stop):
+            for m in range(4):
+                nc.tensor.matmul_mx(
+                    out=acc[c, m][:],
+                    lhsT=u_codes[b][:, P * m : P * (m + 1)].bitcast(FP8X4),
+                    lhsT_scale=u_scales[b][:, P * m : P * (m + 1)],
+                    rhs=g2w[b, c],
+                    rhs_scale=g2s[b, c],
+                    start=start,
+                    stop=stop,
+                )
+
+        copied = {}
+
+        def empty_banks(c):
+            for m in range(4):
+                copied[c, m] = ring.tile([P, N], F32, name="o")
+                nc.scalar.copy(copied[c, m][:], acc[c, m][:])
+
+        def add_and_store(c):
+            for m in range(4):
+                res = r_t[c // 2][:, m, N * (c % 2) : N * (c % 2 + 1)]
+                if (c, m) in copied:
+                    o = copied[c, m]
+                    nc.vector.tensor_tensor(o[:], o[:], res, ADD)
+                else:
+                    o = ring.tile([P, N], F32, name="o")
+                    nc.vector.tensor_tensor(o[:], acc[c, m][:], res, ADD)
+                nc.sync.dma_start(out[P * m : P * (m + 1), N * c : N * (c + 1)], o[:])
+
+        banks(0)
+        banks(1)
+        gather_tab_scales(0, 0, S)
+        gather_tab_words(0, 0, HALF)
+        for c in (0, 1):
+            multiply_tab(0, c, True, False)
+        gather_tab_words(0, HALF, HALF)
+        gather_tab2_scales()
+        gather_tab_words(1, 0, HALF)
+        gather_tab_words(1, HALF, HALF)
+        load_tab_words(2)
+        gather_tab_scales(1, 0, HALF)
+        for c in (0, 1):
+            multiply_tab(1, c, False, False)
+        g0 = interleave_u(0)
+        g1 = interleave_u(1)
+        gather_tab2_words(0, 0, HALF)
+        quantise_u(0, g0)
+        quantise_u(1, g1)
+        for b in (0, 1):
+            for c in (0, 1):
+                multiply_tab2(b, c, False, False)
+        load_r(0)
+        g2 = interleave_u(2)
+        g3 = interleave_u(3)
+        load_r(1)
+        gather_tab2_words(1, 0, HALF)
+        gather_tab_scales(2, 0, HALF)
+        quantise_u(2, g2)
+        quantise_u(3, g3)
+        for b in (2, 3):
+            for c in (0, 1):
+                multiply_tab2(b, c, False, False)
+        for c in (0, 1):
+            gather_tab_words(2, N * c, N)
+            multiply_tab(2, c, False, True)
+            empty_banks(c)
+
+        gather_tab_scales(1, HALF, HALF)
+        gather_tab_scales(2, HALF, HALF)
+        for c in (2, 3):
+            banks(c)
+            multiply_tab(0, c, True, False)
+            multiply_tab(1, c, False, False)
+        for c in (2, 3):
+            lo = N * c
+            for h in (0, 1):
+                gather_tab2_words(h, lo, N)
+                for b in (2 * h, 2 * h + 1):
+                    multiply_tab2(b, c, False, False)
+            gather_tab_words(2, lo, N)
+            multiply_tab(2, c, False, True)
+            add_and_store(c - 2)
+        add_and_store(2)
+        add_and_store(3)

@@ -26,258 +26,180 @@ def tile_list_tab48_res_kernel(tc, tab, w4_words, w4_scales, tab2, u, r, offs, o
     with ExitStack() as ctx:
         keep = ctx.enter_context(tc.tile_pool(name="keep", bufs=1))
         stage = ctx.enter_context(tc.tile_pool(name="stage", bufs=2))
-        swap = ctx.enter_context(tc.tile_pool(name="swap", bufs=2))
-        ring = ctx.enter_context(tc.tile_pool(name="ring", bufs=8))
+        ring = ctx.enter_context(tc.tile_pool(name="ring", bufs=4))
         psum = ctx.enter_context(tc.psum_pool(name="psum", bufs=1))
 
         offs_t = keep.tile([P, S // 16], U16, name="offs_t")
         offs2_t = keep.tile([P, S // 16], U16, name="offs2_t")
-        tab_s0 = keep.tile([P, T // 4], I32, name="tab_s0", align_bytes=64)
-        tab_s12 = keep.tile([P, 2, T // 4], I32, name="tab_s12", align_bytes=64)
-        tab_s = [tab_s0[:], tab_s12[:, 0, :], tab_s12[:, 1, :]]
-        tab2_s = keep.tile([P, T // 4], I32, name="tab2_s", align_bytes=64)
-        tab_w = [keep.tile([P, T], I32, name=f"tab_w{a}", align_bytes=64) for a in range(2)]
+        tab_rows = keep.tile([P, T // 4], I32, name="tab_rows", align_bytes=64)
+        tab2_rows = keep.tile([P, T // 4], I32, name="tab2_rows", align_bytes=64)
+        tab_planes = keep.tile([P, TAB_PASSES, S // 4], I32, name="tab_planes", align_bytes=64)
+        tab2_planes = keep.tile([P, U_PASSES, S // 4], I32, name="tab2_planes", align_bytes=64)
+        tab_w = [keep.tile([P, T], I32, name=f"tab_w{a}", align_bytes=64) for a in range(TAB_PASSES)]
         tab2_w = [keep.tile([P, T], I32, name=f"tab2_w{m}", align_bytes=64) for m in range(2)]
+        u_raw = [keep.tile([P, 4, M], F32, name=f"u_raw{b}") for b in range(U_PASSES)]
         w4_w = keep.tile([P, TAB_PASSES, M // 2], I32, name="w4_w", align_bytes=64)
         w4_s = keep.tile([P, TAB_PASSES, M // 4], I32, name="w4_s", align_bytes=64)
-        moved = [keep.tile([P, S // 4], I32, name=f"moved{b}", align_bytes=64) for b in range(1, U_PASSES)]
-        u_raw = {}
-        r_t = {}
 
-        def load_tab_words(a):
-            if a == 2:
-                tab_w.append(keep.tile([P, T], I32, name="tab_w2", tag="tab_w1", align_bytes=64))
-            nc.sync.dma_start(tab_w[a][:], tab[a, 0 : 512 * T].rearrange("(p b) -> p b", p=P).bitcast(I32))
-
-        def load_tab2_words(m):
-            nc.sync.dma_start(tab2_w[m][:], tab2[m, 0 : 512 * T].rearrange("(p b) -> p b", p=P).bitcast(I32))
-
-        def load_u(a):
-            if a % 2 == 0:
-                pair = swap.tile([P, 2, 4, M], F32, name="pair_u", tag="swap")
-                u_raw[a] = pair[:, 0, :, :]
-                u_raw[a + 1] = pair[:, 1, :, :]
-            hold(u_raw[a][:, 0, 0:16])
-            nc.sync.dma_start(u_raw[a], u[512 * a : 512 * (a + 1), :].rearrange("(p j) n -> p j n", j=4))
-
-        def load_r(h):
-            r_t[h] = swap.tile([P, 4, HALF], F32, name="r_half", tag="swap")
-            nc.sync.dma_start(r_t[h][:], r[:, HALF * h : HALF * (h + 1)].rearrange("(m p) j -> p m j", p=P))
-
-        tab2_rows = tab2[:, 512 * T : 544 * T].rearrange("m (h q b) -> m h q b", h=2, q=16).bitcast(I32)
-
-        def hold(view):
-            nc.vector.memset(view, 0)
-        tab_rows = tab[1:3, 512 * T : 528 * T].rearrange("a (q b) -> q a b", q=16).bitcast(I32)
-        flat = tab.rearrange("a b -> (a b)")
-
-        def load_tab2_scales(m, q):
-            lo = 32 * q + 8 * m
-            nc.scalar.dma_start(tab2_s[lo : lo + 8, :], tab2_rows[m, :, 4 * q : 4 * q + 4, :])
-
-        def load_tab_scales(q):
-            nc.scalar.dma_start(tab_s12[32 * q : 32 * q + 4, :, :], tab_rows[4 * q : 4 * q + 4, :, :])
-
-        nc.vector.memset(tab2_s[:], 0)
+        nc.vector.memset(tab_rows[:], 0)
+        nc.vector.memset(tab2_rows[0:32, :], 0)
+        nc.vector.memset(tab2_rows[96:128, :], 0)
+        nc.vector.memset(tab2_planes[:], 0)
         nc.gpsimd.memset(w4_s[:], 0)
-        nc.sync.dma_start(offs_t[:], offs)
+
         nc.sync.dma_start(offs2_t[:], offs2)
-        for q in range(4):
-            rows = flat[(512 + 4 * q) * T : (544 + 4 * q) * T].rearrange("(p b) -> p b", p=32).bitcast(I32)
-            nc.sync.dma_start(tab_s0[32 * q : 32 * (q + 1), :], rows)
-        load_tab_words(0)
-        nc.gpsimd.dma_start(w4_w[:], w4_words.rearrange("a p b -> p a b").bitcast(I32))
+        for b in range(U_PASSES):
+            m, h = divmod(b, 2)
+            rows = tab2[m, (512 + 16 * h) * T : (528 + 16 * h) * T].rearrange("(q c) -> q c", q=16).bitcast(I32)
+            nc.sync.dma_start(tab2_rows[32 + b : 96 : 4, :], rows)
+        nc.sync.dma_start(offs_t[:], offs)
+        nc.gpsimd.dma_start(
+            tab_rows[32:80, :], tab[:, 512 * T : 528 * T].rearrange("a (q c) -> q a c", q=16).bitcast(I32)
+        )
+        nc.gpsimd.memset(tab_planes[:], 0)
         for q in range(4):
             rows = w4_scales[:, 4 * q : 4 * q + 4, :].rearrange("a r b -> r a b").bitcast(I32)
             nc.gpsimd.dma_start(w4_s[32 * q : 32 * q + 4, :, :], rows)
-        for m in range(2):
-            for q in range(4):
-                load_tab2_scales(m, q)
-        nc.vector.memset(moved[0][:, 0:256], 0)
-        hold(tab_w[1][:, 0:16])
-        load_tab_words(1)
-        nc.vector.memset(tab_s12[:], 0)
-        for q in range(4):
-            load_tab_scales(q)
-        hold(tab2_w[0][:, 0:16])
-        load_tab2_words(0)
+
+        def load_words(dst, src):
+            nc.sync.dma_start(dst[:], src[0 : 512 * T].rearrange("(p b) -> p b", p=P).bitcast(I32))
+
+        def load_u(b):
+            nc.sync.dma_start(u_raw[b][:], u[512 * b : 512 * (b + 1), :].rearrange("(p j) n -> p j n", j=4))
+
+        load_words(tab2_w[0], tab2[0])
         load_u(0)
         load_u(1)
-        hold(tab2_w[1][:, 0:16])
-        load_tab2_words(1)
+        load_words(tab2_w[1], tab2[1])
         load_u(2)
         load_u(3)
-        nc.gpsimd.memset(moved[0][:, 256:512], 0)
-        for b in range(2, U_PASSES):
-            nc.gpsimd.memset(moved[b - 1][:], 0)
+        nc.sync.dma_start(w4_w[:], w4_words.rearrange("a p b -> p a b").bitcast(I32))
+        for a in range(TAB_PASSES):
+            load_words(tab_w[a], tab[a])
+
+        r_t = {}
+
+        def load_r(h):
+            r_t[h] = keep.tile([P, 4, HALF], F32, name=f"r{h}", tag=f"tab2_w{h}", align_bytes=64)
+            nc.sync.dma_start(r_t[h][:], r[:, HALF * h : HALF * (h + 1)].rearrange("(m p) j -> p m j", p=P))
 
         def cols(lo, n):
             return slice(lo // 16, (lo + n) // 16)
 
-        gs = {}
-        gw = {}
-        g2s = {}
-        second_scales = []
-        g2w = {}
+        def gather_scales(rows, lists, planes, passes, name):
+            picked = keep.tile([P, S // 4], I32, name=name, align_bytes=64)
+            nc.vector.tensor_copy(picked[:].bitcast(U8), rows[:].bitcast(U8).indirect(lists[:]))
+            for q in range(4):
+                lo = 32 + 4 * passes * q
+                nc.gpsimd.dma_start(planes[32 * q : 32 * q + 4, :, :], picked[lo : lo + 4 * passes, :])
 
-        def gather_tab_scales(a, lo, n):
-            if lo == HALF:
-                if a == 1:
-                    second_scales.append(keep.tile([P, 2, HALF // 4], I32, name="gs_b", tag="late0", align_bytes=64))
-                t = second_scales[0][:, a - 1, :]
-            else:
-                whole = keep.tile([P, n // 4], I32, name=f"gs{a}_{lo}", align_bytes=64)
-                t = whole[:]
-            nc.vector.tensor_copy(t.bitcast(U8), tab_s[a].bitcast(U8).indirect(offs_t[:, cols(lo, n)]))
-            for c in range(lo, lo + n, N):
-                gs[a, c // N] = t.bitcast(U8)[:, c - lo : c - lo + N]
+        gw = {}
+        g2w = {}
+        pairs = {}
 
         def gather_tab_words(a, lo, n):
-            if a == 2 and lo < HALF:
-                t = keep.tile([P, n], I32, name=f"gw{a}_{lo}", tag=f"late{lo // N}", align_bytes=64)
-            else:
-                t = keep.tile([P, n], I32, name=f"gw{a}_{lo}", align_bytes=64)
+            t = keep.tile([P, n], I32, name=f"gw{a}_{lo}", align_bytes=64)
             nc.vector.tensor_copy(t[:].bitcast(U32), tab_w[a][:].bitcast(U32).indirect(offs_t[:, cols(lo, n)]))
             for c in range(lo, lo + n, N):
                 gw[a, c // N] = t[:, c - lo : c - lo + N].bitcast(FP8X4)
 
-        def gather_tab2_scales():
-            packed = keep.tile([P, S // 4], I32, name="g2s", align_bytes=64)
-            nc.vector.tensor_copy(packed[:].bitcast(U8), tab2_s[:].bitcast(U8).indirect(offs2_t[:]))
-            for b in range(U_PASSES):
-                t = packed if b == 0 else moved[b - 1]
-                if b > 0:
-                    nc.scalar.dma_start(t[0:112, :], packed[4 * b : 4 * b + 112, :])
-                for c in range(S // N):
-                    g2s[b, c] = t[:].bitcast(U8)[:, N * c : N * (c + 1)]
+        def gather_tab2_words(m, half):
+            t = stage.tile([P, HALF], I32, name="pairs", align_bytes=64)
+            nc.vector.tensor_copy(
+                t[:].bitcast(U32), tab2_w[m][:].bitcast(U32).indirect(offs2_t[:, cols(HALF * half, HALF)])
+            )
+            pairs[m, half] = t
 
-        def gather_tab2_words(m, lo, n):
-            if lo == 0:
-                t = keep.tile([P, HALF], I32, name=f"pair{m}", align_bytes=64)
-            else:
-                t = keep.tile([P, N], I32, name=f"pair{m}_{lo}", tag="late1", align_bytes=64)
-            nc.vector.tensor_copy(t[:, 0:n].bitcast(U32), tab2_w[m][:].bitcast(U32).indirect(offs2_t[:, cols(lo, n)]))
-            w = keep.tile([P, 2, 2 * n], U8, name=f"g2w{m}_{lo}", align_bytes=64)
-            nc.vector.tensor_copy(w[:].bitcast(U16), t[:, 0:n].bitcast(U16).rearrange("p (n h) -> p h n", h=2))
+        def part_tab2_words(m, half):
+            w = keep.tile([P, 2, 2 * HALF], U8, name=f"g2w{m}_{half}", align_bytes=64)
+            nc.vector.tensor_copy(w[:].bitcast(U16), pairs[m, half][:].bitcast(U16).rearrange("p (n h) -> p h n", h=2))
             for h in range(2):
-                for c in range(lo, lo + n, N):
-                    g2w[2 * m + h, c // N] = w[:, h, 2 * (c - lo) : 2 * (c - lo + N)].bitcast(FP4X4)
+                for c in range(2):
+                    g2w[2 * m + h, 2 * half + c] = w[:, h, 2 * N * c : 2 * N * (c + 1)].bitcast(FP4X4)
 
         u_codes = {}
         u_scales = {}
 
-        def interleave_u(a):
+        def quantise_u(b):
             grouped = stage.tile([P, M, 4], BF16, name="grouped", align_bytes=64)
-            nc.scalar.copy(grouped[:], u_raw[a].rearrange("p j n -> p n j"))
-            u_codes[a] = keep.tile([P, M], U32, name=f"u_codes{a}", align_bytes=64)
-            u_scales[a] = keep.tile([P, M], U8, name=f"u_scales{a}", align_bytes=64)
-            return grouped
-
-        def quantise_u(a, grouped):
+            nc.scalar.copy(grouped[:], u_raw[b][:].rearrange("p j n -> p n j"))
+            u_codes[b] = keep.tile([P, M], U32, name=f"u_codes{b}", align_bytes=64)
+            u_scales[b] = keep.tile([P, M], U8, name=f"u_scales{b}", align_bytes=64)
             nc.vector.quantize_mx(
-                out=u_codes[a][:].bitcast(FP8X4), scales=u_scales[a][:], in_=grouped[:].rearrange("p n j -> p (n j)")
+                out=u_codes[b][:].bitcast(FP8X4), scales=u_scales[b][:], in_=grouped[:].rearrange("p n j -> p (n j)")
             )
 
         acc = {}
 
-        def banks(c):
-            for m in range(4):
-                acc[c, m] = psum.tile([P, N], F32, name=f"bank{c % 2}{m}")
+        def bank(c, m):
+            acc[c, m] = psum.tile([P, N], F32, name=f"bank{c % 2}{m}")
 
-        def multiply_tab(a, c, start, stop):
-            for m in range(4):
-                nc.tensor.matmul_mx(
-                    out=acc[c, m][:],
-                    lhsT=w4_w[:, a, 64 * m : 64 * (m + 1)].bitcast(FP4X4),
-                    lhsT_scale=w4_s[:, a, 32 * m : 32 * (m + 1)].bitcast(U8),
-                    rhs=gw[a, c],
-                    rhs_scale=gs[a, c],
-                    start=start,
-                    stop=stop,
-                )
+        def multiply_tab(a, c, m):
+            nc.tensor.matmul_mx(
+                out=acc[c, m][:],
+                lhsT=w4_w[:, a, 64 * m : 64 * (m + 1)].bitcast(FP4X4),
+                lhsT_scale=w4_s[:, a, 32 * m : 32 * (m + 1)].bitcast(U8),
+                rhs=gw[a, c],
+                rhs_scale=tab_planes[:, a, 128 * c : 128 * (c + 1)].bitcast(U8),
+                start=False,
+                stop=a == TAB_PASSES - 1,
+            )
 
-        def multiply_tab2(b, c, start, stop):
-            for m in range(4):
-                nc.tensor.matmul_mx(
-                    out=acc[c, m][:],
-                    lhsT=u_codes[b][:, P * m : P * (m + 1)].bitcast(FP8X4),
-                    lhsT_scale=u_scales[b][:, P * m : P * (m + 1)],
-                    rhs=g2w[b, c],
-                    rhs_scale=g2s[b, c],
-                    start=start,
-                    stop=stop,
-                )
+        def multiply_tab2(b, c, m):
+            nc.tensor.matmul_mx(
+                out=acc[c, m][:],
+                lhsT=u_codes[b][:, P * m : P * (m + 1)].bitcast(FP8X4),
+                lhsT_scale=u_scales[b][:, P * m : P * (m + 1)],
+                rhs=g2w[b, c],
+                rhs_scale=tab2_planes[:, b, 128 * c : 128 * (c + 1)].bitcast(U8),
+                start=b == 0,
+                stop=False,
+            )
 
-        copied = {}
+        gather_scales(tab2_rows, offs2_t, tab2_planes, U_PASSES, "tab2_picked")
+        gather_scales(tab_rows, offs_t, tab_planes, TAB_PASSES, "tab_picked")
 
-        def empty_banks(c):
+        for c in range(2):
             for m in range(4):
-                copied[c, m] = ring.tile([P, N], F32, name="o")
-                nc.scalar.copy(copied[c, m][:], acc[c, m][:])
+                bank(c, m)
+        for pair in range(2):
+            for half in range(2):
+                gather_tab2_words(pair, half)
+            for half in range(2):
+                part_tab2_words(pair, half)
+            load_r(pair)
+            for b in (2 * pair, 2 * pair + 1):
+                quantise_u(b)
+                for c in range(2):
+                    for m in range(4):
+                        multiply_tab2(b, c, m)
+        for a in range(TAB_PASSES - 1):
+            for half in range(2):
+                gather_tab_words(a, HALF * half, HALF)
+            for c in range(2):
+                for m in range(4):
+                    multiply_tab(a, c, m)
+        last = TAB_PASSES - 1
+        sums = {}
+        for c in range(2):
+            gather_tab_words(last, N * c, N)
+            sums[c] = keep.tile([P, 4, N], F32, name=f"sums{c}")
+            for m in range(4):
+                multiply_tab(last, c, m)
+                nc.scalar.copy(sums[c][:, m, :], acc[c, m][:])
+        for c in range(2, 4):
+            gather_tab_words(last, N * c, N)
+        for c in range(2):
+            nc.vector.tensor_tensor(sums[c][:], sums[c][:], r_t[0][:, :, N * c : N * (c + 1)], ADD)
+            nc.sync.dma_start(out[:, N * c : N * (c + 1)].rearrange("(m p) j -> p m j", p=P), sums[c][:])
 
-        def add_and_store(c):
+        for c in range(2, 4):
             for m in range(4):
-                res = r_t[c // 2][:, m, N * (c % 2) : N * (c % 2 + 1)]
-                if (c, m) in copied:
-                    o = copied[c, m]
-                    nc.vector.tensor_tensor(o[:], o[:], res, ADD)
-                else:
-                    o = ring.tile([P, N], F32, name="o")
-                    nc.vector.tensor_tensor(o[:], acc[c, m][:], res, ADD)
+                bank(c, m)
+                for b in range(U_PASSES):
+                    multiply_tab2(b, c, m)
+                for a in range(TAB_PASSES):
+                    multiply_tab(a, c, m)
+                o = ring.tile([P, N], F32, name="o")
+                nc.vector.tensor_tensor(o[:], acc[c, m][:], r_t[1][:, m, N * (c - 2) : N * (c - 1)], ADD)
                 nc.sync.dma_start(out[P * m : P * (m + 1), N * c : N * (c + 1)], o[:])
-
-        banks(0)
-        banks(1)
-        gather_tab_scales(0, 0, S)
-        gather_tab_words(0, 0, HALF)
-        for c in (0, 1):
-            multiply_tab(0, c, True, False)
-        gather_tab_words(0, HALF, HALF)
-        gather_tab2_scales()
-        gather_tab_words(1, 0, HALF)
-        gather_tab_words(1, HALF, HALF)
-        load_tab_words(2)
-        gather_tab_scales(1, 0, HALF)
-        for c in (0, 1):
-            multiply_tab(1, c, False, False)
-        g0 = interleave_u(0)
-        g1 = interleave_u(1)
-        gather_tab2_words(0, 0, HALF)
-        quantise_u(0, g0)
-        quantise_u(1, g1)
-        for b in (0, 1):
-            for c in (0, 1):
-                multiply_tab2(b, c, False, False)
-        load_r(0)
-        g2 = interleave_u(2)
-        g3 = interleave_u(3)
-        load_r(1)
-        gather_tab2_words(1, 0, HALF)
-        gather_tab_scales(2, 0, HALF)
-        quantise_u(2, g2)
-        quantise_u(3, g3)
-        for b in (2, 3):
-            for c in (0, 1):
-                multiply_tab2(b, c, False, False)
-        for c in (0, 1):
-            gather_tab_words(2, N * c, N)
-            multiply_tab(2, c, False, True)
-            empty_banks(c)
-
-        gather_tab_scales(1, HALF, HALF)
-        gather_tab_scales(2, HALF, HALF)
-        for c in (2, 3):
-            banks(c)
-            multiply_tab(0, c, True, False)
-            multiply_tab(1, c, False, False)
-        for c in (2, 3):
-            lo = N * c
-            for h in (0, 1):
-                gather_tab2_words(h, lo, N)
-                for b in (2 * h, 2 * h + 1):
-                    multiply_tab2(b, c, False, False)
-            gather_tab_words(2, lo, N)
-            multiply_tab(2, c, False, True)
-            add_and_store(c - 2)
-        add_and_store(2)
-        add_and_store(3)

@@ -31,21 +31,16 @@ def tile_list_tab48_res_kernel(tc, tab, w4_words, w4_scales, tab2, u, r, offs, o
 
         offs_t = keep.tile([P, S // 16], U16, name="offs_t")
         offs2_t = keep.tile([P, S // 16], U16, name="offs2_t")
-        tab_rows = keep.tile([P, T // 4], I32, name="tab_rows", align_bytes=64)
-        tab2_rows = keep.tile([P, T // 4], I32, name="tab2_rows", align_bytes=64)
+        tab_rows = keep.tile([P, T // 4], I32, name="tab_rows", tag="small", align_bytes=64)
+        tab2_rows = keep.tile([P, T // 4], I32, name="tab2_rows", tag="big2", align_bytes=64)
         tab_planes = keep.tile([P, TAB_PASSES, S // 4], I32, name="tab_planes", align_bytes=64)
         tab2_planes = keep.tile([P, U_PASSES, S // 4], I32, name="tab2_planes", align_bytes=64)
-        tab_w = [keep.tile([P, T], I32, name=f"tab_w{a}", align_bytes=64) for a in range(TAB_PASSES)]
-        tab2_w = [keep.tile([P, T], I32, name=f"tab2_w{m}", align_bytes=64) for m in range(2)]
-        u_raw = [keep.tile([P, 4, M], F32, name=f"u_raw{b}") for b in range(U_PASSES)]
-        w4_w = keep.tile([P, TAB_PASSES, M // 2], I32, name="w4_w", align_bytes=64)
-        w4_s = keep.tile([P, TAB_PASSES, M // 4], I32, name="w4_s", align_bytes=64)
 
         nc.vector.memset(tab_rows[:], 0)
         nc.vector.memset(tab2_rows[0:32, :], 0)
         nc.vector.memset(tab2_rows[96:128, :], 0)
         nc.vector.memset(tab2_planes[:], 0)
-        nc.gpsimd.memset(w4_s[:], 0)
+        nc.vector.memset(tab_planes[:], 0)
 
         nc.sync.dma_start(offs2_t[:], offs2)
         for b in range(U_PASSES):
@@ -53,35 +48,44 @@ def tile_list_tab48_res_kernel(tc, tab, w4_words, w4_scales, tab2, u, r, offs, o
             rows = tab2[m, (512 + 16 * h) * T : (528 + 16 * h) * T].rearrange("(q c) -> q c", q=16).bitcast(I32)
             nc.sync.dma_start(tab2_rows[32 + b : 96 : 4, :], rows)
         nc.sync.dma_start(offs_t[:], offs)
-        nc.gpsimd.dma_start(
+        nc.scalar.dma_start(
             tab_rows[32:80, :], tab[:, 512 * T : 528 * T].rearrange("a (q c) -> q a c", q=16).bitcast(I32)
         )
-        nc.gpsimd.memset(tab_planes[:], 0)
-        for q in range(4):
-            rows = w4_scales[:, 4 * q : 4 * q + 4, :].rearrange("a r b -> r a b").bitcast(I32)
-            nc.gpsimd.dma_start(w4_s[32 * q : 32 * q + 4, :, :], rows)
 
-        def load_words(dst, src):
-            nc.sync.dma_start(dst[:], src[0 : 512 * T].rearrange("(p b) -> p b", p=P).bitcast(I32))
-
-        def load_u(b):
-            nc.sync.dma_start(u_raw[b][:], u[512 * b : 512 * (b + 1), :].rearrange("(p j) n -> p j n", j=4))
-
-        load_words(tab2_w[0], tab2[0])
-        load_u(0)
-        load_u(1)
-        load_words(tab2_w[1], tab2[1])
-        load_u(2)
-        load_u(3)
-        nc.sync.dma_start(w4_w[:], w4_words.rearrange("a p b -> p a b").bitcast(I32))
-        for a in range(TAB_PASSES):
-            load_words(tab_w[a], tab[a])
-
+        tab_w = {}
+        tab2_w = {}
+        u_raw = {}
         r_t = {}
+        w4 = {}
 
-        def load_r(h):
-            r_t[h] = keep.tile([P, 4, HALF], F32, name=f"r{h}", tag=f"tab2_w{h}", align_bytes=64)
+        def load_words(into, key, src, tag):
+            into[key] = keep.tile([P, T], I32, name=f"words_{tag}", tag=tag, align_bytes=64)
+            nc.sync.dma_start(into[key][:], src[0 : 512 * T].rearrange("(p b) -> p b", p=P).bitcast(I32))
+
+        def load_u(b, tag):
+            both = keep.tile([P, 2, 4, M], F32, name=f"u_raw{b}", tag=tag, align_bytes=64)
+            for i in range(2):
+                u_raw[b + i] = both[:, i, :, :]
+                rows = u[512 * (b + i) : 512 * (b + i + 1), :]
+                nc.sync.dma_start(u_raw[b + i], rows.rearrange("(p j) n -> p j n", j=4))
+
+        def load_w4():
+            both = keep.tile([P, TAB_PASSES, M // 2 + M // 4], I32, name="w4_both", tag="small", align_bytes=64)
+            w4["words"] = both[:, :, 0 : M // 2]
+            w4["scales"] = both[:, :, M // 2 :]
+            nc.gpsimd.memset(w4["scales"], 0)
+            nc.sync.dma_start(w4["words"], w4_words.rearrange("a p b -> p a b").bitcast(I32))
+            for q in range(4):
+                rows = w4_scales[:, 4 * q : 4 * q + 4, :].rearrange("a r b -> r a b").bitcast(I32)
+                nc.sync.dma_start(both[32 * q : 32 * q + 4, :, M // 2 :], rows)
+
+        def load_r(h, tag):
+            r_t[h] = keep.tile([P, 4, HALF], F32, name=f"r{h}", tag=tag, align_bytes=64)
             nc.sync.dma_start(r_t[h][:], r[:, HALF * h : HALF * (h + 1)].rearrange("(m p) j -> p m j", p=P))
+
+        load_words(tab2_w, 0, tab2[0], "big0")
+        load_u(0, "u_first")
+        load_words(tab2_w, 1, tab2[1], "big1")
 
         def cols(lo, n):
             return slice(lo // 16, (lo + n) // 16)
@@ -91,7 +95,7 @@ def tile_list_tab48_res_kernel(tc, tab, w4_words, w4_scales, tab2, u, r, offs, o
             nc.vector.tensor_copy(picked[:].bitcast(U8), rows[:].bitcast(U8).indirect(lists[:]))
             for q in range(4):
                 lo = 32 + 4 * passes * q
-                nc.gpsimd.dma_start(planes[32 * q : 32 * q + 4, :, :], picked[lo : lo + 4 * passes, :])
+                nc.sync.dma_start(planes[32 * q : 32 * q + 4, :, :], picked[lo : lo + 4 * passes, :])
 
         gw = {}
         g2w = {}
@@ -122,7 +126,7 @@ def tile_list_tab48_res_kernel(tc, tab, w4_words, w4_scales, tab2, u, r, offs, o
 
         def quantise_u(b):
             grouped = stage.tile([P, M, 4], BF16, name="grouped", align_bytes=64)
-            nc.scalar.copy(grouped[:], u_raw[b][:].rearrange("p j n -> p n j"))
+            nc.scalar.copy(grouped[:], u_raw[b].rearrange("p j n -> p n j"))
             u_codes[b] = keep.tile([P, M], U32, name=f"u_codes{b}", align_bytes=64)
             u_scales[b] = keep.tile([P, M], U8, name=f"u_scales{b}", align_bytes=64)
             nc.vector.quantize_mx(
@@ -137,8 +141,8 @@ def tile_list_tab48_res_kernel(tc, tab, w4_words, w4_scales, tab2, u, r, offs, o
         def multiply_tab(a, c, m):
             nc.tensor.matmul_mx(
                 out=acc[c, m][:],
-                lhsT=w4_w[:, a, 64 * m : 64 * (m + 1)].bitcast(FP4X4),
-                lhsT_scale=w4_s[:, a, 32 * m : 32 * (m + 1)].bitcast(U8),
+                lhsT=w4["words"][:, a, 64 * m : 64 * (m + 1)].bitcast(FP4X4),
+                lhsT_scale=w4["scales"][:, a, 32 * m : 32 * (m + 1)].bitcast(U8),
                 rhs=gw[a, c],
                 rhs_scale=tab_planes[:, a, 128 * c : 128 * (c + 1)].bitcast(U8),
                 start=False,
@@ -157,7 +161,9 @@ def tile_list_tab48_res_kernel(tc, tab, w4_words, w4_scales, tab2, u, r, offs, o
             )
 
         gather_scales(tab2_rows, offs2_t, tab2_planes, U_PASSES, "tab2_picked")
+        load_u(2, "big2")
         gather_scales(tab_rows, offs_t, tab_planes, TAB_PASSES, "tab_picked")
+        load_w4()
 
         for c in range(2):
             for m in range(4):
@@ -167,15 +173,17 @@ def tile_list_tab48_res_kernel(tc, tab, w4_words, w4_scales, tab2, u, r, offs, o
                 gather_tab2_words(pair, half)
             for half in range(2):
                 part_tab2_words(pair, half)
-            load_r(pair)
+            load_words(tab_w, pair, tab[pair], f"big{pair}")
             for b in (2 * pair, 2 * pair + 1):
                 quantise_u(b)
                 for c in range(2):
                     for m in range(4):
                         multiply_tab2(b, c, m)
+        load_words(tab_w, 2, tab[2], "big2")
         for a in range(TAB_PASSES - 1):
             for half in range(2):
                 gather_tab_words(a, HALF * half, HALF)
+            load_r(a, f"big{a}")
             for c in range(2):
                 for m in range(4):
                     multiply_tab(a, c, m)

@@ -25,7 +25,6 @@ def tile_list_tab48_res_kernel(tc, tab, w4_words, w4_scales, tab2, u, r, offs, o
     nc = tc.nc
     with ExitStack() as ctx:
         keep = ctx.enter_context(tc.tile_pool(name="keep", bufs=1))
-        stage = ctx.enter_context(tc.tile_pool(name="stage", bufs=2))
         ring = ctx.enter_context(tc.tile_pool(name="ring", bufs=4))
         psum = ctx.enter_context(tc.psum_pool(name="psum", bufs=1))
 
@@ -39,8 +38,8 @@ def tile_list_tab48_res_kernel(tc, tab, w4_words, w4_scales, tab2, u, r, offs, o
         nc.vector.memset(tab_rows[:], 0)
         nc.vector.memset(tab2_rows[0:32, :], 0)
         nc.vector.memset(tab2_rows[96:128, :], 0)
-        nc.vector.memset(tab2_planes[:], 0)
-        nc.vector.memset(tab_planes[:], 0)
+        nc.gpsimd.memset(tab2_planes[:], 0)
+        nc.gpsimd.memset(tab_planes[:], 0)
 
         nc.sync.dma_start(offs2_t[:], offs2)
         for b in range(U_PASSES):
@@ -77,11 +76,13 @@ def tile_list_tab48_res_kernel(tc, tab, w4_words, w4_scales, tab2, u, r, offs, o
             nc.sync.dma_start(w4["words"], w4_words.rearrange("a p b -> p a b").bitcast(I32))
             for q in range(4):
                 rows = w4_scales[:, 4 * q : 4 * q + 4, :].rearrange("a r b -> r a b").bitcast(I32)
-                nc.sync.dma_start(both[32 * q : 32 * q + 4, :, M // 2 :], rows)
+                nc.gpsimd.dma_start(both[32 * q : 32 * q + 4, :, M // 2 :], rows)
 
-        def load_r(h, tag):
-            r_t[h] = keep.tile([P, 4, HALF], F32, name=f"r{h}", tag=tag, align_bytes=64)
-            nc.sync.dma_start(r_t[h][:], r[:, HALF * h : HALF * (h + 1)].rearrange("(m p) j -> p m j", p=P))
+        def load_r(c, chunks, tag):
+            t = keep.tile([P, 4, N * chunks], F32, name=f"r{c}", tag=tag, align_bytes=64)
+            nc.sync.dma_start(t[:], r[:, N * c : N * (c + chunks)].rearrange("(m p) j -> p m j", p=P))
+            for i in range(chunks):
+                r_t[c + i] = t[:, :, N * i : N * (i + 1)]
 
         load_words(tab2_w, 0, tab2[0], "big0")
         load_u(0, "u_first")
@@ -95,20 +96,19 @@ def tile_list_tab48_res_kernel(tc, tab, w4_words, w4_scales, tab2, u, r, offs, o
             nc.vector.tensor_copy(picked[:].bitcast(U8), rows[:].bitcast(U8).indirect(lists[:]))
             for q in range(4):
                 lo = 32 + 4 * passes * q
-                nc.sync.dma_start(planes[32 * q : 32 * q + 4, :, :], picked[lo : lo + 4 * passes, :])
+                nc.gpsimd.dma_start(planes[32 * q : 32 * q + 4, :, :], picked[lo : lo + 4 * passes, :])
 
         gw = {}
         g2w = {}
         pairs = {}
 
-        def gather_tab_words(a, lo, n):
-            t = keep.tile([P, n], I32, name=f"gw{a}_{lo}", align_bytes=64)
-            nc.vector.tensor_copy(t[:].bitcast(U32), tab_w[a][:].bitcast(U32).indirect(offs_t[:, cols(lo, n)]))
+        def gather_tab_words(a, lo, n, t):
+            nc.vector.tensor_copy(t.bitcast(U32), tab_w[a][:].bitcast(U32).indirect(offs_t[:, cols(lo, n)]))
             for c in range(lo, lo + n, N):
                 gw[a, c // N] = t[:, c - lo : c - lo + N].bitcast(FP8X4)
 
-        def gather_tab2_words(m, half):
-            t = stage.tile([P, HALF], I32, name="pairs", align_bytes=64)
+        def gather_tab2_words(m, half, tag):
+            t = keep.tile([P, HALF], I32, name=f"pairs{m}{half}", tag=tag, align_bytes=64)
             nc.vector.tensor_copy(
                 t[:].bitcast(U32), tab2_w[m][:].bitcast(U32).indirect(offs2_t[:, cols(HALF * half, HALF)])
             )
@@ -124,8 +124,8 @@ def tile_list_tab48_res_kernel(tc, tab, w4_words, w4_scales, tab2, u, r, offs, o
         u_codes = {}
         u_scales = {}
 
-        def quantise_u(b):
-            grouped = stage.tile([P, M, 4], BF16, name="grouped", align_bytes=64)
+        def quantise_u(b, tag):
+            grouped = keep.tile([P, M, 4], BF16, name=f"grouped{b}", tag=tag, align_bytes=64)
             nc.scalar.copy(grouped[:], u_raw[b].rearrange("p j n -> p n j"))
             u_codes[b] = keep.tile([P, M], U32, name=f"u_codes{b}", align_bytes=64)
             u_scales[b] = keep.tile([P, M], U8, name=f"u_scales{b}", align_bytes=64)
@@ -138,7 +138,7 @@ def tile_list_tab48_res_kernel(tc, tab, w4_words, w4_scales, tab2, u, r, offs, o
         def bank(c, m):
             acc[c, m] = psum.tile([P, N], F32, name=f"bank{c % 2}{m}")
 
-        def multiply_tab(a, c, m):
+        def multiply_tab(a, c, m, stop):
             nc.tensor.matmul_mx(
                 out=acc[c, m][:],
                 lhsT=w4["words"][:, a, 64 * m : 64 * (m + 1)].bitcast(FP4X4),
@@ -146,7 +146,7 @@ def tile_list_tab48_res_kernel(tc, tab, w4_words, w4_scales, tab2, u, r, offs, o
                 rhs=gw[a, c],
                 rhs_scale=tab_planes[:, a, 128 * c : 128 * (c + 1)].bitcast(U8),
                 start=False,
-                stop=a == TAB_PASSES - 1,
+                stop=stop,
             )
 
         def multiply_tab2(b, c, m):
@@ -168,46 +168,74 @@ def tile_list_tab48_res_kernel(tc, tab, w4_words, w4_scales, tab2, u, r, offs, o
         for c in range(2):
             for m in range(4):
                 bank(c, m)
-        for pair in range(2):
-            for half in range(2):
-                gather_tab2_words(pair, half)
-            for half in range(2):
-                part_tab2_words(pair, half)
-            load_words(tab_w, pair, tab[pair], f"big{pair}")
-            for b in (2 * pair, 2 * pair + 1):
-                quantise_u(b)
-                for c in range(2):
-                    for m in range(4):
-                        multiply_tab2(b, c, m)
-        load_words(tab_w, 2, tab[2], "big2")
-        for a in range(TAB_PASSES - 1):
-            for half in range(2):
-                gather_tab_words(a, HALF * half, HALF)
-            load_r(a, f"big{a}")
+
+        def first_half_tab2(b):
             for c in range(2):
                 for m in range(4):
-                    multiply_tab(a, c, m)
+                    multiply_tab2(b, c, m)
+
+        gather_tab2_words(0, 0, "stage0")
+        part_tab2_words(0, 0)
+        quantise_u(0, "stage1")
+        first_half_tab2(0)
+        quantise_u(1, "stage2")
+        first_half_tab2(1)
+        load_words(tab_w, 0, tab[0], "u_first")
+        gather_tab2_words(0, 1, "stage2")
+        load_words(tab_w, 1, tab[1], "big0")
+        gather_tab2_words(1, 0, "stage0")
+        part_tab2_words(0, 1)
+        part_tab2_words(1, 0)
+        load_words(tab_w, 2, tab[2], "stage0")
+        quantise_u(2, "stage1")
+        first_half_tab2(2)
+        gather_tab2_words(1, 1, "stage1")
+        quantise_u(3, "stage2")
+        first_half_tab2(3)
+        part_tab2_words(1, 1)
+        load_r(0, 1, "stage1")
+        load_r(1, 1, "big2")
+        load_r(2, 2, "stage2")
         last = TAB_PASSES - 1
+        for a in range(last):
+            first = keep.tile([P, HALF], I32, name=f"gw{a}_first", align_bytes=64)
+            gather_tab_words(a, 0, HALF, first[:])
+            for c in range(2):
+                for m in range(4):
+                    multiply_tab(a, c, m, False)
         sums = {}
         for c in range(2):
-            gather_tab_words(last, N * c, N)
+            closing = keep.tile([P, N], I32, name=f"gw_closing{c}", tag=f"late{c}", align_bytes=64)
+            gather_tab_words(last, N * c, N, closing[:])
             sums[c] = keep.tile([P, 4, N], F32, name=f"sums{c}")
             for m in range(4):
-                multiply_tab(last, c, m)
+                multiply_tab(last, c, m, True)
                 nc.scalar.copy(sums[c][:, m, :], acc[c, m][:])
-        for c in range(2, 4):
-            gather_tab_words(last, N * c, N)
-        for c in range(2):
-            nc.vector.tensor_tensor(sums[c][:], sums[c][:], r_t[0][:, :, N * c : N * (c + 1)], ADD)
+
+        filler = keep.tile([P, N], I32, name="gw_last2", align_bytes=64)
+        gather_tab_words(last, 2 * N, N, filler[:])
+        late = keep.tile([P, last, N], I32, name="gw_late2", tag="late0", align_bytes=64)
+        for a in range(last):
+            gather_tab_words(a, 2 * N, N, late[:, a, :])
+
+        def add_and_store_sums(c):
+            nc.vector.tensor_tensor(sums[c][:], sums[c][:], r_t[c], ADD)
             nc.sync.dma_start(out[:, N * c : N * (c + 1)].rearrange("(m p) j -> p m j", p=P), sums[c][:])
 
-        for c in range(2, 4):
+        add_and_store_sums(0)
+        latest = keep.tile([P, TAB_PASSES, N], I32, name="gw_late3", tag="stage1", align_bytes=64)
+        for a in range(TAB_PASSES):
+            gather_tab_words(a, 3 * N, N, latest[:, a, :])
+        add_and_store_sums(1)
+
+        for c in (2, 3):
             for m in range(4):
                 bank(c, m)
                 for b in range(U_PASSES):
                     multiply_tab2(b, c, m)
+            for m in range(4):
                 for a in range(TAB_PASSES):
-                    multiply_tab(a, c, m)
+                    multiply_tab(a, c, m, a == last)
                 o = ring.tile([P, N], F32, name="o")
-                nc.vector.tensor_tensor(o[:], acc[c, m][:], r_t[1][:, m, N * (c - 2) : N * (c - 1)], ADD)
+                nc.vector.tensor_tensor(o[:], acc[c, m][:], r_t[c][:, m, :], ADD)
                 nc.sync.dma_start(out[P * m : P * (m + 1), N * c : N * (c + 1)], o[:])

@@ -32,14 +32,19 @@ def tile_list_tab48_res_kernel(tc, tab, w4_words, w4_scales, tab2, u, r, offs, o
         offs2_t = keep.tile([P, S // 16], U16, name="offs2_t")
         tab_rows = keep.tile([P, T // 4], I32, name="tab_rows", tag="small", align_bytes=64)
         tab2_rows = keep.tile([P, T // 4], I32, name="tab2_rows", tag="big2", align_bytes=64)
-        tab_planes = keep.tile([P, TAB_PASSES, S // 4], I32, name="tab_planes", align_bytes=64)
-        tab2_planes = keep.tile([P, U_PASSES, S // 4], I32, name="tab2_planes", align_bytes=64)
+        tab_planes = {0: keep.tile([P, TAB_PASSES, HALF // 4], I32, name="tab_planes0", align_bytes=64)}
+        tab2_planes = {0: keep.tile([P, U_PASSES, HALF // 4], I32, name="tab2_planes0", align_bytes=64)}
 
-        nc.vector.memset(tab_rows[:], 0)
+        nc.gpsimd.memset(tab_rows[:], 0)
         nc.vector.memset(tab2_rows[0:32, :], 0)
         nc.vector.memset(tab2_rows[96:128, :], 0)
-        nc.gpsimd.memset(tab2_planes[:], 0)
-        nc.gpsimd.memset(tab_planes[:], 0)
+        w4_s = keep.tile([P, TAB_PASSES, M // 4], I32, name="w4_s", align_bytes=64)
+        nc.gpsimd.memset(w4_s[:], 0)
+        for q in (0, 2, 1, 3):
+            rows = w4_scales[:, 4 * q : 4 * q + 4, :].rearrange("a r b -> r a b").bitcast(I32)
+            nc.gpsimd.dma_start(w4_s[32 * q : 32 * q + 4, :, :], rows)
+        nc.gpsimd.memset(tab2_planes[0][:], 0)
+        nc.gpsimd.memset(tab_planes[0][:], 0)
 
         nc.sync.dma_start(offs2_t[:], offs2)
         for b in range(U_PASSES):
@@ -68,15 +73,9 @@ def tile_list_tab48_res_kernel(tc, tab, w4_words, w4_scales, tab2, u, r, offs, o
                 rows = u[512 * (b + i) : 512 * (b + i + 1), :]
                 nc.sync.dma_start(u_raw[b + i], rows.rearrange("(p j) n -> p j n", j=4))
 
-        def load_w4():
-            both = keep.tile([P, TAB_PASSES, M // 2 + M // 4], I32, name="w4_both", tag="small", align_bytes=64)
-            w4["words"] = both[:, :, 0 : M // 2]
-            w4["scales"] = both[:, :, M // 2 :]
-            nc.gpsimd.memset(w4["scales"], 0)
-            nc.sync.dma_start(w4["words"], w4_words.rearrange("a p b -> p a b").bitcast(I32))
-            for q in range(4):
-                rows = w4_scales[:, 4 * q : 4 * q + 4, :].rearrange("a r b -> r a b").bitcast(I32)
-                nc.gpsimd.dma_start(both[32 * q : 32 * q + 4, :, M // 2 :], rows)
+        def load_w4_words():
+            w4["words"] = keep.tile([P, TAB_PASSES, M // 2], I32, name="w4_w", tag="small", align_bytes=64)
+            nc.sync.dma_start(w4["words"][:], w4_words.rearrange("a p b -> p a b").bitcast(I32))
 
         def load_r(c, chunks, tag):
             t = keep.tile([P, 4, N * chunks], F32, name=f"r{c}", tag=tag, align_bytes=64)
@@ -91,12 +90,16 @@ def tile_list_tab48_res_kernel(tc, tab, w4_words, w4_scales, tab2, u, r, offs, o
         def cols(lo, n):
             return slice(lo // 16, (lo + n) // 16)
 
-        def gather_scales(rows, lists, planes, passes, name):
+        def gather_scales(rows, lists, name):
             picked = keep.tile([P, S // 4], I32, name=name, align_bytes=64)
             nc.vector.tensor_copy(picked[:].bitcast(U8), rows[:].bitcast(U8).indirect(lists[:]))
-            for q in range(4):
+            return picked
+
+        def move_scales(picked, planes, passes, half, queue):
+            for q in (0, 2, 1, 3):
                 lo = 32 + 4 * passes * q
-                nc.gpsimd.dma_start(planes[32 * q : 32 * q + 4, :, :], picked[lo : lo + 4 * passes, :])
+                words = slice(half * HALF // 4, (half + 1) * HALF // 4)
+                queue.dma_start(planes[32 * q : 32 * q + 4, :, :], picked[lo : lo + 4 * passes, words])
 
         gw = {}
         g2w = {}
@@ -142,9 +145,9 @@ def tile_list_tab48_res_kernel(tc, tab, w4_words, w4_scales, tab2, u, r, offs, o
             nc.tensor.matmul_mx(
                 out=acc[c, m][:],
                 lhsT=w4["words"][:, a, 64 * m : 64 * (m + 1)].bitcast(FP4X4),
-                lhsT_scale=w4["scales"][:, a, 32 * m : 32 * (m + 1)].bitcast(U8),
+                lhsT_scale=w4_s[:, a, 32 * m : 32 * (m + 1)].bitcast(U8),
                 rhs=gw[a, c],
-                rhs_scale=tab_planes[:, a, 128 * c : 128 * (c + 1)].bitcast(U8),
+                rhs_scale=tab_planes[c // 2][:, a, 128 * (c % 2) : 128 * (c % 2 + 1)].bitcast(U8),
                 start=False,
                 stop=stop,
             )
@@ -155,15 +158,17 @@ def tile_list_tab48_res_kernel(tc, tab, w4_words, w4_scales, tab2, u, r, offs, o
                 lhsT=u_codes[b][:, P * m : P * (m + 1)].bitcast(FP8X4),
                 lhsT_scale=u_scales[b][:, P * m : P * (m + 1)],
                 rhs=g2w[b, c],
-                rhs_scale=tab2_planes[:, b, 128 * c : 128 * (c + 1)].bitcast(U8),
+                rhs_scale=tab2_planes[c // 2][:, b, 128 * (c % 2) : 128 * (c % 2 + 1)].bitcast(U8),
                 start=b == 0,
                 stop=False,
             )
 
-        gather_scales(tab2_rows, offs2_t, tab2_planes, U_PASSES, "tab2_picked")
+        tab2_picked = gather_scales(tab2_rows, offs2_t, "tab2_picked")
+        move_scales(tab2_picked, tab2_planes[0], U_PASSES, 0, nc.gpsimd)
         load_u(2, "big2")
-        gather_scales(tab_rows, offs_t, tab_planes, TAB_PASSES, "tab_picked")
-        load_w4()
+        tab_picked = gather_scales(tab_rows, offs_t, "tab_picked")
+        move_scales(tab_picked, tab_planes[0], TAB_PASSES, 0, nc.gpsimd)
+        load_w4_words()
 
         for c in range(2):
             for m in range(4):
@@ -187,22 +192,31 @@ def tile_list_tab48_res_kernel(tc, tab, w4_words, w4_scales, tab2, u, r, offs, o
         part_tab2_words(0, 1)
         part_tab2_words(1, 0)
         load_words(tab_w, 2, tab[2], "stage0")
+        late_planes = keep.tile([P, U_PASSES + TAB_PASSES, HALF // 4], I32, name="late_planes", tag="stage2", align_bytes=64)
+        nc.gpsimd.memset(late_planes[:], 0)
+        tab2_planes[1] = late_planes[:, 0:U_PASSES, :]
+        tab_planes[1] = late_planes[:, U_PASSES:, :]
+        move_scales(tab2_picked, tab2_planes[1], U_PASSES, 1, nc.sync)
+        move_scales(tab_picked, tab_planes[1], TAB_PASSES, 1, nc.sync)
         quantise_u(2, "stage1")
         first_half_tab2(2)
-        gather_tab2_words(1, 1, "stage1")
-        quantise_u(3, "stage2")
+        quantise_u(3, "stage3")
         first_half_tab2(3)
+        load_r(0, 1, "big2")
+        gather_tab2_words(1, 1, "stage3")
+        load_r(1, 1, "big1")
         part_tab2_words(1, 1)
-        load_r(0, 1, "stage1")
-        load_r(1, 1, "big2")
-        load_r(2, 2, "stage2")
+        load_r(2, 2, "stage3")
         last = TAB_PASSES - 1
         for a in range(last):
-            first = keep.tile([P, HALF], I32, name=f"gw{a}_first", align_bytes=64)
-            gather_tab_words(a, 0, HALF, first[:])
             for c in range(2):
+                first = keep.tile([P, N], I32, name=f"gw{a}_first{c}", align_bytes=64)
+                gather_tab_words(a, N * c, N, first[:])
                 for m in range(4):
                     multiply_tab(a, c, m, False)
+            if a == 0:
+                second = keep.tile([P, HALF], I32, name="gw0_second", align_bytes=64)
+                gather_tab_words(0, HALF, HALF, second[:])
         sums = {}
         for c in range(2):
             closing = keep.tile([P, N], I32, name=f"gw_closing{c}", tag=f"late{c}", align_bytes=64)
@@ -214,18 +228,17 @@ def tile_list_tab48_res_kernel(tc, tab, w4_words, w4_scales, tab2, u, r, offs, o
 
         filler = keep.tile([P, N], I32, name="gw_last2", align_bytes=64)
         gather_tab_words(last, 2 * N, N, filler[:])
-        late = keep.tile([P, last, N], I32, name="gw_late2", tag="late0", align_bytes=64)
-        for a in range(last):
-            gather_tab_words(a, 2 * N, N, late[:, a, :])
+        late = keep.tile([P, N], I32, name="gw_late2", tag="late0", align_bytes=64)
+        gather_tab_words(1, 2 * N, N, late[:])
 
         def add_and_store_sums(c):
             nc.vector.tensor_tensor(sums[c][:], sums[c][:], r_t[c], ADD)
             nc.sync.dma_start(out[:, N * c : N * (c + 1)].rearrange("(m p) j -> p m j", p=P), sums[c][:])
 
         add_and_store_sums(0)
-        latest = keep.tile([P, TAB_PASSES, N], I32, name="gw_late3", tag="stage1", align_bytes=64)
-        for a in range(TAB_PASSES):
-            gather_tab_words(a, 3 * N, N, latest[:, a, :])
+        latest = keep.tile([P, 2, N], I32, name="gw_late3", tag="big2", align_bytes=64)
+        for a in (1, 2):
+            gather_tab_words(a, 3 * N, N, latest[:, a - 1, :])
         add_and_store_sums(1)
 
         for c in (2, 3):

@@ -25,7 +25,7 @@ def tile_list_tab48_res_kernel(tc, tab, w4_words, w4_scales, tab2, u, r, offs, o
     nc = tc.nc
     with ExitStack() as ctx:
         keep = ctx.enter_context(tc.tile_pool(name="keep", bufs=1))
-        ring = ctx.enter_context(tc.tile_pool(name="ring", bufs=4))
+        ring = ctx.enter_context(tc.tile_pool(name="ring", bufs=8))
         psum = ctx.enter_context(tc.psum_pool(name="psum", bufs=1))
 
         offs_t = keep.tile([P, S // 16], U16, name="offs_t")
@@ -164,10 +164,10 @@ def tile_list_tab48_res_kernel(tc, tab, w4_words, w4_scales, tab2, u, r, offs, o
             )
 
         tab2_picked = gather_scales(tab2_rows, offs2_t, "tab2_picked")
-        move_scales(tab2_picked, tab2_planes[0], U_PASSES, 0, nc.gpsimd)
+        move_scales(tab2_picked, tab2_planes[0], U_PASSES, 0, nc.sync)
         load_u(2, "big2")
         tab_picked = gather_scales(tab_rows, offs_t, "tab_picked")
-        move_scales(tab_picked, tab_planes[0], TAB_PASSES, 0, nc.gpsimd)
+        move_scales(tab_picked, tab_planes[0], TAB_PASSES, 0, nc.sync)
         load_w4_words()
 
         for c in range(2):
@@ -215,8 +215,8 @@ def tile_list_tab48_res_kernel(tc, tab, w4_words, w4_scales, tab2, u, r, offs, o
                 for m in range(4):
                     multiply_tab(a, c, m, False)
             if a == 0:
-                second = keep.tile([P, HALF], I32, name="gw0_second", align_bytes=64)
-                gather_tab_words(0, HALF, HALF, second[:])
+                third = keep.tile([P, N], I32, name="gw0_third", align_bytes=64)
+                gather_tab_words(0, 2 * N, N, third[:])
         sums = {}
         for c in range(2):
             closing = keep.tile([P, N], I32, name=f"gw_closing{c}", tag=f"late{c}", align_bytes=64)
@@ -236,10 +236,13 @@ def tile_list_tab48_res_kernel(tc, tab, w4_words, w4_scales, tab2, u, r, offs, o
             nc.sync.dma_start(out[:, N * c : N * (c + 1)].rearrange("(m p) j -> p m j", p=P), sums[c][:])
 
         add_and_store_sums(0)
-        latest = keep.tile([P, 2, N], I32, name="gw_late3", tag="big2", align_bytes=64)
-        for a in (1, 2):
-            gather_tab_words(a, 3 * N, N, latest[:, a - 1, :])
-        add_and_store_sums(1)
+        latest = keep.tile([P, TAB_PASSES, N], I32, name="gw_late3", tag="big2", align_bytes=64)
+        for a in range(TAB_PASSES):
+            gather_tab_words(a, 3 * N, N, latest[:, a, :])
+        totals = keep.tile([P, 4, N], F32, name="totals", tag="stage0", align_bytes=64)
+        for m in range(4):
+            nc.gpsimd.tensor_tensor(totals[:, m, :], sums[1][:, m, :], r_t[1][:, m, :], ADD)
+            nc.scalar.dma_start(out[P * m : P * (m + 1), N : 2 * N], totals[:, m, :])
 
         for c in (2, 3):
             for m in range(4):

@@ -25,26 +25,28 @@ def tile_list_tab48_res_kernel(tc, tab, w4_words, w4_scales, tab2, u, r, offs, o
     nc = tc.nc
     with ExitStack() as ctx:
         keep = ctx.enter_context(tc.tile_pool(name="keep", bufs=1))
-        ring = ctx.enter_context(tc.tile_pool(name="ring", bufs=8))
+        ring = ctx.enter_context(tc.tile_pool(name="ring", bufs=4))
         psum = ctx.enter_context(tc.psum_pool(name="psum", bufs=1))
 
         offs_t = keep.tile([P, S // 16], U16, name="offs_t")
         offs2_t = keep.tile([P, S // 16], U16, name="offs2_t")
         tab_rows = keep.tile([P, T // 4], I32, name="tab_rows", tag="small", align_bytes=64)
         tab2_rows = keep.tile([P, T // 4], I32, name="tab2_rows", tag="big2", align_bytes=64)
-        tab_planes = {0: keep.tile([P, TAB_PASSES, HALF // 4], I32, name="tab_planes0", align_bytes=64)}
-        tab2_planes = {0: keep.tile([P, U_PASSES, HALF // 4], I32, name="tab2_planes0", align_bytes=64)}
+        tab_ring = keep.tile([P, TAB_PASSES + 1, HALF // 4], I32, name="tab_ring", align_bytes=64)
+        tab2_ring = keep.tile([P, U_PASSES, HALF // 4], I32, name="tab2_ring", align_bytes=64)
+        tab_planes = {h: tab_ring[:, h : h + TAB_PASSES, :] for h in range(2)}
+        tab2_planes = {h: tab2_ring[:] for h in range(2)}
 
+        w4_s = keep.tile([P, TAB_PASSES, M // 4], I32, name="w4_s", align_bytes=64)
         nc.gpsimd.memset(tab_rows[:], 0)
+        nc.gpsimd.memset(tab2_ring[:], 0)
+        nc.gpsimd.memset(w4_s[:], 0)
         nc.vector.memset(tab2_rows[0:32, :], 0)
         nc.vector.memset(tab2_rows[96:128, :], 0)
-        w4_s = keep.tile([P, TAB_PASSES, M // 4], I32, name="w4_s", align_bytes=64)
-        nc.gpsimd.memset(w4_s[:], 0)
         for q in (0, 2, 1, 3):
             rows = w4_scales[:, 4 * q : 4 * q + 4, :].rearrange("a r b -> r a b").bitcast(I32)
             nc.gpsimd.dma_start(w4_s[32 * q : 32 * q + 4, :, :], rows)
-        nc.gpsimd.memset(tab2_planes[0][:], 0)
-        nc.gpsimd.memset(tab_planes[0][:], 0)
+        nc.gpsimd.memset(tab_ring[:], 0)
 
         nc.sync.dma_start(offs2_t[:], offs2)
         for b in range(U_PASSES):
@@ -77,11 +79,11 @@ def tile_list_tab48_res_kernel(tc, tab, w4_words, w4_scales, tab2, u, r, offs, o
             w4["words"] = keep.tile([P, TAB_PASSES, M // 2], I32, name="w4_w", tag="small", align_bytes=64)
             nc.sync.dma_start(w4["words"][:], w4_words.rearrange("a p b -> p a b").bitcast(I32))
 
-        def load_r(c, chunks, tag):
-            t = keep.tile([P, 4, N * chunks], F32, name=f"r{c}", tag=tag, align_bytes=64)
-            nc.sync.dma_start(t[:], r[:, N * c : N * (c + chunks)].rearrange("(m p) j -> p m j", p=P))
-            for i in range(chunks):
-                r_t[c + i] = t[:, :, N * i : N * (i + 1)]
+        def load_r(first, count, tag):
+            t = keep.tile([P, count, S], F32, name=f"r{first}", tag=tag, align_bytes=64)
+            for i in range(count):
+                r_t[first + i] = t[:, i, :]
+                nc.sync.dma_start(r_t[first + i], r[P * (first + i) : P * (first + i + 1), :])
 
         load_words(tab2_w, 0, tab2[0], "big0")
         load_u(0, "u_first")
@@ -118,7 +120,7 @@ def tile_list_tab48_res_kernel(tc, tab, w4_words, w4_scales, tab2, u, r, offs, o
             pairs[m, half] = t
 
         def part_tab2_words(m, half):
-            w = keep.tile([P, 2, 2 * HALF], U8, name=f"g2w{m}_{half}", align_bytes=64)
+            w = keep.tile([P, 2, 2 * HALF], U8, name=f"g2w{m}_{half}", tag=f"g2w{m}_{half}", align_bytes=64)
             nc.vector.tensor_copy(w[:].bitcast(U16), pairs[m, half][:].bitcast(U16).rearrange("p (n h) -> p h n", h=2))
             for h in range(2):
                 for c in range(2):
@@ -138,8 +140,8 @@ def tile_list_tab48_res_kernel(tc, tab, w4_words, w4_scales, tab2, u, r, offs, o
 
         acc = {}
 
-        def bank(c, m):
-            acc[c, m] = psum.tile([P, N], F32, name=f"bank{c % 2}{m}")
+        def bank(c, m, i):
+            acc[c, m] = psum.tile([P, N], F32, name=f"bank{i}")
 
         def multiply_tab(a, c, m, stop):
             nc.tensor.matmul_mx(
@@ -172,7 +174,7 @@ def tile_list_tab48_res_kernel(tc, tab, w4_words, w4_scales, tab2, u, r, offs, o
 
         for c in range(2):
             for m in range(4):
-                bank(c, m)
+                bank(c, m, 4 * c + m)
 
         def first_half_tab2(b):
             for c in range(2):
@@ -185,73 +187,95 @@ def tile_list_tab48_res_kernel(tc, tab, w4_words, w4_scales, tab2, u, r, offs, o
         first_half_tab2(0)
         quantise_u(1, "stage2")
         first_half_tab2(1)
-        load_words(tab_w, 0, tab[0], "u_first")
+        first, second, last = 1, 2, 0
+        load_words(tab_w, first, tab[first], "u_first")
         gather_tab2_words(0, 1, "stage2")
-        load_words(tab_w, 1, tab[1], "big0")
+        load_words(tab_w, second, tab[second], "big0")
         gather_tab2_words(1, 0, "stage0")
         part_tab2_words(0, 1)
         part_tab2_words(1, 0)
-        load_words(tab_w, 2, tab[2], "stage0")
-        late_planes = keep.tile([P, U_PASSES + TAB_PASSES, HALF // 4], I32, name="late_planes", tag="stage2", align_bytes=64)
-        nc.gpsimd.memset(late_planes[:], 0)
-        tab2_planes[1] = late_planes[:, 0:U_PASSES, :]
-        tab_planes[1] = late_planes[:, U_PASSES:, :]
-        move_scales(tab2_picked, tab2_planes[1], U_PASSES, 1, nc.sync)
-        move_scales(tab_picked, tab_planes[1], TAB_PASSES, 1, nc.sync)
+        load_words(tab_w, last, tab[last], "stage0")
         quantise_u(2, "stage1")
         first_half_tab2(2)
         quantise_u(3, "stage3")
         first_half_tab2(3)
-        load_r(0, 1, "big2")
+        move_scales(tab2_picked, tab2_planes[1], U_PASSES, 1, nc.sync)
+        load_r(0, 2, "g2w1_0")
         gather_tab2_words(1, 1, "stage3")
-        load_r(1, 1, "big1")
         part_tab2_words(1, 1)
-        load_r(2, 2, "stage3")
-        last = TAB_PASSES - 1
-        for a in range(last):
+        for a in (first, second):
             for c in range(2):
-                first = keep.tile([P, N], I32, name=f"gw{a}_first{c}", align_bytes=64)
-                gather_tab_words(a, N * c, N, first[:])
+                early = keep.tile([P, N], I32, name=f"gw{a}_{c}", tag=f"gw{a}_{c}", align_bytes=64)
+                gather_tab_words(a, N * c, N, early[:])
                 for m in range(4):
                     multiply_tab(a, c, m, False)
-            if a == 0:
-                third = keep.tile([P, N], I32, name="gw0_third", align_bytes=64)
-                gather_tab_words(0, 2 * N, N, third[:])
+            if a == first:
+                third = keep.tile([P, N], I32, name="gw_third", align_bytes=64)
+                gather_tab_words(first, 2 * N, N, third[:])
+        move_scales(tab_picked, tab_planes[1], TAB_PASSES, 1, nc.sync)
+        load_r(2, 2, f"gw{second}_1")
+
         sums = {}
+        for pair in range(2):
+            both = keep.tile([P, 2, N], F32, name=f"sums{pair}", tag=f"sums{pair}", align_bytes=64)
+            sums[2 * pair] = both[:, 0, :]
+            sums[2 * pair + 1] = both[:, 1, :]
         for c in range(2):
-            closing = keep.tile([P, N], I32, name=f"gw_closing{c}", tag=f"late{c}", align_bytes=64)
+            closing = keep.tile([P, N], I32, name=f"gw_closing{c}", tag=f"closing{c}", align_bytes=64)
             gather_tab_words(last, N * c, N, closing[:])
-            sums[c] = keep.tile([P, 4, N], F32, name=f"sums{c}")
             for m in range(4):
                 multiply_tab(last, c, m, True)
-                nc.scalar.copy(sums[c][:, m, :], acc[c, m][:])
-
-        filler = keep.tile([P, N], I32, name="gw_last2", align_bytes=64)
-        gather_tab_words(last, 2 * N, N, filler[:])
-        late = keep.tile([P, N], I32, name="gw_late2", tag="late0", align_bytes=64)
-        gather_tab_words(1, 2 * N, N, late[:])
-
-        def add_and_store_sums(c):
-            nc.vector.tensor_tensor(sums[c][:], sums[c][:], r_t[c], ADD)
-            nc.sync.dma_start(out[:, N * c : N * (c + 1)].rearrange("(m p) j -> p m j", p=P), sums[c][:])
-
-        add_and_store_sums(0)
-        latest = keep.tile([P, TAB_PASSES, N], I32, name="gw_late3", tag="big2", align_bytes=64)
-        for a in range(TAB_PASSES):
-            gather_tab_words(a, 3 * N, N, latest[:, a, :])
-        totals = keep.tile([P, 4, N], F32, name="totals", tag="stage0", align_bytes=64)
-        for m in range(4):
-            nc.gpsimd.tensor_tensor(totals[:, m, :], sums[1][:, m, :], r_t[1][:, m, :], ADD)
-            nc.scalar.dma_start(out[P * m : P * (m + 1), N : 2 * N], totals[:, m, :])
+                if c == 0:
+                    nc.scalar.copy(sums[m], acc[c, m][:])
 
         for c in (2, 3):
-            for m in range(4):
-                bank(c, m)
-                for b in range(U_PASSES):
-                    multiply_tab2(b, c, m)
-            for m in range(4):
-                for a in range(TAB_PASSES):
-                    multiply_tab(a, c, m, a == last)
-                o = ring.tile([P, N], F32, name="o")
-                nc.vector.tensor_tensor(o[:], acc[c, m][:], r_t[c][:, m, :], ADD)
-                nc.sync.dma_start(out[P * m : P * (m + 1), N * c : N * (c + 1)], o[:])
+            rest = keep.tile([P, N], I32, name=f"gw_last{c}", align_bytes=64)
+            gather_tab_words(last, N * c, N, rest[:])
+        for m in range(2):
+            nc.vector.tensor_tensor(r_t[m][:, N:HALF], acc[1, m][:], r_t[m][:, N:HALF], ADD)
+            nc.vector.tensor_tensor(r_t[m][:, 0:N], sums[m], r_t[m][:, 0:N], ADD)
+            nc.sync.dma_start(out[P * m : P * (m + 1), 0:HALF], r_t[m][:, 0:HALF])
+        late = keep.tile([P, 3, N], I32, name="gw_late", tag="sums0", align_bytes=64)
+        for i, (a, c) in enumerate(((first, 3), (second, 2), (second, 3))):
+            gather_tab_words(a, N * c, N, late[:, i, :])
+
+        early_totals = keep.tile([P, 2, HALF], F32, name="early_totals", tag="big0", align_bytes=64)
+        for m in (2, 3):
+            nc.gpsimd.tensor_tensor(early_totals[:, m - 2, 0:N], sums[m], r_t[m][:, 0:N], ADD)
+            nc.vector.tensor_tensor(early_totals[:, m - 2, N:HALF], acc[1, m][:], r_t[m][:, N:HALF], ADD)
+            nc.sync.dma_start(out[P * m : P * (m + 1), 0:HALF], early_totals[:, m - 2, :])
+
+        totals = {}
+
+        def add(c, m):
+            if c == 2:
+                totals[m] = ring.tile([P, HALF], F32, name="total")
+            lo = N * (c - 2)
+            nc.vector.tensor_tensor(totals[m][:, lo : lo + N], acc[c, m][:], r_t[m][:, N * c : N * (c + 1)], ADD)
+
+        def store(m, lo, n):
+            nc.sync.dma_start(out[P * m : P * (m + 1), HALF + lo : HALF + lo + n], totals[m][:, lo : lo + n])
+
+        groups = [(c, m) for m in range(4) for c in (2, 3)]
+        for i, (c, m) in enumerate(groups[:4]):
+            bank(c, m, i)
+            for b in range(U_PASSES):
+                multiply_tab2(b, c, m)
+        for a in (last, first, second):
+            for c, m in groups[:4]:
+                multiply_tab(a, c, m, a == second)
+        for c, m in groups[:4]:
+            add(c, m)
+            if c == 3:
+                store(m, 0, HALF)
+        for i, (c, m) in enumerate(groups[4:]):
+            bank(c, m, 4 + i)
+            for b in range(U_PASSES):
+                multiply_tab2(b, c, m)
+            for a in (last, first, second):
+                multiply_tab(a, c, m, a == second)
+            add(c, m)
+            if m == 3:
+                store(m, N * (c - 2), N)
+            elif c == 3:
+                store(m, 0, HALF)

@@ -32,31 +32,24 @@ def tile_list_tab48_res_kernel(tc, tab, w4_words, w4_scales, tab2, u, r, offs, o
         offs2_t = keep.tile([P, S // 16], U16, name="offs2_t")
         tab_rows = keep.tile([P, T // 4], I32, name="tab_rows", tag="small", align_bytes=64)
         tab2_rows = keep.tile([P, T // 4], I32, name="tab2_rows", tag="big2", align_bytes=64)
-        tab_ring = keep.tile([P, TAB_PASSES + 1, HALF // 4], I32, name="tab_ring", align_bytes=64)
-        tab2_ring = keep.tile([P, U_PASSES, HALF // 4], I32, name="tab2_ring", align_bytes=64)
-        tab_planes = {h: tab_ring[:, h : h + TAB_PASSES, :] for h in range(2)}
-        tab2_planes = {h: tab2_ring[:] for h in range(2)}
+        tab_ring = keep.tile([P, TAB_PASSES, HALF // 4], I32, name="tab_ring", align_bytes=64)
+        tab_planes = {0: tab_ring}
+        tab2_planes = [keep.tile([P, 2, HALF // 4], I32, name=f"tab2_planes{h}", align_bytes=64) for h in range(2)]
 
         w4_s = keep.tile([P, TAB_PASSES, M // 4], I32, name="w4_s", align_bytes=64)
         nc.gpsimd.memset(tab_rows[:], 0)
-        nc.gpsimd.memset(tab2_ring[:], 0)
-        nc.gpsimd.memset(w4_s[:], 0)
         nc.vector.memset(tab2_rows[0:32, :], 0)
         nc.vector.memset(tab2_rows[96:128, :], 0)
         for q in (0, 2, 1, 3):
             rows = w4_scales[:, 4 * q : 4 * q + 4, :].rearrange("a r b -> r a b").bitcast(I32)
             nc.gpsimd.dma_start(w4_s[32 * q : 32 * q + 4, :, :], rows)
-        nc.gpsimd.memset(tab_ring[:], 0)
 
         nc.sync.dma_start(offs2_t[:], offs2)
-        for b in range(U_PASSES):
-            m, h = divmod(b, 2)
-            rows = tab2[m, (512 + 16 * h) * T : (528 + 16 * h) * T].rearrange("(q c) -> q c", q=16).bitcast(I32)
-            nc.sync.dma_start(tab2_rows[32 + b : 96 : 4, :], rows)
+        for j in (0, 2, 1, 3):
+            rows = tab2[:, 512 * T : 544 * T].rearrange("m (g j c) -> j g m c", j=4, c=T)[j].bitcast(I32)
+            lo = 32 + 32 * (j // 2) + j % 2
+            nc.sync.dma_start(tab2_rows[lo : lo + 31 : 2, :], rows)
         nc.sync.dma_start(offs_t[:], offs)
-        nc.scalar.dma_start(
-            tab_rows[32:80, :], tab[:, 512 * T : 528 * T].rearrange("a (q c) -> q a c", q=16).bitcast(I32)
-        )
 
         tab_w = {}
         tab2_w = {}
@@ -68,9 +61,11 @@ def tile_list_tab48_res_kernel(tc, tab, w4_words, w4_scales, tab2, u, r, offs, o
             into[key] = keep.tile([P, T], I32, name=f"words_{tag}", tag=tag, align_bytes=64)
             nc.sync.dma_start(into[key][:], src[0 : 512 * T].rearrange("(p b) -> p b", p=P).bitcast(I32))
 
-        def load_u(b, tag):
+        def load_u(b, tag, with_moves):
             both = keep.tile([P, 2, 4, M], F32, name=f"u_raw{b}", tag=tag, align_bytes=64)
             for i in range(2):
+                if with_moves:
+                    move_tab2_scales(0, i)
                 u_raw[b + i] = both[:, i, :, :]
                 rows = u[512 * (b + i) : 512 * (b + i + 1), :]
                 nc.sync.dma_start(u_raw[b + i], rows.rearrange("(p j) n -> p j n", j=4))
@@ -82,11 +77,16 @@ def tile_list_tab48_res_kernel(tc, tab, w4_words, w4_scales, tab2, u, r, offs, o
         def load_r(first, count, tag):
             t = keep.tile([P, count, S], F32, name=f"r{first}", tag=tag, align_bytes=64)
             for i in range(count):
+                if first == 0:
+                    move_tab2_scales(1, i)
                 r_t[first + i] = t[:, i, :]
                 nc.sync.dma_start(r_t[first + i], r[P * (first + i) : P * (first + i + 1), :])
 
         load_words(tab2_w, 0, tab2[0], "big0")
-        load_u(0, "u_first")
+        for a in range(TAB_PASSES):
+            rows = tab[a, 512 * T : 528 * T].rearrange("(q c) -> q c", q=16).bitcast(I32)
+            nc.sync.dma_start(tab_rows[32 + 4 * a : 32 + 4 * a + 46 : 3, :], rows)
+        load_u(0, "u_first", False)
         load_words(tab2_w, 1, tab2[1], "big1")
 
         def cols(lo, n):
@@ -97,11 +97,17 @@ def tile_list_tab48_res_kernel(tc, tab, w4_words, w4_scales, tab2, u, r, offs, o
             nc.vector.tensor_copy(picked[:].bitcast(U8), rows[:].bitcast(U8).indirect(lists[:]))
             return picked
 
-        def move_scales(picked, planes, passes, half, queue):
-            for q in (0, 2, 1, 3):
-                lo = 32 + 4 * passes * q
-                words = slice(half * HALF // 4, (half + 1) * HALF // 4)
-                queue.dma_start(planes[32 * q : 32 * q + 4, :, :], picked[lo : lo + 4 * passes, words])
+        def move_tab2_scales(half, h):
+            words = slice(half * HALF // 4, (half + 1) * HALF // 4)
+            for j in range(4):
+                lo = 32 + 32 * (j // 2) + j % 2 + 16 * h
+                nc.sync.dma_start(tab2_planes[h][j:P:32, :, :], tab2_picked[lo : lo + 15 : 2, words])
+
+        def move_tab_scales(half):
+            words = slice(half * HALF // 4, (half + 1) * HALF // 4)
+            for j in range(4):
+                lo = 32 + 3 * j
+                nc.sync.dma_start(tab_planes[half][j:P:32, :, :], tab_picked[lo : lo + 45 : 4, words])
 
         gw = {}
         g2w = {}
@@ -160,17 +166,13 @@ def tile_list_tab48_res_kernel(tc, tab, w4_words, w4_scales, tab2, u, r, offs, o
                 lhsT=u_codes[b][:, P * m : P * (m + 1)].bitcast(FP8X4),
                 lhsT_scale=u_scales[b][:, P * m : P * (m + 1)],
                 rhs=g2w[b, c],
-                rhs_scale=tab2_planes[c // 2][:, b, 128 * (c % 2) : 128 * (c % 2 + 1)].bitcast(U8),
+                rhs_scale=tab2_planes[b % 2][:, b // 2, 128 * (c % 2) : 128 * (c % 2 + 1)].bitcast(U8),
                 start=b == 0,
                 stop=False,
             )
 
         tab2_picked = gather_scales(tab2_rows, offs2_t, "tab2_picked")
-        move_scales(tab2_picked, tab2_planes[0], U_PASSES, 0, nc.sync)
-        load_u(2, "big2")
-        tab_picked = gather_scales(tab_rows, offs_t, "tab_picked")
-        move_scales(tab_picked, tab_planes[0], TAB_PASSES, 0, nc.sync)
-        load_w4_words()
+        load_u(2, "big2", True)
 
         for c in range(2):
             for m in range(4):
@@ -182,6 +184,9 @@ def tile_list_tab48_res_kernel(tc, tab, w4_words, w4_scales, tab2, u, r, offs, o
                     multiply_tab2(b, c, m)
 
         gather_tab2_words(0, 0, "stage0")
+        tab_picked = gather_scales(tab_rows, offs_t, "tab_picked")
+        move_tab_scales(0)
+        load_w4_words()
         part_tab2_words(0, 0)
         quantise_u(0, "stage1")
         first_half_tab2(0)
@@ -199,21 +204,21 @@ def tile_list_tab48_res_kernel(tc, tab, w4_words, w4_scales, tab2, u, r, offs, o
         first_half_tab2(2)
         quantise_u(3, "stage3")
         first_half_tab2(3)
-        move_scales(tab2_picked, tab2_planes[1], U_PASSES, 1, nc.sync)
         load_r(0, 2, "g2w1_0")
         gather_tab2_words(1, 1, "stage3")
         part_tab2_words(1, 1)
         for a in (first, second):
             for c in range(2):
-                early = keep.tile([P, N], I32, name=f"gw{a}_{c}", tag=f"gw{a}_{c}", align_bytes=64)
+                early = keep.tile([P, N], I32, name=f"gw{a}_{c}", tag=f"gw{a}_0" + "b" * c, align_bytes=64)
                 gather_tab_words(a, N * c, N, early[:])
                 for m in range(4):
                     multiply_tab(a, c, m, False)
             if a == first:
                 third = keep.tile([P, N], I32, name="gw_third", align_bytes=64)
                 gather_tab_words(first, 2 * N, N, third[:])
-        move_scales(tab_picked, tab_planes[1], TAB_PASSES, 1, nc.sync)
-        load_r(2, 2, f"gw{second}_1")
+        tab_planes[1] = keep.tile([P, TAB_PASSES, HALF // 4], I32, name="tab_late", tag=f"gw{second}_0", align_bytes=64)
+        move_tab_scales(1)
+        load_r(2, 2, f"gw{second}_0b")
 
         sums = {}
         for pair in range(2):
@@ -259,7 +264,10 @@ def tile_list_tab48_res_kernel(tc, tab, w4_words, w4_scales, tab2, u, r, offs, o
         groups = [(c, m) for m in range(4) for c in (2, 3)]
         for i, (c, m) in enumerate(groups[:4]):
             bank(c, m, i)
-            for b in range(U_PASSES):
+            for b in (0, 2):
+                multiply_tab2(b, c, m)
+        for c, m in groups[:4]:
+            for b in (1, 3):
                 multiply_tab2(b, c, m)
         for a in (last, first, second):
             for c, m in groups[:4]:

@@ -25,7 +25,7 @@ def tile_list_tab48_res_kernel(tc, tab, w4_words, w4_scales, tab2, u, r, offs, o
     nc = tc.nc
     with ExitStack() as ctx:
         keep = ctx.enter_context(tc.tile_pool(name="keep", bufs=1))
-        ring = ctx.enter_context(tc.tile_pool(name="ring", bufs=4))
+        shared = ctx.enter_context(tc.tile_pool(name="shared", bufs=1))
         psum = ctx.enter_context(tc.psum_pool(name="psum", bufs=1))
 
         offs_t = keep.tile([P, S // 16], U16, name="offs_t")
@@ -40,9 +40,9 @@ def tile_list_tab48_res_kernel(tc, tab, w4_words, w4_scales, tab2, u, r, offs, o
         nc.gpsimd.memset(tab_rows[:], 0)
         nc.vector.memset(tab2_rows[0:32, :], 0)
         nc.vector.memset(tab2_rows[96:128, :], 0)
-        for q in (0, 2, 1, 3):
-            rows = w4_scales[:, 4 * q : 4 * q + 4, :].rearrange("a r b -> r a b").bitcast(I32)
-            nc.gpsimd.dma_start(w4_s[32 * q : 32 * q + 4, :, :], rows)
+        for j in range(4):
+            rows = w4_scales[:, j:16:4, :].rearrange("a q b -> q a b").bitcast(I32)
+            nc.gpsimd.dma_start(w4_s[j:P:32, :, :], rows)
 
         nc.sync.dma_start(offs2_t[:], offs2)
         for j in (0, 2, 1, 3):
@@ -74,13 +74,8 @@ def tile_list_tab48_res_kernel(tc, tab, w4_words, w4_scales, tab2, u, r, offs, o
             w4["words"] = keep.tile([P, TAB_PASSES, M // 2], I32, name="w4_w", tag="small", align_bytes=64)
             nc.sync.dma_start(w4["words"][:], w4_words.rearrange("a p b -> p a b").bitcast(I32))
 
-        def load_r(first, count, tag):
-            t = keep.tile([P, count, S], F32, name=f"r{first}", tag=tag, align_bytes=64)
-            for i in range(count):
-                if first == 0:
-                    move_tab2_scales(1, i)
-                r_t[first + i] = t[:, i, :]
-                nc.sync.dma_start(r_t[first + i], r[P * (first + i) : P * (first + i + 1), :])
+        def load_r(m):
+            nc.sync.dma_start(r_t[m], r[P * m : P * (m + 1), :])
 
         load_words(tab2_w, 0, tab2[0], "big0")
         for a in range(TAB_PASSES):
@@ -126,7 +121,10 @@ def tile_list_tab48_res_kernel(tc, tab, w4_words, w4_scales, tab2, u, r, offs, o
             pairs[m, half] = t
 
         def part_tab2_words(m, half):
-            w = keep.tile([P, 2, 2 * HALF], U8, name=f"g2w{m}_{half}", tag=f"g2w{m}_{half}", align_bytes=64)
+            if (m, half) == (1, 0):
+                w = shared.tile([P, 2, 2 * HALF], U8, name="g2w1_0", offset=HALF, align_bytes=64)
+            else:
+                w = keep.tile([P, 2, 2 * HALF], U8, name=f"g2w{m}_{half}", align_bytes=64)
             nc.vector.tensor_copy(w[:].bitcast(U16), pairs[m, half][:].bitcast(U16).rearrange("p (n h) -> p h n", h=2))
             for h in range(2):
                 for c in range(2):
@@ -149,7 +147,7 @@ def tile_list_tab48_res_kernel(tc, tab, w4_words, w4_scales, tab2, u, r, offs, o
         def bank(c, m, i):
             acc[c, m] = psum.tile([P, N], F32, name=f"bank{i}")
 
-        def multiply_tab(a, c, m, stop):
+        def multiply_tab(a, c, m, stop=False):
             nc.tensor.matmul_mx(
                 out=acc[c, m][:],
                 lhsT=w4["words"][:, a, 64 * m : 64 * (m + 1)].bitcast(FP4X4),
@@ -160,15 +158,15 @@ def tile_list_tab48_res_kernel(tc, tab, w4_words, w4_scales, tab2, u, r, offs, o
                 stop=stop,
             )
 
-        def multiply_tab2(b, c, m):
+        def multiply_tab2(b, c, m, start=False, stop=False):
             nc.tensor.matmul_mx(
                 out=acc[c, m][:],
                 lhsT=u_codes[b][:, P * m : P * (m + 1)].bitcast(FP8X4),
                 lhsT_scale=u_scales[b][:, P * m : P * (m + 1)],
                 rhs=g2w[b, c],
                 rhs_scale=tab2_planes[b % 2][:, b // 2, 128 * (c % 2) : 128 * (c % 2 + 1)].bitcast(U8),
-                start=b == 0,
-                stop=False,
+                start=start,
+                stop=stop,
             )
 
         tab2_picked = gather_scales(tab2_rows, offs2_t, "tab2_picked")
@@ -181,7 +179,7 @@ def tile_list_tab48_res_kernel(tc, tab, w4_words, w4_scales, tab2, u, r, offs, o
         def first_half_tab2(b):
             for c in range(2):
                 for m in range(4):
-                    multiply_tab2(b, c, m)
+                    multiply_tab2(b, c, m, start=b == 0)
 
         gather_tab2_words(0, 0, "stage0")
         tab_picked = gather_scales(tab_rows, offs_t, "tab_picked")
@@ -190,100 +188,90 @@ def tile_list_tab48_res_kernel(tc, tab, w4_words, w4_scales, tab2, u, r, offs, o
         part_tab2_words(0, 0)
         quantise_u(0, "stage1")
         first_half_tab2(0)
+        gather_tab2_words(0, 1, "stage1")
         quantise_u(1, "stage2")
         first_half_tab2(1)
         first, second, last = 1, 2, 0
         load_words(tab_w, first, tab[first], "u_first")
-        gather_tab2_words(0, 1, "stage2")
         load_words(tab_w, second, tab[second], "big0")
         gather_tab2_words(1, 0, "stage0")
         part_tab2_words(0, 1)
         part_tab2_words(1, 0)
         load_words(tab_w, last, tab[last], "stage0")
-        quantise_u(2, "stage1")
+        quantise_u(2, "stage2")
         first_half_tab2(2)
+        gather_tab2_words(1, 1, "stage2")
         quantise_u(3, "stage3")
         first_half_tab2(3)
-        load_r(0, 2, "g2w1_0")
-        gather_tab2_words(1, 1, "stage3")
+        tab_planes[1] = shared.tile([P, TAB_PASSES, HALF // 4], I32, name="tab_late", offset=0, align_bytes=64)
+        r_all = shared.tile([P, 4, S], F32, name="r_all", offset=TAB_PASSES * HALF, align_bytes=64)
+        for m in range(4):
+            r_t[m] = r_all[:, m, :]
+        move_tab2_scales(1, 0)
+        load_r(0)
+        move_tab_scales(1)
+        load_r(1)
+        move_tab2_scales(1, 1)
+        load_r(2)
+        load_r(3)
         part_tab2_words(1, 1)
+        more = keep.tile([P, HALF], I32, name="gw_more", align_bytes=64)
+        gather_tab_words(first, HALF, HALF, more[:])
         for a in (first, second):
             for c in range(2):
-                early = keep.tile([P, N], I32, name=f"gw{a}_{c}", tag=f"gw{a}_0" + "b" * c, align_bytes=64)
+                early = keep.tile([P, N], I32, name=f"gw{a}_{c}", align_bytes=64)
                 gather_tab_words(a, N * c, N, early[:])
                 for m in range(4):
                     multiply_tab(a, c, m, False)
-            if a == first:
-                third = keep.tile([P, N], I32, name="gw_third", align_bytes=64)
-                gather_tab_words(first, 2 * N, N, third[:])
-        tab_planes[1] = keep.tile([P, TAB_PASSES, HALF // 4], I32, name="tab_late", tag=f"gw{second}_0", align_bytes=64)
-        move_tab_scales(1)
-        load_r(2, 2, f"gw{second}_0b")
 
-        sums = {}
-        for pair in range(2):
-            both = keep.tile([P, 2, N], F32, name=f"sums{pair}", tag=f"sums{pair}", align_bytes=64)
-            sums[2 * pair] = both[:, 0, :]
-            sums[2 * pair + 1] = both[:, 1, :]
+        sums = keep.tile([P, 4, N], F32, name="sums")
         for c in range(2):
             closing = keep.tile([P, N], I32, name=f"gw_closing{c}", tag=f"closing{c}", align_bytes=64)
             gather_tab_words(last, N * c, N, closing[:])
             for m in range(4):
                 multiply_tab(last, c, m, True)
                 if c == 0:
-                    nc.scalar.copy(sums[m], acc[c, m][:])
+                    nc.scalar.copy(sums[:, m, :], acc[c, m][:])
 
-        for c in (2, 3):
-            rest = keep.tile([P, N], I32, name=f"gw_last{c}", align_bytes=64)
-            gather_tab_words(last, N * c, N, rest[:])
-        for m in range(2):
-            nc.vector.tensor_tensor(r_t[m][:, N:HALF], acc[1, m][:], r_t[m][:, N:HALF], ADD)
-            nc.vector.tensor_tensor(r_t[m][:, 0:N], sums[m], r_t[m][:, 0:N], ADD)
-            nc.sync.dma_start(out[P * m : P * (m + 1), 0:HALF], r_t[m][:, 0:HALF])
-        late = keep.tile([P, 3, N], I32, name="gw_late", tag="sums0", align_bytes=64)
-        for i, (a, c) in enumerate(((first, 3), (second, 2), (second, 3))):
-            gather_tab_words(a, N * c, N, late[:, i, :])
+        rest = keep.tile([P, HALF], I32, name="gw_rest", align_bytes=64)
+        gather_tab_words(last, HALF, HALF, rest[:])
+        late = keep.tile([P, HALF], I32, name="gw_late", tag="closing0", align_bytes=64)
+        gather_tab_words(second, HALF, HALF, late[:])
 
-        early_totals = keep.tile([P, 2, HALF], F32, name="early_totals", tag="big0", align_bytes=64)
-        for m in (2, 3):
-            nc.gpsimd.tensor_tensor(early_totals[:, m - 2, 0:N], sums[m], r_t[m][:, 0:N], ADD)
-            nc.vector.tensor_tensor(early_totals[:, m - 2, N:HALF], acc[1, m][:], r_t[m][:, N:HALF], ADD)
-            nc.sync.dma_start(out[P * m : P * (m + 1), 0:HALF], early_totals[:, m - 2, :])
-
-        totals = {}
-
-        def add(c, m):
-            if c == 2:
-                totals[m] = ring.tile([P, HALF], F32, name="total")
-            lo = N * (c - 2)
-            nc.vector.tensor_tensor(totals[m][:, lo : lo + N], acc[c, m][:], r_t[m][:, N * c : N * (c + 1)], ADD)
+        def add(c, m, y):
+            cols_c = r_t[m][:, N * c : N * (c + 1)]
+            nc.vector.tensor_tensor(cols_c, y, cols_c, ADD)
 
         def store(m, lo, n):
-            nc.sync.dma_start(out[P * m : P * (m + 1), HALF + lo : HALF + lo + n], totals[m][:, lo : lo + n])
+            nc.sync.dma_start(out[P * m : P * (m + 1), lo : lo + n], r_t[m][:, lo : lo + n])
+
+        for m in range(4):
+            add(1, m, acc[1, m][:])
+            add(0, m, sums[:, m, :])
+            store(m, 0, HALF)
 
         groups = [(c, m) for m in range(4) for c in (2, 3)]
         for i, (c, m) in enumerate(groups[:4]):
             bank(c, m, i)
-            for b in (0, 2):
-                multiply_tab2(b, c, m)
-        for c, m in groups[:4]:
-            for b in (1, 3):
-                multiply_tab2(b, c, m)
+            multiply_tab2(0, c, m, start=True)
+            multiply_tab2(2, c, m)
         for a in (last, first, second):
             for c, m in groups[:4]:
-                multiply_tab(a, c, m, a == second)
+                multiply_tab(a, c, m)
         for c, m in groups[:4]:
-            add(c, m)
+            multiply_tab2(1, c, m)
+            multiply_tab2(3, c, m, stop=True)
+            add(c, m, acc[c, m][:])
             if c == 3:
-                store(m, 0, HALF)
+                store(m, HALF, HALF)
         for i, (c, m) in enumerate(groups[4:]):
             bank(c, m, 4 + i)
-            for b in range(U_PASSES):
-                multiply_tab2(b, c, m)
+            for b in (1, 3, 0, 2):
+                multiply_tab2(b, c, m, start=b == 1)
             for a in (last, first, second):
                 multiply_tab(a, c, m, a == second)
-            add(c, m)
+            add(c, m, acc[c, m][:])
             if m == 3:
-                store(m, N * (c - 2), N)
+                store(m, N * c, N)
             elif c == 3:
-                store(m, 0, HALF)
+                store(m, HALF, HALF)

@@ -30,10 +30,9 @@ def tile_list_tab48_res_kernel(tc, tab, w4_words, w4_scales, tab2, u, r, offs, o
 
         offs_t = keep.tile([P, S // 16], U16, name="offs_t")
         offs2_t = keep.tile([P, S // 16], U16, name="offs2_t")
-        tab_rows = keep.tile([P, T // 4], I32, name="tab_rows", tag="small", align_bytes=64)
-        tab2_rows = keep.tile([P, T // 4], I32, name="tab2_rows", tag="big2", align_bytes=64)
-        tab_ring = keep.tile([P, TAB_PASSES, HALF // 4], I32, name="tab_ring", align_bytes=64)
-        tab_planes = {0: tab_ring}
+        tab_rows = keep.tile([P, T // 4], I32, name="tab_rows", tag="rows_then_w4", align_bytes=64)
+        tab2_rows = keep.tile([P, T // 4], I32, name="tab2_rows", tag="rows_then_u3", align_bytes=64)
+        tab_planes = {}
         tab2_planes = [keep.tile([P, 2, HALF // 4], I32, name=f"tab2_planes{h}", align_bytes=64) for h in range(2)]
 
         w4_s = keep.tile([P, TAB_PASSES, M // 4], I32, name="w4_s", align_bytes=64)
@@ -54,35 +53,24 @@ def tile_list_tab48_res_kernel(tc, tab, w4_words, w4_scales, tab2, u, r, offs, o
         tab_w = {}
         tab2_w = {}
         u_raw = {}
-        r_t = {}
         w4 = {}
 
         def load_words(into, key, src, tag):
             into[key] = keep.tile([P, T], I32, name=f"words_{tag}", tag=tag, align_bytes=64)
             nc.sync.dma_start(into[key][:], src[0 : 512 * T].rearrange("(p b) -> p b", p=P).bitcast(I32))
 
-        def load_u(b, tag, with_moves):
-            both = keep.tile([P, 2, 4, M], F32, name=f"u_raw{b}", tag=tag, align_bytes=64)
-            for i in range(2):
-                if with_moves:
-                    move_tab2_scales(0, i)
-                u_raw[b + i] = both[:, i, :, :]
-                rows = u[512 * (b + i) : 512 * (b + i + 1), :]
-                nc.sync.dma_start(u_raw[b + i], rows.rearrange("(p j) n -> p j n", j=4))
+        def load_u(b, tag):
+            u_raw[b] = keep.tile([P, 4, M], F32, name=f"u_raw{b}", tag=tag, align_bytes=64)
+            nc.sync.dma_start(u_raw[b][:], u[512 * b : 512 * (b + 1), :].rearrange("(p j) n -> p j n", j=4))
 
-        def load_w4_words():
-            w4["words"] = keep.tile([P, TAB_PASSES, M // 2], I32, name="w4_w", tag="small", align_bytes=64)
-            nc.sync.dma_start(w4["words"][:], w4_words.rearrange("a p b -> p a b").bitcast(I32))
-
-        def load_r(m):
-            nc.sync.dma_start(r_t[m], r[P * m : P * (m + 1), :])
-
-        load_words(tab2_w, 0, tab2[0], "big0")
+        load_words(tab2_w, 0, tab2[0], "tab2_w0")
         for a in range(TAB_PASSES):
             rows = tab[a, 512 * T : 528 * T].rearrange("(q c) -> q c", q=16).bitcast(I32)
             nc.sync.dma_start(tab_rows[32 + 4 * a : 32 + 4 * a + 46 : 3, :], rows)
-        load_u(0, "u_first", False)
-        load_words(tab2_w, 1, tab2[1], "big1")
+        load_u(0, "u0_then_first")
+        load_u(1, "u1_then_planes")
+        load_words(tab2_w, 1, tab2[1], "tab2_w1")
+        load_u(2, "u2")
 
         def cols(lo, n):
             return slice(lo // 16, (lo + n) // 16)
@@ -113,29 +101,25 @@ def tile_list_tab48_res_kernel(tc, tab, w4_words, w4_scales, tab2, u, r, offs, o
             for c in range(lo, lo + n, N):
                 gw[a, c // N] = t[:, c - lo : c - lo + N].bitcast(FP8X4)
 
-        def gather_tab2_words(m, half, tag):
-            t = keep.tile([P, HALF], I32, name=f"pairs{m}{half}", tag=tag, align_bytes=64)
-            nc.vector.tensor_copy(
-                t[:].bitcast(U32), tab2_w[m][:].bitcast(U32).indirect(offs2_t[:, cols(HALF * half, HALF)])
-            )
-            pairs[m, half] = t
+        def gather_tab2_words(m, lo, n, t):
+            nc.vector.tensor_copy(t.bitcast(U32), tab2_w[m][:].bitcast(U32).indirect(offs2_t[:, cols(lo, n)]))
+            pairs[m, lo] = t
 
-        def part_tab2_words(m, half):
-            if (m, half) == (1, 0):
-                w = shared.tile([P, 2, 2 * HALF], U8, name="g2w1_0", offset=HALF, align_bytes=64)
-            else:
-                w = keep.tile([P, 2, 2 * HALF], U8, name=f"g2w{m}_{half}", align_bytes=64)
-            nc.vector.tensor_copy(w[:].bitcast(U16), pairs[m, half][:].bitcast(U16).rearrange("p (n h) -> p h n", h=2))
+        def part_tab2_words(m, lo, n, src, w):
+            nc.vector.tensor_copy(w[:].bitcast(U16), src.bitcast(U16).rearrange("p (n h) -> p h n", h=2))
             for h in range(2):
-                for c in range(2):
-                    g2w[2 * m + h, 2 * half + c] = w[:, h, 2 * N * c : 2 * N * (c + 1)].bitcast(FP4X4)
+                for c in range(n // N):
+                    g2w[2 * m + h, lo // N + c] = w[:, h, 2 * N * c : 2 * N * (c + 1)].bitcast(FP4X4)
+
+        def parted(name, n):
+            return keep.tile([P, 2, 2 * n], U8, name=name, align_bytes=64)
 
         u_codes = {}
         u_scales = {}
 
         def quantise_u(b, tag):
             grouped = keep.tile([P, M, 4], BF16, name=f"grouped{b}", tag=tag, align_bytes=64)
-            nc.scalar.copy(grouped[:], u_raw[b].rearrange("p j n -> p n j"))
+            nc.scalar.copy(grouped[:], u_raw[b][:].rearrange("p j n -> p n j"))
             u_codes[b] = keep.tile([P, M], U32, name=f"u_codes{b}", align_bytes=64)
             u_scales[b] = keep.tile([P, M], U8, name=f"u_scales{b}", align_bytes=64)
             nc.vector.quantize_mx(
@@ -170,7 +154,9 @@ def tile_list_tab48_res_kernel(tc, tab, w4_words, w4_scales, tab2, u, r, offs, o
             )
 
         tab2_picked = gather_scales(tab2_rows, offs2_t, "tab2_picked")
-        load_u(2, "big2", True)
+        move_tab2_scales(0, 0)
+        load_u(3, "rows_then_u3")
+        move_tab2_scales(0, 1)
 
         for c in range(2):
             for m in range(4):
@@ -181,32 +167,41 @@ def tile_list_tab48_res_kernel(tc, tab, w4_words, w4_scales, tab2, u, r, offs, o
                 for m in range(4):
                     multiply_tab2(b, c, m, start=b == 0)
 
-        gather_tab2_words(0, 0, "stage0")
+        stage0 = keep.tile([P, HALF], I32, name="stage0", tag="stage0", align_bytes=64)
+        gather_tab2_words(0, 0, HALF, stage0[:])
         tab_picked = gather_scales(tab_rows, offs_t, "tab_picked")
-        move_tab_scales(0)
-        load_w4_words()
-        part_tab2_words(0, 0)
-        quantise_u(0, "stage1")
-        first_half_tab2(0)
-        gather_tab2_words(0, 1, "stage1")
-        quantise_u(1, "stage2")
-        first_half_tab2(1)
+        w4["words"] = keep.tile([P, TAB_PASSES, M // 2], I32, name="w4_w", tag="rows_then_w4", align_bytes=64)
+        nc.sync.dma_start(w4["words"][:], w4_words.rearrange("a p b -> p a b").bitcast(I32))
+        part_tab2_words(0, 0, HALF, stage0[:], parted("g2w0_first", HALF))
+        quantise_u(0, "grouped0")
         first, second, last = 1, 2, 0
-        load_words(tab_w, first, tab[first], "u_first")
-        load_words(tab_w, second, tab[second], "big0")
-        gather_tab2_words(1, 0, "stage0")
-        part_tab2_words(0, 1)
-        part_tab2_words(1, 0)
-        load_words(tab_w, last, tab[last], "stage0")
-        quantise_u(2, "stage2")
+        load_words(tab_w, first, tab[first], "u0_then_first")
+        first_half_tab2(0)
+        stage1 = keep.tile([P, HALF], I32, name="stage1", tag="grouped0", align_bytes=64)
+        gather_tab2_words(0, HALF, HALF, stage1[:])
+        quantise_u(1, "grouped1_then_second")
+        tab_planes[0] = keep.tile([P, TAB_PASSES, HALF // 4], I32, name="tab_early", tag="u1_then_planes", align_bytes=64)
+        move_tab_scales(0)
+        load_words(tab_w, second, tab[second], "grouped1_then_second")
+        first_half_tab2(1)
+        stage2 = keep.tile([P, 3 * N], I32, name="stage2", tag="stage0", align_bytes=64)
+        gather_tab2_words(1, 0, 3 * N, stage2[:])
+        part_tab2_words(0, HALF, HALF, stage1[:], parted("g2w0_second", HALF))
+        g2w1_first = shared.tile([P, 2, 2 * HALF], U8, name="g2w1_first", offset=HALF, align_bytes=64)
+        part_tab2_words(1, 0, HALF, stage2[:, 0:HALF], g2w1_first)
+        quantise_u(2, "grouped2_then_last")
+        load_words(tab_w, last, tab[last], "grouped2_then_last")
         first_half_tab2(2)
-        gather_tab2_words(1, 1, "stage2")
-        quantise_u(3, "stage3")
+        part_tab2_words(1, HALF, N, stage2[:, HALF : 3 * N], parted("g2w1_third", N))
+        quantise_u(3, "grouped0")
         first_half_tab2(3)
+
         tab_planes[1] = shared.tile([P, TAB_PASSES, HALF // 4], I32, name="tab_late", offset=0, align_bytes=64)
         r_all = shared.tile([P, 4, S], F32, name="r_all", offset=TAB_PASSES * HALF, align_bytes=64)
-        for m in range(4):
-            r_t[m] = r_all[:, m, :]
+
+        def load_r(m):
+            nc.sync.dma_start(r_all[:, m, :], r[P * m : P * (m + 1), :])
+
         move_tab2_scales(1, 0)
         load_r(0)
         move_tab_scales(1)
@@ -214,64 +209,61 @@ def tile_list_tab48_res_kernel(tc, tab, w4_words, w4_scales, tab2, u, r, offs, o
         move_tab2_scales(1, 1)
         load_r(2)
         load_r(3)
-        part_tab2_words(1, 1)
-        more = keep.tile([P, HALF], I32, name="gw_more", align_bytes=64)
-        gather_tab_words(first, HALF, HALF, more[:])
-        for a in (first, second):
-            for c in range(2):
-                early = keep.tile([P, N], I32, name=f"gw{a}_{c}", align_bytes=64)
-                gather_tab_words(a, N * c, N, early[:])
-                for m in range(4):
-                    multiply_tab(a, c, m, False)
 
-        sums = keep.tile([P, 4, N], F32, name="sums")
+        gw_first = keep.tile([P, 3 * N], I32, name="gw_first", align_bytes=64)
+        gather_tab_words(first, 0, 3 * N, gw_first[:])
         for c in range(2):
-            closing = keep.tile([P, N], I32, name=f"gw_closing{c}", tag=f"closing{c}", align_bytes=64)
-            gather_tab_words(last, N * c, N, closing[:])
+            for m in range(4):
+                multiply_tab(first, c, m)
+        for c in (2, 0, 1):
+            t = keep.tile([P, N], I32, name=f"gw_second{c}", align_bytes=64)
+            gather_tab_words(second, N * c, N, t[:])
+            if c < 2:
+                for m in range(4):
+                    multiply_tab(second, c, m)
+
+        late_at = TAB_PASSES * HALF + 4 * 4 * S
+        closing = shared.tile([P, 2, N], I32, name="closing", offset=late_at, align_bytes=64)
+        sums = keep.tile([P, 4, HALF], F32, name="sums")
+        for c in range(2):
+            gather_tab_words(last, N * c, N, closing[:, c, :])
             for m in range(4):
                 multiply_tab(last, c, m, True)
-                if c == 0:
-                    nc.scalar.copy(sums[:, m, :], acc[c, m][:])
+                nc.scalar.copy(sums[:, m, N * c : N * (c + 1)], acc[c, m][:])
 
         rest = keep.tile([P, HALF], I32, name="gw_rest", align_bytes=64)
         gather_tab_words(last, HALF, HALF, rest[:])
-        late = keep.tile([P, HALF], I32, name="gw_late", tag="closing0", align_bytes=64)
-        gather_tab_words(second, HALF, HALF, late[:])
+        late2 = shared.tile([P, N], I32, name="late2", offset=late_at, align_bytes=64)
+        late1 = shared.tile([P, 2, N], I32, name="late1", offset=late_at + 4 * N, align_bytes=64)
+        gather_tab2_words(1, 3 * N, N, late2[:])
+        gather_tab_words(first, 3 * N, N, late1[:, 0, :])
+        part_tab2_words(1, 3 * N, N, late2[:], parted("g2w1_fourth", N))
+        gather_tab_words(second, 3 * N, N, late1[:, 1, :])
 
-        def add(c, m, y):
-            cols_c = r_t[m][:, N * c : N * (c + 1)]
-            nc.vector.tensor_tensor(cols_c, y, cols_c, ADD)
-
-        def store(m, lo, n):
-            nc.sync.dma_start(out[P * m : P * (m + 1), lo : lo + n], r_t[m][:, lo : lo + n])
+        def add(m, lo, n, y):
+            cols_r = r_all[:, m, lo : lo + n]
+            nc.vector.tensor_tensor(cols_r, y, cols_r, ADD)
+            nc.sync.dma_start(out[P * m : P * (m + 1), lo : lo + n], cols_r)
 
         for m in range(4):
-            add(1, m, acc[1, m][:])
-            add(0, m, sums[:, m, :])
-            store(m, 0, HALF)
+            add(m, 0, HALF, sums[:, m, :])
 
-        groups = [(c, m) for m in range(4) for c in (2, 3)]
-        for i, (c, m) in enumerate(groups[:4]):
-            bank(c, m, i)
-            multiply_tab2(0, c, m, start=True)
-            multiply_tab2(2, c, m)
-        for a in (last, first, second):
-            for c, m in groups[:4]:
-                multiply_tab(a, c, m)
-        for c, m in groups[:4]:
-            multiply_tab2(1, c, m)
-            multiply_tab2(3, c, m, stop=True)
-            add(c, m, acc[c, m][:])
-            if c == 3:
-                store(m, HALF, HALF)
-        for i, (c, m) in enumerate(groups[4:]):
-            bank(c, m, 4 + i)
+        for m in range(4):
+            bank(2, m, m)
+        for b in (0, 2):
+            for m in range(4):
+                multiply_tab2(b, 2, m, start=b == 0)
+        for a in (first, second, last):
+            for m in range(4):
+                multiply_tab(a, 2, m)
+        for m in range(4):
+            multiply_tab2(1, 2, m)
+            multiply_tab2(3, 2, m, stop=True)
+            add(m, 2 * N, N, acc[2, m][:])
+        for m in range(4):
+            bank(3, m, 4 + m)
             for b in (1, 3, 0, 2):
-                multiply_tab2(b, c, m, start=b == 1)
+                multiply_tab2(b, 3, m, start=b == 1)
             for a in (last, first, second):
-                multiply_tab(a, c, m, a == second)
-            add(c, m, acc[c, m][:])
-            if m == 3:
-                store(m, N * c, N)
-            elif c == 3:
-                store(m, HALF, HALF)
+                multiply_tab(a, 3, m, a == second)
+            add(m, 3 * N, N, acc[3, m][:])

@@ -33,7 +33,9 @@ def tile_list_tab48_res_kernel(tc, tab, w4_words, w4_scales, tab2, u, r, offs, o
         tab_rows = keep.tile([P, T // 4], I32, name="tab_rows", tag="rows_then_w4", align_bytes=64)
         tab2_rows = keep.tile([P, T // 4], I32, name="tab2_rows", tag="rows_then_u3", align_bytes=64)
         tab_planes = {}
-        tab2_planes = [keep.tile([P, 2, HALF // 4], I32, name=f"tab2_planes{h}", align_bytes=64) for h in range(2)]
+        tab2_planes = {}
+        for h in range(2):
+            tab2_planes[h, 0] = keep.tile([P, 2, HALF // 4], I32, name=f"tab2_planes{h}", align_bytes=64)
 
         w4_s = keep.tile([P, TAB_PASSES, M // 4], I32, name="w4_s", align_bytes=64)
         nc.gpsimd.memset(tab_rows[:], 0)
@@ -84,13 +86,19 @@ def tile_list_tab48_res_kernel(tc, tab, w4_words, w4_scales, tab2, u, r, offs, o
             words = slice(half * HALF // 4, (half + 1) * HALF // 4)
             for j in range(4):
                 lo = 32 + 32 * (j // 2) + j % 2 + 16 * h
-                nc.sync.dma_start(tab2_planes[h][j:P:32, :, :], tab2_picked[lo : lo + 15 : 2, words])
+                nc.sync.dma_start(tab2_planes[h, half][j:P:32, :, :], tab2_picked[lo : lo + 15 : 2, words])
 
-        def move_tab_scales(half):
-            words = slice(half * HALF // 4, (half + 1) * HALF // 4)
+        def move_tab_scales_early(a, tag):
+            plane = keep.tile([P, HALF // 4], I32, name=f"tab_early{a}", tag=tag, align_bytes=64)
+            tab_planes[a, 0] = plane[:]
+            for j in range(4):
+                lo = 32 + 3 * j + 4 * a
+                nc.sync.dma_start(plane[j:P:32, :], tab_picked[lo : lo + 37 : 12, 0 : HALF // 4])
+
+        def move_tab_scales_late():
             for j in range(4):
                 lo = 32 + 3 * j
-                nc.sync.dma_start(tab_planes[half][j:P:32, :, :], tab_picked[lo : lo + 45 : 4, words])
+                nc.sync.dma_start(tab_late[j:P:32, :, :], tab_picked[lo : lo + 45 : 4, HALF // 4 : S // 4])
 
         gw = {}
         g2w = {}
@@ -134,10 +142,10 @@ def tile_list_tab48_res_kernel(tc, tab, w4_words, w4_scales, tab2, u, r, offs, o
         def multiply_tab(a, c, m, stop=False):
             nc.tensor.matmul_mx(
                 out=acc[c, m][:],
-                lhsT=w4["words"][:, a, 64 * m : 64 * (m + 1)].bitcast(FP4X4),
+                lhsT=w4[a][:, 64 * m : 64 * (m + 1)].bitcast(FP4X4),
                 lhsT_scale=w4_s[:, a, 32 * m : 32 * (m + 1)].bitcast(U8),
                 rhs=gw[a, c],
-                rhs_scale=tab_planes[c // 2][:, a, 128 * (c % 2) : 128 * (c % 2 + 1)].bitcast(U8),
+                rhs_scale=tab_planes[a, c // 2][:, 128 * (c % 2) : 128 * (c % 2 + 1)].bitcast(U8),
                 start=False,
                 stop=stop,
             )
@@ -148,7 +156,7 @@ def tile_list_tab48_res_kernel(tc, tab, w4_words, w4_scales, tab2, u, r, offs, o
                 lhsT=u_codes[b][:, P * m : P * (m + 1)].bitcast(FP8X4),
                 lhsT_scale=u_scales[b][:, P * m : P * (m + 1)],
                 rhs=g2w[b, c],
-                rhs_scale=tab2_planes[b % 2][:, b // 2, 128 * (c % 2) : 128 * (c % 2 + 1)].bitcast(U8),
+                rhs_scale=tab2_planes[b % 2, c // 2][:, b // 2, 128 * (c % 2) : 128 * (c % 2 + 1)].bitcast(U8),
                 start=start,
                 stop=stop,
             )
@@ -170,8 +178,9 @@ def tile_list_tab48_res_kernel(tc, tab, w4_words, w4_scales, tab2, u, r, offs, o
         stage0 = keep.tile([P, HALF], I32, name="stage0", tag="stage0", align_bytes=64)
         gather_tab2_words(0, 0, HALF, stage0[:])
         tab_picked = gather_scales(tab_rows, offs_t, "tab_picked")
-        w4["words"] = keep.tile([P, TAB_PASSES, M // 2], I32, name="w4_w", tag="rows_then_w4", align_bytes=64)
-        nc.sync.dma_start(w4["words"][:], w4_words.rearrange("a p b -> p a b").bitcast(I32))
+        w4_early = keep.tile([P, 2, M // 2], I32, name="w4_early", tag="rows_then_w4", align_bytes=64)
+        nc.sync.dma_start(w4_early[:], w4_words[1:3].rearrange("a p b -> p a b").bitcast(I32))
+        w4[1], w4[2] = w4_early[:, 0, :], w4_early[:, 1, :]
         part_tab2_words(0, 0, HALF, stage0[:], parted("g2w0_first", HALF))
         quantise_u(0, "grouped0")
         first, second, last = 1, 2, 0
@@ -180,38 +189,49 @@ def tile_list_tab48_res_kernel(tc, tab, w4_words, w4_scales, tab2, u, r, offs, o
         stage1 = keep.tile([P, HALF], I32, name="stage1", tag="grouped0", align_bytes=64)
         gather_tab2_words(0, HALF, HALF, stage1[:])
         quantise_u(1, "grouped1_then_second")
-        tab_planes[0] = keep.tile([P, TAB_PASSES, HALF // 4], I32, name="tab_early", tag="u1_then_planes", align_bytes=64)
-        move_tab_scales(0)
+        move_tab_scales_early(first, "u1_then_planes")
         load_words(tab_w, second, tab[second], "grouped1_then_second")
         first_half_tab2(1)
         stage2 = keep.tile([P, 3 * N], I32, name="stage2", tag="stage0", align_bytes=64)
         gather_tab2_words(1, 0, 3 * N, stage2[:])
         part_tab2_words(0, HALF, HALF, stage1[:], parted("g2w0_second", HALF))
-        g2w1_first = shared.tile([P, 2, 2 * HALF], U8, name="g2w1_first", offset=HALF, align_bytes=64)
+        g2w1_first = shared.tile([P, 2, 2 * HALF], U8, name="g2w1_first", offset=2 * HALF, align_bytes=64)
         part_tab2_words(1, 0, HALF, stage2[:, 0:HALF], g2w1_first)
         quantise_u(2, "grouped2_then_last")
+        move_tab_scales_early(second, "u2")
         load_words(tab_w, last, tab[last], "grouped2_then_last")
         first_half_tab2(2)
         part_tab2_words(1, HALF, N, stage2[:, HALF : 3 * N], parted("g2w1_third", N))
         quantise_u(3, "grouped0")
+        w4_last = keep.tile([P, M // 2], I32, name="w4_last", tag="rows_then_u3", align_bytes=64)
+        nc.sync.dma_start(w4_last[:], w4_words[last].bitcast(I32))
+        w4[last] = w4_last[:]
+        move_tab_scales_early(last, "grouped0")
         first_half_tab2(3)
 
-        tab_planes[1] = shared.tile([P, TAB_PASSES, HALF // 4], I32, name="tab_late", offset=0, align_bytes=64)
-        r_all = shared.tile([P, 4, S], F32, name="r_all", offset=TAB_PASSES * HALF, align_bytes=64)
+        tab_late = shared.tile([P, TAB_PASSES, HALF // 4], I32, name="tab_late", offset=0, align_bytes=64)
+        for a in range(TAB_PASSES):
+            tab_planes[a, 1] = tab_late[:, a, :]
+        tab2_planes[0, 1] = shared.tile([P, 2, HALF // 4], I32, name="tab2_late", offset=3 * HALF, align_bytes=64)
+        tab2_planes[1, 1] = tab2_planes[1, 0]
+        r_all = shared.tile([P, 4, S], F32, name="r_all", offset=5 * HALF, align_bytes=64)
 
-        def load_r(m):
-            nc.sync.dma_start(r_all[:, m, :], r[P * m : P * (m + 1), :])
+        def load_r(m, tiles, half):
+            items = slice(HALF * half, HALF * (half + 1))
+            rows = r[P * m : P * (m + tiles), items].rearrange("(m p) n -> p m n", p=P)
+            nc.sync.dma_start(r_all[:, m : m + tiles, items], rows)
 
+        load_r(0, 2, 0)
         move_tab2_scales(1, 0)
-        load_r(0)
-        move_tab_scales(1)
-        load_r(1)
+        load_r(2, 1, 0)
+        move_tab_scales_late()
+        load_r(3, 1, 0)
         move_tab2_scales(1, 1)
-        load_r(2)
-        load_r(3)
+        load_r(0, 2, 1)
+        load_r(2, 2, 1)
 
-        gw_first = keep.tile([P, 3 * N], I32, name="gw_first", align_bytes=64)
-        gather_tab_words(first, 0, 3 * N, gw_first[:])
+        gw_first = keep.tile([P, S], I32, name="gw_first", align_bytes=64)
+        gather_tab_words(first, 0, S, gw_first[:])
         for c in range(2):
             for m in range(4):
                 multiply_tab(first, c, m)
@@ -222,7 +242,7 @@ def tile_list_tab48_res_kernel(tc, tab, w4_words, w4_scales, tab2, u, r, offs, o
                 for m in range(4):
                     multiply_tab(second, c, m)
 
-        late_at = TAB_PASSES * HALF + 4 * 4 * S
+        late_at = 5 * HALF + 4 * 4 * S
         closing = shared.tile([P, 2, N], I32, name="closing", offset=late_at, align_bytes=64)
         sums = keep.tile([P, 4, HALF], F32, name="sums")
         for c in range(2):
@@ -234,19 +254,21 @@ def tile_list_tab48_res_kernel(tc, tab, w4_words, w4_scales, tab2, u, r, offs, o
         rest = keep.tile([P, HALF], I32, name="gw_rest", align_bytes=64)
         gather_tab_words(last, HALF, HALF, rest[:])
         late2 = shared.tile([P, N], I32, name="late2", offset=late_at, align_bytes=64)
-        late1 = shared.tile([P, 2, N], I32, name="late1", offset=late_at + 4 * N, align_bytes=64)
+        late1 = shared.tile([P, N], I32, name="late1", offset=late_at + 4 * N, align_bytes=64)
         gather_tab2_words(1, 3 * N, N, late2[:])
-        gather_tab_words(first, 3 * N, N, late1[:, 0, :])
+        gather_tab_words(second, 3 * N, N, late1[:])
         part_tab2_words(1, 3 * N, N, late2[:], parted("g2w1_fourth", N))
-        gather_tab_words(second, 3 * N, N, late1[:, 1, :])
 
         def add(m, lo, n, y):
             cols_r = r_all[:, m, lo : lo + n]
             nc.vector.tensor_tensor(cols_r, y, cols_r, ADD)
-            nc.sync.dma_start(out[P * m : P * (m + 1), lo : lo + n], cols_r)
+
+        def store(m, lo, n):
+            nc.sync.dma_start(out[P * m : P * (m + 1), lo : lo + n], r_all[:, m, lo : lo + n])
 
         for m in range(4):
             add(m, 0, HALF, sums[:, m, :])
+            store(m, 0, HALF)
 
         for m in range(4):
             bank(2, m, m)
@@ -260,6 +282,7 @@ def tile_list_tab48_res_kernel(tc, tab, w4_words, w4_scales, tab2, u, r, offs, o
             multiply_tab2(1, 2, m)
             multiply_tab2(3, 2, m, stop=True)
             add(m, 2 * N, N, acc[2, m][:])
+        store(3, 2 * N, N)
         for m in range(4):
             bank(3, m, 4 + m)
             for b in (1, 3, 0, 2):
@@ -267,3 +290,7 @@ def tile_list_tab48_res_kernel(tc, tab, w4_words, w4_scales, tab2, u, r, offs, o
             for a in (last, first, second):
                 multiply_tab(a, 3, m, a == second)
             add(m, 3 * N, N, acc[3, m][:])
+            if m < 3:
+                store(m, HALF, HALF)
+            else:
+                store(m, 3 * N, N)

@@ -114,7 +114,10 @@ def tile_list_tab48_res_kernel(tc, tab, w4_words, w4_scales, tab2, u, r, offs, o
             pairs[m, lo] = t
 
         def part_tab2_words(m, lo, n, src, w):
-            nc.vector.tensor_copy(w[:].bitcast(U16), src.bitcast(U16).rearrange("p (n h) -> p h n", h=2))
+            nc.vector.tensor_copy(
+                w[:].bitcast(U16).rearrange("p h (g i) -> p g h i", i=8),
+                src.bitcast(U16).rearrange("p (g i h) -> p g h i", i=8, h=2),
+            )
             for h in range(2):
                 for c in range(n // N):
                     g2w[2 * m + h, lo // N + c] = w[:, h, 2 * N * c : 2 * N * (c + 1)].bitcast(FP4X4)

@@ -233,34 +233,36 @@ def tile_list_tab48_res_kernel(tc, tab, w4_words, w4_scales, tab2, u, r, offs, o
         load_r(0, 2, 1)
         load_r(2, 2, 1)
 
-        gw_first = keep.tile([P, S], I32, name="gw_first", align_bytes=64)
-        gather_tab_words(first, 0, S, gw_first[:])
+        gw_first = keep.tile([P, 2, HALF], I32, name="gw_first", align_bytes=64)
+        gather_tab_words(first, HALF, HALF, gw_first[:, 1, :])
         for c in range(2):
+            gather_tab_words(first, N * c, N, gw_first[:, 0, N * c : N * (c + 1)])
             for m in range(4):
                 multiply_tab(first, c, m)
-        for c in (2, 0, 1):
+        for c in range(2):
             t = keep.tile([P, N], I32, name=f"gw_second{c}", align_bytes=64)
             gather_tab_words(second, N * c, N, t[:])
-            if c < 2:
-                for m in range(4):
-                    multiply_tab(second, c, m)
+            for m in range(4):
+                multiply_tab(second, c, m)
 
         late_at = 5 * HALF + 4 * 4 * S
         closing = shared.tile([P, 2, N], I32, name="closing", offset=late_at, align_bytes=64)
-        sums = keep.tile([P, 4, HALF], F32, name="sums")
+        sums = keep.tile([P, 4, N], F32, name="sums")
         for c in range(2):
             gather_tab_words(last, N * c, N, closing[:, c, :])
             for m in range(4):
                 multiply_tab(last, c, m, True)
-                nc.scalar.copy(sums[:, m, N * c : N * (c + 1)], acc[c, m][:])
+                if c == 0:
+                    nc.scalar.copy(sums[:, m, :], acc[c, m][:])
 
         rest = keep.tile([P, HALF], I32, name="gw_rest", align_bytes=64)
         gather_tab_words(last, HALF, HALF, rest[:])
         late2 = shared.tile([P, N], I32, name="late2", offset=late_at, align_bytes=64)
-        late1 = shared.tile([P, N], I32, name="late1", offset=late_at + 4 * N, align_bytes=64)
+        late1 = shared.tile([P, 2, N], I32, name="late1", offset=late_at + 4 * N, align_bytes=64)
         gather_tab2_words(1, 3 * N, N, late2[:])
-        gather_tab_words(second, 3 * N, N, late1[:])
+        gather_tab_words(second, 2 * N, N, late1[:, 0, :])
         part_tab2_words(1, 3 * N, N, late2[:], parted("g2w1_fourth", N))
+        gather_tab_words(second, 3 * N, N, late1[:, 1, :])
 
         def add(m, lo, n, y):
             cols_r = r_all[:, m, lo : lo + n]
@@ -269,16 +271,18 @@ def tile_list_tab48_res_kernel(tc, tab, w4_words, w4_scales, tab2, u, r, offs, o
         def store(m, lo, n):
             nc.sync.dma_start(out[P * m : P * (m + 1), lo : lo + n], r_all[:, m, lo : lo + n])
 
+        first_half = keep.tile([P, 4, HALF], F32, name="first_half", tag="grouped1_then_second", align_bytes=64)
         for m in range(4):
-            add(m, 0, HALF, sums[:, m, :])
-            store(m, 0, HALF)
+            nc.vector.tensor_tensor(first_half[:, m, N:HALF], acc[1, m][:], r_all[:, m, N:HALF], ADD)
+            nc.gpsimd.tensor_tensor(first_half[:, m, 0:N], sums[:, m, :], r_all[:, m, 0:N], ADD)
+            nc.sync.dma_start(out[P * m : P * (m + 1), 0:HALF], first_half[:, m, :])
 
         for m in range(4):
             bank(2, m, m)
         for b in (0, 2):
             for m in range(4):
                 multiply_tab2(b, 2, m, start=b == 0)
-        for a in (first, second, last):
+        for a in (first, last, second):
             for m in range(4):
                 multiply_tab(a, 2, m)
         for m in range(4):

@@ -66,9 +66,8 @@ def tile_list_tab48_res_kernel(tc, tab, w4_words, w4_scales, tab2, u, r, offs, o
             nc.sync.dma_start(u_raw[b][:], u[512 * b : 512 * (b + 1), :].rearrange("(p j) n -> p j n", j=4))
 
         load_words(tab2_w, 0, tab2[0], "tab2_w0")
-        for a in range(TAB_PASSES):
-            rows = tab[a, 512 * T : 528 * T].rearrange("(q c) -> q c", q=16).bitcast(I32)
-            nc.sync.dma_start(tab_rows[32 + 4 * a : 32 + 4 * a + 46 : 3, :], rows)
+        rows = tab[:, 512 * T : 528 * T].rearrange("a (q c) -> q a c", q=16).bitcast(I32)
+        nc.sync.dma_start(tab_rows[32:80, :], rows)
         load_u(0, "u0_then_first")
         load_u(1, "u1_then_planes")
         load_words(tab2_w, 1, tab2[1], "tab2_w1")
@@ -88,17 +87,17 @@ def tile_list_tab48_res_kernel(tc, tab, w4_words, w4_scales, tab2, u, r, offs, o
                 lo = 32 + 32 * (j // 2) + j % 2 + 16 * h
                 nc.sync.dma_start(tab2_planes[h, half][j:P:32, :, :], tab2_picked[lo : lo + 15 : 2, words])
 
-        def move_tab_scales_early(a, tag):
-            plane = keep.tile([P, HALF // 4], I32, name=f"tab_early{a}", tag=tag, align_bytes=64)
-            tab_planes[a, 0] = plane[:]
+        def move_tab_scales(a, half, halves, plane):
+            for i in range(halves):
+                tab_planes[a, half + i] = plane[:, HALF // 4 * i : HALF // 4 * (i + 1)]
             for j in range(4):
-                lo = 32 + 3 * j + 4 * a
-                nc.sync.dma_start(plane[j:P:32, :], tab_picked[lo : lo + 37 : 12, 0 : HALF // 4])
+                lo = 32 + 3 * j + a
+                words = slice(HALF // 4 * half, HALF // 4 * (half + halves))
+                nc.sync.dma_start(plane[j:P:32, :], tab_picked[lo : lo + 37 : 12, words])
 
-        def move_tab_scales_late():
-            for j in range(4):
-                lo = 32 + 3 * j
-                nc.sync.dma_start(tab_late[j:P:32, :, :], tab_picked[lo : lo + 45 : 4, HALF // 4 : S // 4])
+        def move_tab_scales_early(a, halves, tag):
+            plane = keep.tile([P, halves * HALF // 4], I32, name=f"tab_early{a}", tag=tag, align_bytes=64)
+            move_tab_scales(a, 0, halves, plane)
 
         gw = {}
         g2w = {}
@@ -107,7 +106,7 @@ def tile_list_tab48_res_kernel(tc, tab, w4_words, w4_scales, tab2, u, r, offs, o
         def gather_tab_words(a, lo, n, t):
             nc.vector.tensor_copy(t.bitcast(U32), tab_w[a][:].bitcast(U32).indirect(offs_t[:, cols(lo, n)]))
             for c in range(lo, lo + n, N):
-                gw[a, c // N] = t[:, c - lo : c - lo + N].bitcast(FP8X4)
+                gw[a, c // N] = t[:, c - lo : c - lo + N]
 
         def gather_tab2_words(m, lo, n, t):
             nc.vector.tensor_copy(t.bitcast(U32), tab2_w[m][:].bitcast(U32).indirect(offs2_t[:, cols(lo, n)]))
@@ -120,7 +119,7 @@ def tile_list_tab48_res_kernel(tc, tab, w4_words, w4_scales, tab2, u, r, offs, o
             )
             for h in range(2):
                 for c in range(n // N):
-                    g2w[2 * m + h, lo // N + c] = w[:, h, 2 * N * c : 2 * N * (c + 1)].bitcast(FP4X4)
+                    g2w[2 * m + h, lo // N + c] = w[:, h, 2 * N * c : 2 * N * (c + 1)]
 
         def parted(name, n):
             return keep.tile([P, 2, 2 * n], U8, name=name, align_bytes=64)
@@ -142,24 +141,26 @@ def tile_list_tab48_res_kernel(tc, tab, w4_words, w4_scales, tab2, u, r, offs, o
         def bank(c, m, i):
             acc[c, m] = psum.tile([P, N], F32, name=f"bank{i}")
 
-        def multiply_tab(a, c, m, stop=False):
+        def multiply_tab(a, c, m, stop=False, lo=0, n=N, start=False):
+            at = (N * (c % 2) + lo) // 4
             nc.tensor.matmul_mx(
                 out=acc[c, m][:],
                 lhsT=w4[a][:, 64 * m : 64 * (m + 1)].bitcast(FP4X4),
                 lhsT_scale=w4_s[:, a, 32 * m : 32 * (m + 1)].bitcast(U8),
-                rhs=gw[a, c],
-                rhs_scale=tab_planes[a, c // 2][:, 128 * (c % 2) : 128 * (c % 2 + 1)].bitcast(U8),
-                start=False,
+                rhs=gw[a, c][:, lo : lo + n].bitcast(FP8X4),
+                rhs_scale=tab_planes[a, c // 2][:, at : at + n // 4].bitcast(U8),
+                start=start,
                 stop=stop,
             )
 
-        def multiply_tab2(b, c, m, start=False, stop=False):
+        def multiply_tab2(b, c, m, start=False, stop=False, lo=0, n=N):
+            at = (N * (c % 2) + lo) // 4
             nc.tensor.matmul_mx(
                 out=acc[c, m][:],
                 lhsT=u_codes[b][:, P * m : P * (m + 1)].bitcast(FP8X4),
                 lhsT_scale=u_scales[b][:, P * m : P * (m + 1)],
-                rhs=g2w[b, c],
-                rhs_scale=tab2_planes[b % 2, c // 2][:, b // 2, 128 * (c % 2) : 128 * (c % 2 + 1)].bitcast(U8),
+                rhs=g2w[b, c][:, 2 * lo : 2 * (lo + n)].bitcast(FP4X4),
+                rhs_scale=tab2_planes[b % 2, c // 2][:, b // 2, at : at + n // 4].bitcast(U8),
                 start=start,
                 stop=stop,
             )
@@ -192,7 +193,7 @@ def tile_list_tab48_res_kernel(tc, tab, w4_words, w4_scales, tab2, u, r, offs, o
         stage1 = keep.tile([P, HALF], I32, name="stage1", tag="grouped0", align_bytes=64)
         gather_tab2_words(0, HALF, HALF, stage1[:])
         quantise_u(1, "grouped1_then_second")
-        move_tab_scales_early(first, "u1_then_planes")
+        move_tab_scales_early(first, 1, "u1_then_planes")
         load_words(tab_w, second, tab[second], "grouped1_then_second")
         first_half_tab2(1)
         stage2 = keep.tile([P, 3 * N], I32, name="stage2", tag="stage0", align_bytes=64)
@@ -201,7 +202,7 @@ def tile_list_tab48_res_kernel(tc, tab, w4_words, w4_scales, tab2, u, r, offs, o
         g2w1_first = shared.tile([P, 2, 2 * HALF], U8, name="g2w1_first", offset=2 * HALF, align_bytes=64)
         part_tab2_words(1, 0, HALF, stage2[:, 0:HALF], g2w1_first)
         quantise_u(2, "grouped2_then_last")
-        move_tab_scales_early(second, "u2")
+        move_tab_scales_early(second, 1, "u2")
         load_words(tab_w, last, tab[last], "grouped2_then_last")
         first_half_tab2(2)
         part_tab2_words(1, HALF, N, stage2[:, HALF : 3 * N], parted("g2w1_third", N))
@@ -209,14 +210,14 @@ def tile_list_tab48_res_kernel(tc, tab, w4_words, w4_scales, tab2, u, r, offs, o
         w4_last = keep.tile([P, M // 2], I32, name="w4_last", tag="rows_then_u3", align_bytes=64)
         nc.sync.dma_start(w4_last[:], w4_words[last].bitcast(I32))
         w4[last] = w4_last[:]
-        move_tab_scales_early(last, "grouped0")
+        move_tab_scales_early(last, 2, "grouped0")
         first_half_tab2(3)
 
-        tab_late = shared.tile([P, TAB_PASSES, HALF // 4], I32, name="tab_late", offset=0, align_bytes=64)
-        for a in range(TAB_PASSES):
-            tab_planes[a, 1] = tab_late[:, a, :]
-        tab2_planes[0, 1] = shared.tile([P, 2, HALF // 4], I32, name="tab2_late", offset=3 * HALF, align_bytes=64)
+        tab2_planes[0, 1] = shared.tile([P, 2, HALF // 4], I32, name="tab2_late", offset=HALF, align_bytes=64)
         tab2_planes[1, 1] = tab2_planes[1, 0]
+        late_planes = {}
+        for i, a in enumerate((first, second)):
+            late_planes[a] = shared.tile([P, HALF // 4], I32, name=f"tab_late{a}", offset=(3 + i) * HALF, align_bytes=64)
         r_all = shared.tile([P, 4, S], F32, name="r_all", offset=5 * HALF, align_bytes=64)
 
         def load_r(m, tiles, half):
@@ -227,23 +228,27 @@ def tile_list_tab48_res_kernel(tc, tab, w4_words, w4_scales, tab2, u, r, offs, o
         load_r(0, 2, 0)
         move_tab2_scales(1, 0)
         load_r(2, 1, 0)
-        move_tab_scales_late()
-        load_r(3, 1, 0)
         move_tab2_scales(1, 1)
-        load_r(0, 2, 1)
+        load_r(3, 1, 0)
+        move_tab_scales(first, 1, 1, late_planes[first])
+        load_r(0, 1, 1)
+        move_tab_scales(second, 1, 1, late_planes[second])
+        load_r(1, 1, 1)
         load_r(2, 2, 1)
 
         gw_first = keep.tile([P, 2, HALF], I32, name="gw_first", align_bytes=64)
         gather_tab_words(first, HALF, HALF, gw_first[:, 1, :])
         for c in range(2):
             gather_tab_words(first, N * c, N, gw_first[:, 0, N * c : N * (c + 1)])
-            for m in range(4):
-                multiply_tab(first, c, m)
+        for m in range(4):
+            multiply_tab(first, 0, m)
         for c in range(2):
             t = keep.tile([P, N], I32, name=f"gw_second{c}", align_bytes=64)
             gather_tab_words(second, N * c, N, t[:])
             for m in range(4):
                 multiply_tab(second, c, m)
+        for m in range(4):
+            multiply_tab(first, 1, m)
 
         late_at = 5 * HALF + 4 * 4 * S
         closing = shared.tile([P, 2, N], I32, name="closing", offset=late_at, align_bytes=64)
@@ -255,8 +260,9 @@ def tile_list_tab48_res_kernel(tc, tab, w4_words, w4_scales, tab2, u, r, offs, o
                 if c == 0:
                     nc.scalar.copy(sums[:, m, :], acc[c, m][:])
 
-        rest = keep.tile([P, HALF], I32, name="gw_rest", align_bytes=64)
-        gather_tab_words(last, HALF, HALF, rest[:])
+        rest = keep.tile([P, 2, N], I32, name="gw_rest", align_bytes=64)
+        for c in (2, 3):
+            gather_tab_words(last, N * c, N, rest[:, c - 2, :])
         late2 = shared.tile([P, N], I32, name="late2", offset=late_at, align_bytes=64)
         late1 = shared.tile([P, 2, N], I32, name="late1", offset=late_at + 4 * N, align_bytes=64)
         gather_tab2_words(1, 3 * N, N, late2[:])
@@ -279,25 +285,30 @@ def tile_list_tab48_res_kernel(tc, tab, w4_words, w4_scales, tab2, u, r, offs, o
 
         for m in range(4):
             bank(2, m, m)
-        for b in (0, 2):
-            for m in range(4):
-                multiply_tab2(b, 2, m, start=b == 0)
-        for a in (first, last, second):
-            for m in range(4):
-                multiply_tab(a, 2, m)
         for m in range(4):
-            multiply_tab2(1, 2, m)
-            multiply_tab2(3, 2, m, stop=True)
+            multiply_tab(last, 2, m, start=True)
+        for b in (0, 2, 1, 3):
+            for m in range(4):
+                multiply_tab2(b, 2, m)
+        for m in range(4):
+            multiply_tab(first, 2, m)
+        for m in range(4):
+            multiply_tab(second, 2, m, stop=True)
             add(m, 2 * N, N, acc[2, m][:])
         store(3, 2 * N, N)
-        for m in range(4):
+        for m in range(3):
             bank(3, m, 4 + m)
-            for b in (1, 3, 0, 2):
-                multiply_tab2(b, 3, m, start=b == 1)
-            for a in (last, first, second):
-                multiply_tab(a, 3, m, a == second)
+            for a in (second, first, last):
+                multiply_tab(a, 3, m, start=a == second)
+            for b in range(4):
+                multiply_tab2(b, 3, m, stop=b == 3)
             add(m, 3 * N, N, acc[3, m][:])
-            if m < 3:
-                store(m, HALF, HALF)
-            else:
-                store(m, 3 * N, N)
+            store(m, HALF, HALF)
+        for i, free_bank in enumerate((7, 0, 1, 2)):
+            acc[3, 3] = psum.tile([P, P], F32, name=f"bank{free_bank}")
+            for a in (second, first, last):
+                multiply_tab(a, 3, 3, lo=P * i, n=P, start=a == second)
+            for b in range(4):
+                multiply_tab2(b, 3, 3, stop=b == 3, lo=P * i, n=P)
+            add(3, 3 * N + P * i, P, acc[3, 3][:])
+            store(3, 3 * N + P * i, P)

@@ -231,9 +231,8 @@ def tile_list_tab48_res_kernel(tc, tab, w4_words, w4_scales, tab2, u, r, offs, o
         move_tab2_scales(1, 1)
         load_r(3, 1, 0)
         move_tab_scales(first, 1, 1, late_planes[first])
-        load_r(0, 1, 1)
+        load_r(0, 2, 1)
         move_tab_scales(second, 1, 1, late_planes[second])
-        load_r(1, 1, 1)
         load_r(2, 2, 1)
 
         gw_first = keep.tile([P, 2, HALF], I32, name="gw_first", align_bytes=64)
@@ -292,11 +291,19 @@ def tile_list_tab48_res_kernel(tc, tab, w4_words, w4_scales, tab2, u, r, offs, o
                 multiply_tab2(b, 2, m)
         for m in range(4):
             multiply_tab(first, 2, m)
+        bank(3, 0, 4)
+        for a in (first, last):
+            multiply_tab(a, 3, 0, start=a == first)
+        for b in range(4):
+            multiply_tab2(b, 3, 0)
         for m in range(4):
             multiply_tab(second, 2, m, stop=True)
             add(m, 2 * N, N, acc[2, m][:])
+        multiply_tab(second, 3, 0, stop=True)
+        add(0, 3 * N, N, acc[3, 0][:])
+        store(0, HALF, HALF)
         store(3, 2 * N, N)
-        for m in range(3):
+        for m in (1, 2):
             bank(3, m, 4 + m)
             for a in (second, first, last):
                 multiply_tab(a, 3, m, start=a == second)
@@ -311,4 +318,6 @@ def tile_list_tab48_res_kernel(tc, tab, w4_words, w4_scales, tab2, u, r, offs, o
             for b in range(4):
                 multiply_tab2(b, 3, 3, stop=b == 3, lo=P * i, n=P)
             add(3, 3 * N + P * i, P, acc[3, 3][:])
-            store(3, 3 * N + P * i, P)
+            if i == 2:
+                store(3, 3 * N, 3 * P)
+        store(3, S - P, P)

@@ -246,6 +246,8 @@ def tile_list_tab48_res_kernel(tc, tab, w4_words, w4_scales, tab2, u, r, offs, o
             gather_tab_words(second, N * c, N, t[:])
             for m in range(4):
                 multiply_tab(second, c, m)
+        third = keep.tile([P, N], I32, name="gw_second2", align_bytes=64)
+        gather_tab_words(second, 2 * N, N, third[:])
         for m in range(4):
             multiply_tab(first, 1, m)
 
@@ -260,14 +262,13 @@ def tile_list_tab48_res_kernel(tc, tab, w4_words, w4_scales, tab2, u, r, offs, o
                     nc.scalar.copy(sums[:, m, :], acc[c, m][:])
 
         rest = keep.tile([P, 2, N], I32, name="gw_rest", align_bytes=64)
-        for c in (2, 3):
-            gather_tab_words(last, N * c, N, rest[:, c - 2, :])
+        gather_tab_words(last, 2 * N, N, rest[:, 0, :])
         late2 = shared.tile([P, N], I32, name="late2", offset=late_at, align_bytes=64)
-        late1 = shared.tile([P, 2, N], I32, name="late1", offset=late_at + 4 * N, align_bytes=64)
+        late1 = shared.tile([P, N], I32, name="late1", offset=late_at + 4 * N, align_bytes=64)
         gather_tab2_words(1, 3 * N, N, late2[:])
-        gather_tab_words(second, 2 * N, N, late1[:, 0, :])
+        gather_tab_words(last, 3 * N, N, rest[:, 1, :])
         part_tab2_words(1, 3 * N, N, late2[:], parted("g2w1_fourth", N))
-        gather_tab_words(second, 3 * N, N, late1[:, 1, :])
+        gather_tab_words(second, 3 * N, N, late1[:])
 
         def add(m, lo, n, y):
             cols_r = r_all[:, m, lo : lo + n]

@@ -278,9 +278,11 @@ def tile_list_tab48_res_kernel(tc, tab, w4_words, w4_scales, tab2, u, r, offs, o
             nc.sync.dma_start(out[P * m : P * (m + 1), lo : lo + n], r_all[:, m, lo : lo + n])
 
         first_half = keep.tile([P, 4, HALF], F32, name="first_half", tag="grouped1_then_second", align_bytes=64)
-        for m in range(4):
+        for m in (0, 2, 3, 1):
             nc.vector.tensor_tensor(first_half[:, m, N:HALF], acc[1, m][:], r_all[:, m, N:HALF], ADD)
-            nc.gpsimd.tensor_tensor(first_half[:, m, 0:N], sums[:, m, :], r_all[:, m, 0:N], ADD)
+        for m in (2, 3, 0, 1):
+            engine = nc.gpsimd if m >= 2 else nc.vector
+            engine.tensor_tensor(first_half[:, m, 0:N], sums[:, m, :], r_all[:, m, 0:N], ADD)
             nc.sync.dma_start(out[P * m : P * (m + 1), 0:HALF], first_half[:, m, :])
 
         for m in range(4):

@@ -20,6 +20,9 @@ FP8X4 = mybir.dt.float8_e4m3fn_x4
 FP4X4 = mybir.dt.float4_e2m1fn_x4
 ADD = mybir.AluOpType.add
 
+STRETCH = 64
+AT_PLANE, AT_WEIGHTS, AT_WEIGHT_SCALES = 16, 32, 48
+
 
 def tile_list_tab48_res_kernel(tc, tab, w4_words, w4_scales, tab2, u, r, offs, offs2, out):
     nc = tc.nc
@@ -30,14 +33,16 @@ def tile_list_tab48_res_kernel(tc, tab, w4_words, w4_scales, tab2, u, r, offs, o
 
         offs_t = keep.tile([P, S // 16], U16, name="offs_t")
         offs2_t = keep.tile([P, S // 16], U16, name="offs2_t")
-        tab_rows = keep.tile([P, T // 4], I32, name="tab_rows", tag="rows_then_w4", align_bytes=64)
-        tab2_rows = keep.tile([P, T // 4], I32, name="tab2_rows", tag="rows_then_u3", align_bytes=64)
+        tab_rows = keep.tile([P, T // 4], I32, name="tab_rows", tag="rows_then_w4", align_bytes=256)
+        tab2_rows = keep.tile([P, T // 4], I32, name="tab2_rows", tag="rows_then_u3", align_bytes=256)
         tab_planes = {}
         tab2_planes = {}
         for h in range(2):
-            tab2_planes[h, 0] = keep.tile([P, 2, HALF // 4], I32, name=f"tab2_planes{h}", align_bytes=64)
+            wide = keep.tile([P, HALF // 2 + STRETCH], I32, name=f"tab2_planes{h}", align_bytes=256)
+            tab2_planes[h, 0] = wide[:, AT_PLANE : AT_PLANE + HALF // 2].rearrange("p (m c) -> p m c", m=2)
 
-        w4_s = keep.tile([P, TAB_PASSES, M // 4], I32, name="w4_s", align_bytes=64)
+        wide = keep.tile([P, TAB_PASSES * M // 4 + STRETCH], I32, name="w4_s", align_bytes=256)
+        w4_s = wide[:, AT_WEIGHT_SCALES : AT_WEIGHT_SCALES + TAB_PASSES * M // 4].rearrange("p (a c) -> p a c", a=TAB_PASSES)
         nc.gpsimd.memset(tab_rows[:], 0)
         nc.vector.memset(tab2_rows[0:32, :], 0)
         nc.vector.memset(tab2_rows[96:128, :], 0)
@@ -58,11 +63,11 @@ def tile_list_tab48_res_kernel(tc, tab, w4_words, w4_scales, tab2, u, r, offs, o
         w4 = {}
 
         def load_words(into, key, src, tag):
-            into[key] = keep.tile([P, T], I32, name=f"words_{tag}", tag=tag, align_bytes=64)
+            into[key] = keep.tile([P, T], I32, name=f"words_{tag}", tag=tag, align_bytes=256)
             nc.sync.dma_start(into[key][:], src[0 : 512 * T].rearrange("(p b) -> p b", p=P).bitcast(I32))
 
         def load_u(b, tag):
-            u_raw[b] = keep.tile([P, 4, M], F32, name=f"u_raw{b}", tag=tag, align_bytes=64)
+            u_raw[b] = keep.tile([P, 4, M], F32, name=f"u_raw{b}", tag=tag, align_bytes=256)
             nc.sync.dma_start(u_raw[b][:], u[512 * b : 512 * (b + 1), :].rearrange("(p j) n -> p j n", j=4))
 
         load_words(tab2_w, 0, tab2[0], "tab2_w0")
@@ -77,7 +82,7 @@ def tile_list_tab48_res_kernel(tc, tab, w4_words, w4_scales, tab2, u, r, offs, o
             return slice(lo // 16, (lo + n) // 16)
 
         def gather_scales(rows, lists, name):
-            picked = keep.tile([P, S // 4], I32, name=name, align_bytes=64)
+            picked = keep.tile([P, S // 4], I32, name=name, align_bytes=256)
             nc.vector.tensor_copy(picked[:].bitcast(U8), rows[:].bitcast(U8).indirect(lists[:]))
             return picked
 
@@ -96,8 +101,8 @@ def tile_list_tab48_res_kernel(tc, tab, w4_words, w4_scales, tab2, u, r, offs, o
                 nc.sync.dma_start(plane[j:P:32, :], tab_picked[lo : lo + 37 : 12, words])
 
         def move_tab_scales_early(a, halves, tag):
-            plane = keep.tile([P, halves * HALF // 4], I32, name=f"tab_early{a}", tag=tag, align_bytes=64)
-            move_tab_scales(a, 0, halves, plane)
+            plane = keep.tile([P, halves * HALF // 4 + STRETCH], I32, name=f"tab_early{a}", tag=tag, align_bytes=256)
+            move_tab_scales(a, 0, halves, plane[:, AT_PLANE : AT_PLANE + halves * HALF // 4])
 
         gw = {}
         g2w = {}
@@ -122,18 +127,20 @@ def tile_list_tab48_res_kernel(tc, tab, w4_words, w4_scales, tab2, u, r, offs, o
                     g2w[2 * m + h, lo // N + c] = w[:, h, 2 * N * c : 2 * N * (c + 1)]
 
         def parted(name, n):
-            return keep.tile([P, 2, 2 * n], U8, name=name, align_bytes=64)
+            return keep.tile([P, 2, 2 * n], U8, name=name, align_bytes=256)
 
         u_codes = {}
         u_scales = {}
 
         def quantise_u(b, tag):
-            grouped = keep.tile([P, M, 4], BF16, name=f"grouped{b}", tag=tag, align_bytes=64)
+            grouped = keep.tile([P, M, 4], BF16, name=f"grouped{b}", tag=tag, align_bytes=256)
             nc.scalar.copy(grouped[:], u_raw[b][:].rearrange("p j n -> p n j"))
-            u_codes[b] = keep.tile([P, M], U32, name=f"u_codes{b}", align_bytes=64)
-            u_scales[b] = keep.tile([P, M], U8, name=f"u_scales{b}", align_bytes=64)
+            codes = keep.tile([P, M + STRETCH], U32, name=f"u_codes{b}", align_bytes=256)
+            scales = keep.tile([P, M + 4 * STRETCH], U8, name=f"u_scales{b}", align_bytes=256)
+            u_codes[b] = codes[:, AT_WEIGHTS : AT_WEIGHTS + M]
+            u_scales[b] = scales[:, 4 * AT_WEIGHT_SCALES : 4 * AT_WEIGHT_SCALES + M]
             nc.vector.quantize_mx(
-                out=u_codes[b][:].bitcast(FP8X4), scales=u_scales[b][:], in_=grouped[:].rearrange("p n j -> p (n j)")
+                out=u_codes[b].bitcast(FP8X4), scales=u_scales[b], in_=grouped[:].rearrange("p n j -> p (n j)")
             )
 
         acc = {}
@@ -179,27 +186,28 @@ def tile_list_tab48_res_kernel(tc, tab, w4_words, w4_scales, tab2, u, r, offs, o
                 for m in range(4):
                     multiply_tab2(b, c, m, start=b == 0)
 
-        stage0 = keep.tile([P, HALF], I32, name="stage0", tag="stage0", align_bytes=64)
+        stage0 = keep.tile([P, HALF], I32, name="stage0", tag="stage0", align_bytes=256)
         gather_tab2_words(0, 0, HALF, stage0[:])
         tab_picked = gather_scales(tab_rows, offs_t, "tab_picked")
-        w4_early = keep.tile([P, 2, M // 2], I32, name="w4_early", tag="rows_then_w4", align_bytes=64)
-        nc.sync.dma_start(w4_early[:], w4_words[1:3].rearrange("a p b -> p a b").bitcast(I32))
+        wide = keep.tile([P, M + STRETCH], I32, name="w4_early", tag="rows_then_w4", align_bytes=256)
+        w4_early = wide[:, AT_WEIGHTS : AT_WEIGHTS + M].rearrange("p (a c) -> p a c", a=2)
+        nc.sync.dma_start(w4_early, w4_words[1:3].rearrange("a p b -> p a b").bitcast(I32))
         w4[1], w4[2] = w4_early[:, 0, :], w4_early[:, 1, :]
         part_tab2_words(0, 0, HALF, stage0[:], parted("g2w0_first", HALF))
         quantise_u(0, "grouped0")
         first, second, last = 1, 2, 0
         load_words(tab_w, first, tab[first], "u0_then_first")
         first_half_tab2(0)
-        stage1 = keep.tile([P, HALF], I32, name="stage1", tag="grouped0", align_bytes=64)
+        stage1 = keep.tile([P, HALF], I32, name="stage1", tag="grouped0", align_bytes=256)
         gather_tab2_words(0, HALF, HALF, stage1[:])
         quantise_u(1, "grouped1_then_second")
         move_tab_scales_early(first, 1, "u1_then_planes")
         load_words(tab_w, second, tab[second], "grouped1_then_second")
         first_half_tab2(1)
-        stage2 = keep.tile([P, 3 * N], I32, name="stage2", tag="stage0", align_bytes=64)
+        stage2 = keep.tile([P, 3 * N], I32, name="stage2", tag="stage0", align_bytes=256)
         gather_tab2_words(1, 0, 3 * N, stage2[:])
         part_tab2_words(0, HALF, HALF, stage1[:], parted("g2w0_second", HALF))
-        g2w1_first = shared.tile([P, 2, 2 * HALF], U8, name="g2w1_first", offset=2 * HALF, align_bytes=64)
+        g2w1_first = shared.tile([P, 2, 2 * HALF], U8, name="g2w1_first", offset=2 * HALF, align_bytes=256)
         part_tab2_words(1, 0, HALF, stage2[:, 0:HALF], g2w1_first)
         quantise_u(2, "grouped2_then_last")
         move_tab_scales_early(second, 1, "u2")
@@ -207,18 +215,18 @@ def tile_list_tab48_res_kernel(tc, tab, w4_words, w4_scales, tab2, u, r, offs, o
         first_half_tab2(2)
         part_tab2_words(1, HALF, N, stage2[:, HALF : 3 * N], parted("g2w1_third", N))
         quantise_u(3, "grouped0")
-        w4_last = keep.tile([P, M // 2], I32, name="w4_last", tag="rows_then_u3", align_bytes=64)
-        nc.sync.dma_start(w4_last[:], w4_words[last].bitcast(I32))
-        w4[last] = w4_last[:]
+        w4_last = keep.tile([P, M // 2 + STRETCH], I32, name="w4_last", tag="rows_then_u3", align_bytes=256)
+        w4[last] = w4_last[:, AT_WEIGHTS : AT_WEIGHTS + M // 2]
+        nc.sync.dma_start(w4[last], w4_words[last].bitcast(I32))
         move_tab_scales_early(last, 2, "grouped0")
         first_half_tab2(3)
 
-        tab2_planes[0, 1] = shared.tile([P, 2, HALF // 4], I32, name="tab2_late", offset=HALF, align_bytes=64)
+        tab2_planes[0, 1] = shared.tile([P, 2, HALF // 4], I32, name="tab2_late", offset=HALF + 4 * AT_PLANE, align_bytes=64)
         tab2_planes[1, 1] = tab2_planes[1, 0]
         late_planes = {}
         for i, a in enumerate((first, second)):
-            late_planes[a] = shared.tile([P, HALF // 4], I32, name=f"tab_late{a}", offset=(3 + i) * HALF, align_bytes=64)
-        r_all = shared.tile([P, 4, S], F32, name="r_all", offset=5 * HALF, align_bytes=64)
+            late_planes[a] = shared.tile([P, HALF // 4], I32, name=f"tab_late{a}", offset=(3 + i) * HALF + 4 * AT_PLANE, align_bytes=64)
+        r_all = shared.tile([P, 4, S], F32, name="r_all", offset=5 * HALF + 4 * STRETCH, align_bytes=256)
 
         def load_r(m, tiles, half):
             items = slice(HALF * half, HALF * (half + 1))
@@ -235,24 +243,24 @@ def tile_list_tab48_res_kernel(tc, tab, w4_words, w4_scales, tab2, u, r, offs, o
         move_tab_scales(second, 1, 1, late_planes[second])
         load_r(2, 2, 1)
 
-        gw_first = keep.tile([P, 2, HALF], I32, name="gw_first", align_bytes=64)
+        gw_first = keep.tile([P, 2, HALF], I32, name="gw_first", align_bytes=256)
         gather_tab_words(first, HALF, HALF, gw_first[:, 1, :])
         for c in range(2):
             gather_tab_words(first, N * c, N, gw_first[:, 0, N * c : N * (c + 1)])
         for m in range(4):
             multiply_tab(first, 0, m)
         for c in range(2):
-            t = keep.tile([P, N], I32, name=f"gw_second{c}", align_bytes=64)
+            t = keep.tile([P, N], I32, name=f"gw_second{c}", align_bytes=256)
             gather_tab_words(second, N * c, N, t[:])
             for m in range(4):
                 multiply_tab(second, c, m)
-        third = keep.tile([P, N], I32, name="gw_second2", align_bytes=64)
+        third = keep.tile([P, N], I32, name="gw_second2", align_bytes=256)
         gather_tab_words(second, 2 * N, N, third[:])
         for m in range(4):
             multiply_tab(first, 1, m)
 
-        late_at = 5 * HALF + 4 * 4 * S
-        closing = shared.tile([P, 2, N], I32, name="closing", offset=late_at, align_bytes=64)
+        late_at = 5 * HALF + 4 * STRETCH + 4 * 4 * S
+        closing = shared.tile([P, 2, N], I32, name="closing", offset=late_at, align_bytes=256)
         sums = keep.tile([P, 4, N], F32, name="sums")
         for c in range(2):
             gather_tab_words(last, N * c, N, closing[:, c, :])
@@ -261,10 +269,10 @@ def tile_list_tab48_res_kernel(tc, tab, w4_words, w4_scales, tab2, u, r, offs, o
                 if c == 0:
                     nc.scalar.copy(sums[:, m, :], acc[c, m][:])
 
-        rest = keep.tile([P, 2, N], I32, name="gw_rest", align_bytes=64)
+        rest = keep.tile([P, 2, N], I32, name="gw_rest", align_bytes=256)
         gather_tab_words(last, 2 * N, N, rest[:, 0, :])
-        late2 = shared.tile([P, N], I32, name="late2", offset=late_at, align_bytes=64)
-        late1 = shared.tile([P, N], I32, name="late1", offset=late_at + 4 * N, align_bytes=64)
+        late2 = shared.tile([P, N], I32, name="late2", offset=late_at, align_bytes=256)
+        late1 = shared.tile([P, N], I32, name="late1", offset=late_at + 4 * N, align_bytes=256)
         gather_tab2_words(1, 3 * N, N, late2[:])
         gather_tab_words(last, 3 * N, N, rest[:, 1, :])
         part_tab2_words(1, 3 * N, N, late2[:], parted("g2w1_fourth", N))
@@ -277,7 +285,7 @@ def tile_list_tab48_res_kernel(tc, tab, w4_words, w4_scales, tab2, u, r, offs, o
         def store(m, lo, n):
             nc.sync.dma_start(out[P * m : P * (m + 1), lo : lo + n], r_all[:, m, lo : lo + n])
 
-        first_half = keep.tile([P, 4, HALF], F32, name="first_half", tag="grouped1_then_second", align_bytes=64)
+        first_half = keep.tile([P, 4, HALF], F32, name="first_half", tag="grouped1_then_second", align_bytes=256)
         for m in (0, 2, 3, 1):
             nc.vector.tensor_tensor(first_half[:, m, N:HALF], acc[1, m][:], r_all[:, m, N:HALF], ADD)
         for m in (2, 3, 0, 1):

@@ -261,7 +261,7 @@ def tile_list_tab48_res_kernel(tc, tab, w4_words, w4_scales, tab2, u, r, offs, o
 
         late_at = 5 * HALF + 4 * STRETCH + 4 * 4 * S
         closing = shared.tile([P, 2, N], I32, name="closing", offset=late_at, align_bytes=256)
-        sums = keep.tile([P, 4, N], F32, name="sums")
+        sums = keep.tile([P, 4, N], F32, name="sums", tag="sums", align_bytes=256)
         for c in range(2):
             gather_tab_words(last, N * c, N, closing[:, c, :])
             for m in range(4):
@@ -272,11 +272,9 @@ def tile_list_tab48_res_kernel(tc, tab, w4_words, w4_scales, tab2, u, r, offs, o
         rest = keep.tile([P, 2, N], I32, name="gw_rest", align_bytes=256)
         gather_tab_words(last, 2 * N, N, rest[:, 0, :])
         late2 = shared.tile([P, N], I32, name="late2", offset=late_at, align_bytes=256)
-        late1 = shared.tile([P, N], I32, name="late1", offset=late_at + 4 * N, align_bytes=256)
         gather_tab2_words(1, 3 * N, N, late2[:])
         gather_tab_words(last, 3 * N, N, rest[:, 1, :])
         part_tab2_words(1, 3 * N, N, late2[:], parted("g2w1_fourth", N))
-        gather_tab_words(second, 3 * N, N, late1[:])
 
         def add(m, lo, n, y):
             cols_r = r_all[:, m, lo : lo + n]
@@ -285,13 +283,16 @@ def tile_list_tab48_res_kernel(tc, tab, w4_words, w4_scales, tab2, u, r, offs, o
         def store(m, lo, n):
             nc.sync.dma_start(out[P * m : P * (m + 1), lo : lo + n], r_all[:, m, lo : lo + n])
 
-        first_half = keep.tile([P, 4, HALF], F32, name="first_half", tag="grouped1_then_second", align_bytes=256)
+        first_half = shared.tile([P, 4, HALF], F32, name="first_half", offset=late_at, align_bytes=256)
         for m in (0, 2, 3, 1):
             nc.vector.tensor_tensor(first_half[:, m, N:HALF], acc[1, m][:], r_all[:, m, N:HALF], ADD)
         for m in (2, 3, 0, 1):
             engine = nc.gpsimd if m >= 2 else nc.vector
             engine.tensor_tensor(first_half[:, m, 0:N], sums[:, m, :], r_all[:, m, 0:N], ADD)
             nc.sync.dma_start(out[P * m : P * (m + 1), 0:HALF], first_half[:, m, :])
+
+        second_last = keep.tile([P, N], I32, name="gw_second3", tag="sums", align_bytes=256)
+        gather_tab_words(second, 3 * N, N, second_last[:])
 
         for m in range(4):
             bank(2, m, m)

@@ -44,16 +44,15 @@ def tile_list_tab48_res_kernel(tc, tab, w4_words, w4_scales, tab2, u, r, offs, o
         wide = keep.tile([P, TAB_PASSES * M // 4 + STRETCH], I32, name="w4_s", align_bytes=256)
         w4_s = wide[:, AT_WEIGHT_SCALES : AT_WEIGHT_SCALES + TAB_PASSES * M // 4].rearrange("p (a c) -> p a c", a=TAB_PASSES)
         nc.gpsimd.memset(tab_rows[:], 0)
-        nc.vector.memset(tab2_rows[0:32, :], 0)
-        nc.vector.memset(tab2_rows[96:128, :], 0)
+        nc.vector.memset(tab2_rows[64:128, :], 0)
         for j in range(4):
             rows = w4_scales[:, j:16:4, :].rearrange("a q b -> q a b").bitcast(I32)
             nc.gpsimd.dma_start(w4_s[j:P:32, :, :], rows)
 
         nc.sync.dma_start(offs2_t[:], offs2)
-        for j in (0, 2, 1, 3):
+        for j in range(4):
             rows = tab2[:, 512 * T : 544 * T].rearrange("m (g j c) -> j g m c", j=4, c=T)[j].bitcast(I32)
-            lo = 32 + 32 * (j // 2) + j % 2
+            lo = 32 * (j // 2) + j % 2
             nc.sync.dma_start(tab2_rows[lo : lo + 31 : 2, :], rows)
         nc.sync.dma_start(offs_t[:], offs)
 
@@ -89,7 +88,7 @@ def tile_list_tab48_res_kernel(tc, tab, w4_words, w4_scales, tab2, u, r, offs, o
         def move_tab2_scales(half, h):
             words = slice(half * HALF // 4, (half + 1) * HALF // 4)
             for j in range(4):
-                lo = 32 + 32 * (j // 2) + j % 2 + 16 * h
+                lo = 32 * (j // 2) + j % 2 + 16 * h
                 nc.sync.dma_start(tab2_planes[h, half][j:P:32, :, :], tab2_picked[lo : lo + 15 : 2, words])
 
         def move_tab_scales(a, half, halves, plane):
@@ -148,10 +147,10 @@ def tile_list_tab48_res_kernel(tc, tab, w4_words, w4_scales, tab2, u, r, offs, o
         def bank(c, m, i):
             acc[c, m] = psum.tile([P, N], F32, name=f"bank{i}")
 
-        def multiply_tab(a, c, m, stop=False, lo=0, n=N, start=False):
+        def multiply_tab(a, c, m, stop=False, lo=0, n=N, start=False, into=0):
             at = (N * (c % 2) + lo) // 4
             nc.tensor.matmul_mx(
-                out=acc[c, m][:],
+                out=acc[c, m][:, into : into + n],
                 lhsT=w4[a][:, 64 * m : 64 * (m + 1)].bitcast(FP4X4),
                 lhsT_scale=w4_s[:, a, 32 * m : 32 * (m + 1)].bitcast(U8),
                 rhs=gw[a, c][:, lo : lo + n].bitcast(FP8X4),
@@ -259,18 +258,26 @@ def tile_list_tab48_res_kernel(tc, tab, w4_words, w4_scales, tab2, u, r, offs, o
         for m in range(4):
             multiply_tab(first, 1, m)
 
+        def gather_last_half(c, lo):
+            window = tab_w[last][:].bitcast(U32).indirect(offs_t[:, cols(N * c + lo, N // 2)])
+            nc.vector.tensor_copy(gw[last, c][:, lo : lo + N // 2].bitcast(U32), window)
+
         late_at = 5 * HALF + 4 * STRETCH + 4 * 4 * S
         closing = shared.tile([P, 2, N], I32, name="closing", offset=late_at, align_bytes=256)
         sums = keep.tile([P, 4, N], F32, name="sums", tag="sums", align_bytes=256)
         for c in range(2):
-            gather_tab_words(last, N * c, N, closing[:, c, :])
-            for m in range(4):
-                multiply_tab(last, c, m, True)
-                if c == 0:
-                    nc.scalar.copy(sums[:, m, :], acc[c, m][:])
+            gw[last, c] = closing[:, c, :]
+            for lo in (0, N // 2):
+                gather_last_half(c, lo)
+                for m in range(4):
+                    multiply_tab(last, c, m, stop=lo > 0, lo=lo, n=N // 2, into=lo)
+                    if c == 0 and lo > 0:
+                        nc.scalar.copy(sums[:, m, :], acc[c, m][:])
 
         rest = keep.tile([P, 2, N], I32, name="gw_rest", align_bytes=256)
-        gather_tab_words(last, 2 * N, N, rest[:, 0, :])
+        gw[last, 2] = rest[:, 0, :]
+        for lo in (0, N // 2):
+            gather_last_half(2, lo)
         late2 = shared.tile([P, N], I32, name="late2", offset=late_at, align_bytes=256)
         gather_tab2_words(1, 3 * N, N, late2[:])
         gather_tab_words(last, 3 * N, N, rest[:, 1, :])
@@ -296,8 +303,9 @@ def tile_list_tab48_res_kernel(tc, tab, w4_words, w4_scales, tab2, u, r, offs, o
 
         for m in range(4):
             bank(2, m, m)
-        for m in range(4):
-            multiply_tab(last, 2, m, start=True)
+        for lo in (0, N // 2):
+            for m in range(4):
+                multiply_tab(last, 2, m, start=lo == 0, lo=lo, n=N // 2, into=lo)
         for b in (0, 2, 1, 3):
             for m in range(4):
                 multiply_tab2(b, 2, m)

@@ -70,8 +70,9 @@ def tile_list_tab48_res_kernel(tc, tab, w4_words, w4_scales, tab2, u, r, offs, o
             nc.sync.dma_start(u_raw[b][:], u[512 * b : 512 * (b + 1), :].rearrange("(p j) n -> p j n", j=4))
 
         load_words(tab2_w, 0, tab2[0], "tab2_w0")
-        rows = tab[:, 512 * T : 528 * T].rearrange("a (q c) -> q a c", q=16).bitcast(I32)
-        nc.sync.dma_start(tab_rows[32:80, :], rows)
+        for a in range(TAB_PASSES):
+            rows = tab[a, 512 * T : 528 * T].rearrange("(q c) -> q c", q=16).bitcast(I32)
+            nc.sync.dma_start(tab_rows[32 + a : 96 : 4, :], rows)
         load_u(0, "u0_then_first")
         load_u(1, "u1_then_planes")
         load_words(tab2_w, 1, tab2[1], "tab2_w1")
@@ -95,9 +96,9 @@ def tile_list_tab48_res_kernel(tc, tab, w4_words, w4_scales, tab2, u, r, offs, o
             for i in range(halves):
                 tab_planes[a, half + i] = plane[:, HALF // 4 * i : HALF // 4 * (i + 1)]
             for j in range(4):
-                lo = 32 + 3 * j + a
+                lo = 32 + 4 * j + a
                 words = slice(HALF // 4 * half, HALF // 4 * (half + halves))
-                nc.sync.dma_start(plane[j:P:32, :], tab_picked[lo : lo + 37 : 12, words])
+                nc.sync.dma_start(plane[j:P:32, :], tab_picked[lo : lo + 49 : 16, words])
 
         def move_tab_scales_early(a, halves, tag):
             plane = keep.tile([P, halves * HALF // 4 + STRETCH], I32, name=f"tab_early{a}", tag=tag, align_bytes=256)
@@ -331,13 +332,13 @@ def tile_list_tab48_res_kernel(tc, tab, w4_words, w4_scales, tab2, u, r, offs, o
                 multiply_tab2(b, 3, m, stop=b == 3)
             add(m, 3 * N, N, acc[3, m][:])
             store(m, HALF, HALF)
-        for i, free_bank in enumerate((7, 0, 1, 2)):
-            acc[3, 3] = psum.tile([P, P], F32, name=f"bank{free_bank}")
+        for lo, n, free_bank in ((0, 2 * P, 7), (2 * P, P, 0), (3 * P, P, 1)):
+            acc[3, 3] = psum.tile([P, n], F32, name=f"bank{free_bank}")
             for a in (second, first, last):
-                multiply_tab(a, 3, 3, lo=P * i, n=P, start=a == second)
+                multiply_tab(a, 3, 3, lo=lo, n=n, start=a == second)
             for b in range(4):
-                multiply_tab2(b, 3, 3, stop=b == 3, lo=P * i, n=P)
-            add(3, 3 * N + P * i, P, acc[3, 3][:])
-            if i == 2:
+                multiply_tab2(b, 3, 3, stop=b == 3, lo=lo, n=n)
+            add(3, 3 * N + lo, n, acc[3, 3][:])
+            if lo == 2 * P:
                 store(3, 3 * N, 3 * P)
         store(3, S - P, P)

from contextlib import ExitStack

import concourse.mybir as mybir

K, L, M, T, S = 1536, 2048, 512, 4096, 2048
P = 128
TAB_PASSES = K // 512
U_PASSES = L // 512
N = 512
HALF = S // 2
FLOPS = 2 * (K + L) * M * S

F32 = mybir.dt.float32
BF16 = mybir.dt.bfloat16
I32 = mybir.dt.int32
U32 = mybir.dt.uint32
U16 = mybir.dt.uint16
U8 = mybir.dt.uint8
FP8X4 = mybir.dt.float8_e4m3fn_x4
FP4X4 = mybir.dt.float4_e2m1fn_x4
ADD = mybir.AluOpType.add

STRETCH = 64
AT_PLANE, AT_WEIGHTS, AT_WEIGHT_SCALES = 16, 32, 48


def tile_list_tab48_res_kernel(tc, tab, w4_words, w4_scales, tab2, u, r, offs, offs2, out):
    nc = tc.nc
    with ExitStack() as ctx:
        keep = ctx.enter_context(tc.tile_pool(name="keep", bufs=1))
        shared = ctx.enter_context(tc.tile_pool(name="shared", bufs=1))
        psum = ctx.enter_context(tc.psum_pool(name="psum", bufs=1))

        offs_t = keep.tile([P, S // 16], U16, name="offs_t")
        offs2_t = keep.tile([P, S // 16], U16, name="offs2_t")
        tab_rows = keep.tile([P, T // 4], I32, name="tab_rows", tag="rows_then_w4", align_bytes=256)
        tab2_rows = keep.tile([P, T // 4], I32, name="tab2_rows", tag="rows_then_u3", align_bytes=256)
        tab_planes = {}
        tab2_planes = {}
        for h in range(2):
            wide = keep.tile([P, HALF // 2 + STRETCH], I32, name=f"tab2_planes{h}", align_bytes=256)
            tab2_planes[h, 0] = wide[:, AT_PLANE : AT_PLANE + HALF // 2].rearrange("p (m c) -> p m c", m=2)

        wide = keep.tile([P, TAB_PASSES * M // 4 + STRETCH], I32, name="w4_s", align_bytes=256)
        w4_s = wide[:, AT_WEIGHT_SCALES : AT_WEIGHT_SCALES + TAB_PASSES * M // 4].rearrange("p (a c) -> p a c", a=TAB_PASSES)
        nc.gpsimd.memset(tab_rows[:], 0)
        nc.vector.memset(tab2_rows[64:128, :], 0)
        for j in range(4):
            rows = w4_scales[:, j:16:4, :].rearrange("a q b -> q a b").bitcast(I32)
            nc.gpsimd.dma_start(w4_s[j:P:32, :, :], rows)

        nc.sync.dma_start(offs2_t[:], offs2)
        for j in range(4):
            rows = tab2[:, 512 * T : 544 * T].rearrange("m (g j c) -> j g m c", j=4, c=T)[j].bitcast(I32)
            lo = 32 * (j // 2) + j % 2
            nc.sync.dma_start(tab2_rows[lo : lo + 31 : 2, :], rows)
        nc.sync.dma_start(offs_t[:], offs)

        tab_w = {}
        tab2_w = {}
        u_raw = {}
        w4 = {}

        def load_words(into, key, src, tag):
            into[key] = keep.tile([P, T], I32, name=f"words_{tag}", tag=tag, align_bytes=256)
            nc.sync.dma_start(into[key][:], src[0 : 512 * T].rearrange("(p b) -> p b", p=P).bitcast(I32))

        def load_u(b, tag):
            u_raw[b] = keep.tile([P, 4, M], F32, name=f"u_raw{b}", tag=tag, align_bytes=256)
            nc.sync.dma_start(u_raw[b][:], u[512 * b : 512 * (b + 1), :].rearrange("(p j) n -> p j n", j=4))

        load_words(tab2_w, 0, tab2[0], "tab2_w0")
        for a in range(TAB_PASSES):
            rows = tab[a, 512 * T : 528 * T].rearrange("(q c) -> q c", q=16).bitcast(I32)
            nc.sync.dma_start(tab_rows[32 + a : 96 : 4, :], rows)
        load_u(0, "u0_then_first")
        load_u(1, "u1_then_planes")
        load_words(tab2_w, 1, tab2[1], "tab2_w1")
        load_u(2, "u2")

        def cols(lo, n):
            return slice(lo // 16, (lo + n) // 16)

        def gather_scales(rows, lists, name):
            picked = keep.tile([P, S // 4], I32, name=name, align_bytes=256)
            nc.vector.tensor_copy(picked[:].bitcast(U8), rows[:].bitcast(U8).indirect(lists[:]))
            return picked

        def move_tab2_scales(half, h):
            words = slice(half * HALF // 4, (half + 1) * HALF // 4)
            for j in range(4):
                lo = 32 * (j // 2) + j % 2 + 16 * h
                nc.sync.dma_start(tab2_planes[h, half][j:P:32, :, :], tab2_picked[lo : lo + 15 : 2, words])

        def move_tab_scales(a, half, halves, plane):
            for i in range(halves):
                tab_planes[a, half + i] = plane[:, HALF // 4 * i : HALF // 4 * (i + 1)]
            for j in range(4):
                lo = 32 + 4 * j + a
                words = slice(HALF // 4 * half, HALF // 4 * (half + halves))
                nc.sync.dma_start(plane[j:P:32, :], tab_picked[lo : lo + 49 : 16, words])

        def move_tab_scales_early(a, halves, tag):
            plane = keep.tile([P, halves * HALF // 4 + STRETCH], I32, name=f"tab_early{a}", tag=tag, align_bytes=256)
            move_tab_scales(a, 0, halves, plane[:, AT_PLANE : AT_PLANE + halves * HALF // 4])

        gw = {}
        g2w = {}
        pairs = {}

        def gather_tab_words(a, lo, n, t):
            nc.vector.tensor_copy(t.bitcast(U32), tab_w[a][:].bitcast(U32).indirect(offs_t[:, cols(lo, n)]))
            for c in range(lo, lo + n, N):
                gw[a, c // N] = t[:, c - lo : c - lo + N]

        def gather_tab2_words(m, lo, n, t):
            nc.vector.tensor_copy(t.bitcast(U32), tab2_w[m][:].bitcast(U32).indirect(offs2_t[:, cols(lo, n)]))
            pairs[m, lo] = t

        def part_tab2_words(m, lo, n, src, w):
            nc.vector.tensor_copy(
                w[:].bitcast(U16).rearrange("p h (g i) -> p g h i", i=8),
                src.bitcast(U16).rearrange("p (g i h) -> p g h i", i=8, h=2),
            )
            for h in range(2):
                for c in range(n // N):
                    g2w[2 * m + h, lo // N + c] = w[:, h, 2 * N * c : 2 * N * (c + 1)]

        def parted(name, n):
            return keep.tile([P, 2, 2 * n], U8, name=name, align_bytes=256)

        u_codes = {}
        u_scales = {}

        def quantise_u(b, tag):
            grouped = keep.tile([P, M, 4], BF16, name=f"grouped{b}", tag=tag, align_bytes=256)
            nc.scalar.copy(grouped[:], u_raw[b][:].rearrange("p j n -> p n j"))
            codes = keep.tile([P, M + STRETCH], U32, name=f"u_codes{b}", align_bytes=256)
            scales = keep.tile([P, M + 4 * STRETCH], U8, name=f"u_scales{b}", align_bytes=256)
            u_codes[b] = codes[:, AT_WEIGHTS : AT_WEIGHTS + M]
            u_scales[b] = scales[:, 4 * AT_WEIGHT_SCALES : 4 * AT_WEIGHT_SCALES + M]
            nc.vector.quantize_mx(
                out=u_codes[b].bitcast(FP8X4), scales=u_scales[b], in_=grouped[:].rearrange("p n j -> p (n j)")
            )

        acc = {}

        def bank(c, m, i):
            acc[c, m] = psum.tile([P, N], F32, name=f"bank{i}")

        def multiply_tab(a, c, m, stop=False, lo=0, n=N, start=False, into=0):
            at = (N * (c % 2) + lo) // 4
            nc.tensor.matmul_mx(
                out=acc[c, m][:, into : into + n],
                lhsT=w4[a][:, 64 * m : 64 * (m + 1)].bitcast(FP4X4),
                lhsT_scale=w4_s[:, a, 32 * m : 32 * (m + 1)].bitcast(U8),
                rhs=gw[a, c][:, lo : lo + n].bitcast(FP8X4),
                rhs_scale=tab_planes[a, c // 2][:, at : at + n // 4].bitcast(U8),
                start=start,
                stop=stop,
            )

        def multiply_tab2(b, c, m, start=False, stop=False, lo=0, n=N):
            at = (N * (c % 2) + lo) // 4
            nc.tensor.matmul_mx(
                out=acc[c, m][:],
                lhsT=u_codes[b][:, P * m : P * (m + 1)].bitcast(FP8X4),
                lhsT_scale=u_scales[b][:, P * m : P * (m + 1)],
                rhs=g2w[b, c][:, 2 * lo : 2 * (lo + n)].bitcast(FP4X4),
                rhs_scale=tab2_planes[b % 2, c // 2][:, b // 2, at : at + n // 4].bitcast(U8),
                start=start,
                stop=stop,
            )

        tab2_picked = gather_scales(tab2_rows, offs2_t, "tab2_picked")
        move_tab2_scales(0, 0)
        load_u(3, "rows_then_u3")
        move_tab2_scales(0, 1)

        for c in range(2):
            for m in range(4):
                bank(c, m, 4 * c + m)

        def first_half_tab2(b):
            for c in range(2):
                for m in range(4):
                    multiply_tab2(b, c, m, start=b == 0)

        stage0 = keep.tile([P, HALF], I32, name="stage0", tag="stage0", align_bytes=256)
        gather_tab2_words(0, 0, HALF, stage0[:])
        tab_picked = gather_scales(tab_rows, offs_t, "tab_picked")
        wide = keep.tile([P, M + STRETCH], I32, name="w4_early", tag="rows_then_w4", align_bytes=256)
        w4_early = wide[:, AT_WEIGHTS : AT_WEIGHTS + M].rearrange("p (a c) -> p a c", a=2)
        nc.sync.dma_start(w4_early, w4_words[1:3].rearrange("a p b -> p a b").bitcast(I32))
        w4[1], w4[2] = w4_early[:, 0, :], w4_early[:, 1, :]
        part_tab2_words(0, 0, HALF, stage0[:], parted("g2w0_first", HALF))
        quantise_u(0, "grouped0")
        first, second, last = 1, 2, 0
        load_words(tab_w, first, tab[first], "u0_then_first")
        first_half_tab2(0)
        stage1 = keep.tile([P, HALF], I32, name="stage1", tag="grouped0", align_bytes=256)
        gather_tab2_words(0, HALF, HALF, stage1[:])
        quantise_u(1, "grouped1_then_second")
        move_tab_scales_early(first, 1, "u1_then_planes")
        load_words(tab_w, second, tab[second], "grouped1_then_second")
        first_half_tab2(1)
        stage2 = keep.tile([P, 3 * N], I32, name="stage2", tag="stage0", align_bytes=256)
        gather_tab2_words(1, 0, 3 * N, stage2[:])
        part_tab2_words(0, HALF, HALF, stage1[:], parted("g2w0_second", HALF))
        g2w1_first = shared.tile([P, 2, 2 * HALF], U8, name="g2w1_first", offset=2 * HALF, align_bytes=256)
        part_tab2_words(1, 0, HALF, stage2[:, 0:HALF], g2w1_first)
        quantise_u(2, "grouped2_then_last")
        move_tab_scales_early(second, 1, "u2")
        load_words(tab_w, last, tab[last], "grouped2_then_last")
        first_half_tab2(2)
        part_tab2_words(1, HALF, N, stage2[:, HALF : 3 * N], parted("g2w1_third", N))
        quantise_u(3, "grouped0")
        w4_last = keep.tile([P, M // 2 + STRETCH], I32, name="w4_last", tag="rows_then_u3", align_bytes=256)
        w4[last] = w4_last[:, AT_WEIGHTS : AT_WEIGHTS + M // 2]
        nc.sync.dma_start(w4[last], w4_words[last].bitcast(I32))
        move_tab_scales_early(last, 2, "grouped0")
        first_half_tab2(3)

        tab2_planes[0, 1] = shared.tile([P, 2, HALF // 4], I32, name="tab2_late", offset=HALF + 4 * AT_PLANE, align_bytes=64)
        tab2_planes[1, 1] = tab2_planes[1, 0]
        late_planes = {}
        for i, a in enumerate((first, second)):
            late_planes[a] = shared.tile([P, HALF // 4], I32, name=f"tab_late{a}", offset=(3 + i) * HALF + 4 * AT_PLANE, align_bytes=64)
        r_all = shared.tile([P, 4, S], F32, name="r_all", offset=5 * HALF + 4 * STRETCH, align_bytes=256)

        def load_r(m, tiles, half):
            items = slice(HALF * half, HALF * (half + 1))
            rows = r[P * m : P * (m + tiles), items].rearrange("(m p) n -> p m n", p=P)
            nc.sync.dma_start(r_all[:, m : m + tiles, items], rows)

        load_r(0, 2, 0)
        move_tab2_scales(1, 0)
        load_r(2, 1, 0)
        move_tab2_scales(1, 1)
        load_r(3, 1, 0)
        move_tab_scales(first, 1, 1, late_planes[first])
        load_r(0, 2, 1)
        move_tab_scales(second, 1, 1, late_planes[second])
        load_r(2, 2, 1)

        gw_first = keep.tile([P, 2, HALF], I32, name="gw_first", align_bytes=256)
        gather_tab_words(first, HALF, HALF, gw_first[:, 1, :])
        for c in range(2):
            gather_tab_words(first, N * c, N, gw_first[:, 0, N * c : N * (c + 1)])
        for m in range(4):
            multiply_tab(first, 0, m)
        for c in range(2):
            t = keep.tile([P, N], I32, name=f"gw_second{c}", align_bytes=256)
            gather_tab_words(second, N * c, N, t[:])
            for m in range(4):
                multiply_tab(second, c, m)
        third = keep.tile([P, N], I32, name="gw_second2", align_bytes=256)
        gather_tab_words(second, 2 * N, N, third[:])
        for m in range(4):
            multiply_tab(first, 1, m)

        def gather_last_half(c, lo):
            window = tab_w[last][:].bitcast(U32).indirect(offs_t[:, cols(N * c + lo, N // 2)])
            nc.vector.tensor_copy(gw[last, c][:, lo : lo + N // 2].bitcast(U32), window)

        late_at = 5 * HALF + 4 * STRETCH + 4 * 4 * S
        closing = shared.tile([P, 2, N], I32, name="closing", offset=late_at, align_bytes=256)
        sums = keep.tile([P, 4, N], F32, name="sums", tag="sums", align_bytes=256)
        for c in range(2):
            gw[last, c] = closing[:, c, :]
            for lo in (0, N // 2):
                gather_last_half(c, lo)
                for m in range(4):
                    multiply_tab(last, c, m, stop=lo > 0, lo=lo, n=N // 2, into=lo)
                    if c == 0 and lo > 0:
                        nc.scalar.copy(sums[:, m, :], acc[c, m][:])

        rest = keep.tile([P, 2, N], I32, name="gw_rest", align_bytes=256)
        gw[last, 2] = rest[:, 0, :]
        for lo in (0, N // 2):
            gather_last_half(2, lo)
        late2 = shared.tile([P, N], I32, name="late2", offset=late_at, align_bytes=256)
        gather_tab2_words(1, 3 * N, N, late2[:])
        gather_tab_words(last, 3 * N, N, rest[:, 1, :])
        part_tab2_words(1, 3 * N, N, late2[:], parted("g2w1_fourth", N))

        def add(m, lo, n, y):
            cols_r = r_all[:, m, lo : lo + n]
            nc.vector.tensor_tensor(cols_r, y, cols_r, ADD)

        def store(m, lo, n):
            nc.sync.dma_start(out[P * m : P * (m + 1), lo : lo + n], r_all[:, m, lo : lo + n])

        first_half = shared.tile([P, 4, HALF], F32, name="first_half", offset=late_at, align_bytes=256)
        for m in (0, 2, 3, 1):
            nc.vector.tensor_tensor(first_half[:, m, N:HALF], acc[1, m][:], r_all[:, m, N:HALF], ADD)
        for m in (2, 3, 0, 1):
            engine = nc.gpsimd if m >= 2 else nc.vector
            engine.tensor_tensor(first_half[:, m, 0:N], sums[:, m, :], r_all[:, m, 0:N], ADD)
            nc.sync.dma_start(out[P * m : P * (m + 1), 0:HALF], first_half[:, m, :])

        second_last = keep.tile([P, N], I32, name="gw_second3", tag="sums", align_bytes=256)
        gather_tab_words(second, 3 * N, N, second_last[:])

        for m in range(4):
            bank(2, m, m)
        for lo in (0, N // 2):
            for m in range(4):
                multiply_tab(last, 2, m, start=lo == 0, lo=lo, n=N // 2, into=lo)
        for b in (0, 2, 1, 3):
            for m in range(4):
                multiply_tab2(b, 2, m)
        for m in range(4):
            multiply_tab(first, 2, m)
        bank(3, 0, 4)
        for a in (first, last):
            multiply_tab(a, 3, 0, start=a == first)
        for b in range(4):
            multiply_tab2(b, 3, 0)
        for m in range(4):
            multiply_tab(second, 2, m, stop=True)
            add(m, 2 * N, N, acc[2, m][:])
        multiply_tab(second, 3, 0, stop=True)
        add(0, 3 * N, N, acc[3, 0][:])
        store(0, HALF, HALF)
        store(3, 2 * N, N)
        for m in (1, 2):
            bank(3, m, 4 + m)
            for a in (second, first, last):
                multiply_tab(a, 3, m, start=a == second)
            for b in range(4):
                multiply_tab2(b, 3, m, stop=b == 3)
            add(m, 3 * N, N, acc[3, m][:])
            store(m, HALF, HALF)
        for lo, n, free_bank in ((0, 2 * P, 7), (2 * P, P, 0), (3 * P, P, 1)):
            acc[3, 3] = psum.tile([P, n], F32, name=f"bank{free_bank}")
            for a in (second, first, last):
                multiply_tab(a, 3, 3, lo=lo, n=n, start=a == second)
            for b in range(4):
                multiply_tab2(b, 3, 3, stop=b == 3, lo=lo, n=n)
            add(3, 3 * N + lo, n, acc[3, 3][:])
            if lo == 2 * P:
                store(3, 3 * N, 3 * P)
        store(3, S - P, P)
